import numpy as np, ml_dtypes
CORES = [24,25,26,27,28,29,30,31]
N = 8
BF = ml_dtypes.bfloat16
def gentries(a):
    return np.ascontiguousarray(a.reshape(8, 16, -1).transpose(0, 2, 1)).reshape(8, -1)
def gtable(e):
    e = np.asarray(e); return np.ascontiguousarray(e.reshape(8, -1, 16).transpose(0, 2, 1)).reshape(128, -1).astype(np.int32)
V, B, BITS, RO = 3072, 128, 11, 3
M = N * B
W = M + V - B
C = 2 ** BITS
def seen(q, p):
    bq = np.ascontiguousarray(q[..., :B].transpose(1, 2, 0, 3)).reshape(8, 16, M)
    bp = np.ascontiguousarray(p[..., :B].transpose(1, 0, 2)).reshape(8, M)
    gs, qps, qgs = [], [], []
    for a in range(N):
        wq = np.concatenate([bq, q[a, :, :, B:]], axis=2); wp = np.concatenate([bp, p[a, :, B:]], axis=1)
        g = np.take_along_axis(wp, p[a], 1)
        gs.append(g); qps.append(np.take_along_axis(wq, p[a][:, None, :], 2)); qgs.append(np.take_along_axis(wq, g[:, None, :], 2))
    return np.stack(gs), np.stack(qps), np.stack(qgs)
def dots(am, z):
    return np.matmul(am.transpose(0, 1, 3, 2), z)
def codes(am, t, z):
    return np.add.reduce(np.where(dots(am, z)[:, :, :BITS] > t[:, :, :BITS], 2 ** np.arange(BITS)[:, None], 0), axis=2)
def forest(rng):
    span = rng.choice(np.array([2, 16, B, M]), (8, 1)); i = np.arange(M)
    o = np.argsort(rng.random((8, M)), axis=1); back = np.minimum(i, (rng.random((8, M)) * span).astype(np.int64) + 1)
    pb = np.zeros((8, M), np.int64); np.put_along_axis(pb, o, np.take_along_axis(o, i - np.where(rng.random((8, M)) < 0.02, 0, back), 1), 1)
    h = V - B; i = np.arange(h); span = rng.choice(np.array([2, 16, B, h]), (N, 8, 1))
    o = np.argsort(rng.random((N, 8, h)), axis=2); back = np.minimum(i, (rng.random((N, 8, h)) * span).astype(np.int64) + 1)
    pi = np.zeros((N, 8, h), np.int64); np.put_along_axis(pi, o, np.take_along_axis(o, i - np.where(rng.random((N, 8, h)) < 0.02, 0, back), 2), 2)
    pi = np.where(rng.random((N, 8, h)) < 0.5, rng.integers(0, M, (N, 8, h)), M + pi)
    return np.concatenate([pb.reshape(8, N, B).transpose(1, 0, 2), pi], axis=2)
def parts(rng):
    amp = rng.choice(np.array([8, 24, 64]), (N, 8, 1, V))
    q = 64 + np.floor((2 * rng.random((N, 8, 16, V)) - 1) * amp).astype(np.int64); q = np.clip(q, 0, 127)
    am = rng.integers(-1, 2, (N, 8, 16, 16))
    t = 128 * np.add.reduce(am, axis=2)[..., None] + rng.integers(-30, 31, (N, 8, 16, 1))
    c = np.clip(rng.choice(np.array([0, 8, 24, 64, 111]), (N, 8, 1, C)) + rng.integers(0, 17, (N, 8, 16, C)), 0, 127)
    return q, forest(rng), am, t, c
def pack(q, p, am, t, c):
    big = np.zeros((N, 128, 128), np.float32)
    for h in range(8): big[:, 16 * h:16 * h + 16, 16 * h:16 * h + 16] = am[:, h]
    return {"q": np.ascontiguousarray(q).reshape(N, 128, V).astype(np.float32).astype(BF), "par": np.stack([gtable(a) for a in p]), "amat": big.astype(BF),
            "clr": np.ascontiguousarray(c).reshape(N, 128, C).astype(np.float32).astype(BF), "th": np.ascontiguousarray(t).reshape(N, 128, 1).astype(np.int32)}
def setup_inputs(rng):
    return pack(*parts(rng))
def setup_inputs_edge(rng):
    q, p, am, t, c = parts(rng); q = 64 + rng.integers(-6, 7, q.shape)
    g, qp, qg = seen(q, p); s = dots(am, q + qg); low = rng.integers(0, 2, (N, 8, 16, 1)); low[:, :, 0] = 0; low[:, :, 1] = 1
    t = np.take_along_axis(s, rng.integers(0, V, (N, 8, 16, 1)), 3) - low
    code = codes(am, t, q + qg); gap = np.abs(q - qg)
    for a in range(N):
        for h in range(8):
            w = np.full(C, -1); w[code[a, h]] = np.arange(V); k = np.nonzero(w >= 0)[0]; n = np.arange(len(k))
            e = gap[a, h][:, w[k]].copy(); x = np.argmax(e, axis=0)
            e[x, n] = e[x, n] - ((rng.random(len(k)) < 0.5) & (e[x, n] > 0)).astype(np.int64)
            c[a, h][:, k] = e
    return pack(q, p, am, t, c)
def setup_inputs_chain(rng):
    q, p, am, t, c = parts(rng); k = np.arange(B)
    for r in range(N):
        p[r, 0::2, :B] = (r + 1) % N * B + (k + (r == N - 1)) % B
        p[r, 1::2, :B] = (r - 1) * B + k if r else np.where(k > 0, (N - 1) * B + k - 1, 0)
        p[r, :, B:] = M + np.arange(V - B) - 1; p[r, :, B] = r * B + B - 1
    c[:, 0:2] = 127; c[:, 2:4] = 0
    return pack(q, p, am, t, c)
def setup_inputs_alike(rng):
    q, p, am, t, c = parts(rng)
    p[:, 0:2, :B] = rng.choice(np.array([0, B - 1, B, M - 1]), (N, 2, B)); p[:, 0:2, B:] = rng.choice(np.array([0, M - 1, M, W - 1]), (N, 2, V - B))
    for r in range(N):
        p[r, 2, :B] = r * B + np.arange(B); p[r, 2, B:] = M + np.arange(V - B)
    p[:, 3, B:] = rng.integers(M, W, (N, V - B)); p[:, 4, B:] = rng.integers(0, M, (N, V - B))
    t[:, 5] = -4096; c[:, 5, :, C - 1] = rng.integers(20, 60, (N, 16)); t[:, 6] = 4096; c[:, 6, :, 0] = rng.integers(20, 60, (N, 16))
    q[:, 7] = 127 * rng.integers(0, 2, (N, 16, V)); one = np.arange(16)[:, None] == rng.integers(0, 16, (N, 1, C))
    c[:, 7] = 127 - (one & (rng.random((N, 1, C)) < 0.7)).astype(np.int64)
    return pack(q, p, am, t, c)
def setup_inputs_spread(rng):
    q, p, am, t, c = parts(rng)
    q = np.clip(np.floor(np.exp2(7.5 * rng.random((N, 8, 1, V))) * rng.random((N, 8, 16, V))).astype(np.int64), 0, 127)
    am = am * (rng.random((N, 8, 16, 16)) < rng.choice(np.array([0.1, 0.4, 1.0]), (N, 8, 1, 16)))
    t = np.floor(np.exp2(12 * rng.random((N, 8, 16, 1)) ** 1.5)).astype(np.int64) * rng.choice(np.array([-1, 1]), (N, 8, 16, 1)); t = np.clip(t, -4096, 4096)
    c = np.clip(np.floor(np.exp2(8 * rng.random((N, 8, 1, C))) * (0.5 + rng.random((N, 8, 16, C)))).astype(np.int64), 0, 127)
    return pack(q, p, am, t, c)
def setup_inputs_large(rng):
    q, p, am, t, c = parts(rng)
    q[:, :5] = 127 - np.floor(rng.random((N, 5, 16, V)) * rng.choice(np.array([1, 4, 16, 40]), (N, 5, 1, V))).astype(np.int64)
    cut = rng.integers(0, 3, (N, 5, 1, 16)); cut[:, 4] = 4; less = -rng.integers(0, 2, (N, 5, 16, 16)); less[:, 4] = -1
    sign = rng.choice(np.array([-1, 1]), (N, 5, 1, 16)); sign[:, 0] = 1; sign[:, 1] = -1
    am[:, :5] = sign * np.where(np.argsort(rng.random((N, 5, 16, 16)), axis=2) < cut, less, 1)
    for h in range(5, 8):
        a = int(rng.integers(0, N)); b = (a + 1) % N; ka = int(rng.integers(0, B)); kb = int(rng.integers(0, B))
        p[:, h] = a * B + ka; p[a, h, ka] = b * B + kb; p[b, h, kb] = b * B + kb
        am[:, h] = np.eye(16, dtype=np.int64); mid = rng.integers(32, 96, (N, 16, 1))
        for r in range(N):
            w = rng.permutation(np.concatenate([np.arange(C), rng.integers(0, C, max(V - C, 0))]))[:V]
            bit = (w[None, :] >> np.arange(16)[:, None]) & 1; bit[BITS:] = rng.integers(0, 2, (16 - BITS, V)); u = rng.random((16, V))
            q[r, h] = np.where(bit == 1, mid[r] + 1 + np.floor(u * (127 - mid[r])).astype(np.int64), np.floor(u * (mid[r] + 1)).astype(np.int64))
        t[:, h] = mid + q[b, h, :, kb][None, :, None]
    g, qp, qg = seen(q, p); s = np.take_along_axis(dots(am, q + qg), rng.integers(0, V, (N, 8, 16, 1)), 3)
    low = np.where((s & 3) == 1, 1, np.where((s & 3) == 3, 0, rng.integers(0, 2, s.shape)))
    t[:, :5] = (s - low)[:, :5]
    c[:] = 127 * rng.integers(0, 2, (N, 8, 1, C))
    return pack(q, p, am, t, c)
def check_inputs(d):
    bad = []
    for k in ("q", "clr"):
        x = np.asarray(d[k]).astype(np.float32)
        if not np.all((x >= 0) & (x <= 127) & (x == np.floor(x))): bad.append("numbers of " + k)
    if np.min(d["th"]) < -4096 or np.max(d["th"]) > 4096: bad.append("range of th")
    x = np.asarray(d["amat"]).astype(np.float32); same = np.arange(128)[:, None] // 16 == np.arange(128)[None, :] // 16
    if not np.all((x == 0) | (same & ((x == 1) | (x == -1)))): bad.append("numbers of amat")
    if np.min(d["par"]) < 0 or np.max(d["par"]) > W - 1: bad.append("range of par")
    if np.max(np.stack([gentries(a) for a in d["par"]])[:, :, :B]) > M - 1: bad.append("parents of border columns")
    return bad
def reference(q, par, amat, clr, th):
    x = q.astype(np.float32).astype(np.int64).reshape(N, 8, 16, V); p = np.stack([gentries(a) for a in par]).astype(np.int64)
    big = amat.astype(np.float32).astype(np.int64); am = np.stack([big[:, 16 * h:16 * h + 16, 16 * h:16 * h + 16] for h in range(8)], axis=1)
    c = clr.astype(np.float32).astype(np.int64).reshape(N, 8, 16, C); t = th.astype(np.int64).reshape(N, 8, 16, 1)
    for rnd in range(RO):
        g, xp, xg = seen(x, p)
        code = codes(am, t, x + xg)
        room = np.take_along_axis(c, code[:, :, None, :], 3)
        ok = np.all(room >= np.abs(x - xg), axis=2)
        p = np.where(ok, g, p); x = np.where(ok[:, :, None, :], x, (x + xp) >> 1)
    return {"yq": x.reshape(N, 128, V).astype(np.float32).astype(BF), "yp": np.stack([gtable(a) for a in p]).astype(np.float32)}

@@ -1,0 +1,446 @@
+from concourse.bass import DstId, RemoteDMATransfer
+from concourse.mybir import AluOpType, AxisListType, ActivationFunctionType
+
+V, B, RO = 3072, 128, 3
+CH, HF, NC = 1024, 512, 3
+WC = CH // 16
+OWN, DUP = 1024, 4096
+BIG = 16384.0
+
+SCRATCH = {"tab": ("sbuf", [128, 4096], "bfloat16"), "clrs": ("sbuf", [128, 2048], "bfloat16"),
+           "c32": ("sbuf", [128, 64], "bfloat16"), "ieye": ("sbuf", [128, 128], "float32"), "eyef": ("sbuf", [128, 128], "float32"),
+           "pb": ("sbuf", [128, 128], "int32"), "s16": ("sbuf", [128, V], "float16"), "s32": ("sbuf", [128, V], "float32")}
+for _names, _w, _t in (("am am2 eye eyen eyes eyeb pbt", 128, "bfloat16"), ("z1 z2 z3", 144, "bfloat16"),
+                       ("i16 i16b", 16, "int32"), ("msk two pw pwm", 16, "float32"), ("blk blks", 8, "int32"),
+                       ("w1 w2 kf thr0 thr1 nb0 nb1", 4, "float32"), ("ki kj thi", 4, "int32"),
+                       ("vd0 vd pin ta tb tc td te tf tg th2 ti p0 p1 p2 p3 pp0 pp1 pp2 sf0 sf1 sf2", 192, "int32"),
+                       ("d0 d1", 192, "bfloat16"), ("pt po hk", 192, "float32"),
+                       ("hg de bits ab vi sbf bg y3 yo oc", V, "bfloat16"), ("x0 x1 x2", DUP + V, "bfloat16")):
+    for _n in _names.split():
+        SCRATCH[_n] = ("sbuf", [128, _w], _t)
+for _r in range(RO):
+    for _n in ("idx", "hoff", "coff", "sel"):
+        SCRATCH["%s%d" % (_n, _r)] = ("sbuf", [128, 192], "uint16")
+for _r in range(RO - 1):
+    SCRATCH["hl%d" % _r] = ("sbuf", [128, 2, 192], "int32")
+    SCRATCH["sg%d" % _r] = ("sbuf", [128, 8, 2, 8], "bfloat16")
+    SCRATCH["dg%d" % _r] = ("sbuf", [128, 2, 256], "bfloat16")
+for _n in ("ph0", "ph1", "ph2", "pc"):
+    SCRATCH[_n] = ("psum", [128, 512], "float32")
+SCRATCH["ps"] = ("psum", [128, CH], "float32")
+SCRATCH["pq"] = ("psum", [128, CH], "float32")
+
+DMAS = ["lpb0", "lpb1", "lpar", "lqb", "lq0", "lq1", "lq2", "lam", "lth", "lclr", "ldup", "ltab0", "ltab1", "syp", "loc"]
+for _r in range(RO - 1):
+    DMAS += ["tab0_%d" % _r, "tab1_%d" % _r, "own_%d" % _r] + ["%s_%d_%d" % (_n, _r, _c) for _c in range(NC) for _n in ("dup", "oc")]
+DMAS += ["syq_%d" % _k for _k in range(2 * NC)]
+SENDS = ["t0", "x0", "t1", "x1", "t2", "x2"]
+SEMAPHORES = ["qA", "qV", "qP", "qG"] + DMAS + ["arr_" + _s for _s in SENDS] + ["out_" + _s for _s in SENDS]
+
+CFGS = """
+bt_0_0_1=V bt_1_0_0=V bt_2_0_1=V bt_2_1_0=V g1_0_0_0=V g1_0_1_0=V g1_0_1_1=V g1_1_0_1=V g1_1_1_0=V g1_2_0_1=V g2_0_0_1=U
+g2_0_1_0=U g2_1_0_1=U g2_1_1_0=U g2_1_2_0=U g2_1_2_1=V g2_2_0_1=U g2_2_1_0=V g2_2_1_1=U g2_2_2_1=U g4_0_0_0=A g4_0_0_1=A
+g4_0_0_2=A g4_0_1_0=A g4_0_1_1=A g4_1_0_0=A g4_1_0_1=A g4_1_1_0=A g4_2_0_0=A g4_2_0_1=A g4_2_1_0=A g4_2_2_0=A hv_0_0_0=A
+hv_0_0_1=A hv_0_0_2=A hv_0_1_0=A hv_1_0_0=A hv_1_0_1=A hv_1_2_0=A hv_2_0_1=A hv_2_1_1=A hv_2_2_1=A hz_2_1_0=V hz_2_2_0=V
+lq1=x0 n1_1_2=1 n1_2_1=1 n1_2_2=1 n2_1_1=1 n3_0_0=1 n3_0_1=1 n3_1_0=1 n3_1_1=1 n3_1_2=1 n3_2_1=1 n3_2_2=1 n4_0_2=1
+n4_1_0=1 n4_1_1=1 na_0_1=1 na_1_2=1 na_2_0=1 nb_1_0=1
+"""
+ORDERS = """
+m_pb lpb0 lpar lqb g_i16 g_ki g_blk g_eye g_vd snd_x0 lpb1 c_i16 m_tab m_z3 c_eye m_c32 m_two c_msk i_t b_t b_d lth lam c_eyes c_eyen lq0 c_nb0 c_thr0 i_p i_f c_kj m_z1 i_d0 i_s i_d1 ltab0 snd_t0 i_s2 i_lo c_pw i_hi c_kf i_u c_pwm i_w i_z c_w1 i_idx c_blk c_cs arr_t0 ltab1 arr_x0 lq2 lq1 m_z2 c_thr1 g1_0_0_0 c_z1 g1_0_0_1 w1_0_0 g1_0_1_0 g1_0_2_0 g1_0_2_1 loc lclr ldup w1_0_2 c1_0_0 g1_0_1_1 w1_0_1 g2_0_0_1 c_eyef c_nb1 c_w2 c1_0_1 ms_0_0_1 bt_0_0_1 g2_0_1_0 c_z3 c_am2 hk_0_0 c_eyeb g2_0_0_0 g2_0_1_1 me_0_0_1 ms_0_0_0 me_0_0_0 ab_0_0_1 bt_0_0_0 ab_0_0_0 c_vd c_z2 c1_0_2 me_0_1_1 w2_0_0 ms_0_1_0 c2_0_0_0 c2_0_0_1 g2_0_2_0 bt_0_1_0 g2_0_2_1 g3_0_0_0 v1_0_0 ms_0_1_1 me_0_1_0 bt_0_1_1 ms_0_2_0 w3_0_0 w2_0_1 ms_0_2_1 p1_0_0 ab_0_1_0 me_0_2_0 me_0_2_1 bt_0_2_0 bt_0_2_1 p2_0_0 p3_0_0 c2_0_1_0 q2_0_0 q1_0_0 q5_0_0 q0_0_0 g4_0_0_0 ab_0_2_0 hk_0_1 hk_0_2 ab_0_2_1 g3_0_1_0 snd_t1 w2_0_2 c2_0_2_0 g3_0_2_0 v1_0_1 m4_0_0_0 g3_0_2_1 hv_0_0_0 w3_0_1 v1_0_2 p1_0_1 g4_0_0_1 g4_0_0_2 snd_x1 arr_t1 p2_0_1 p3_0_1 q1_0_1 q2_0_1 w3_0_2 m4_0_0_1 p1_0_2 q2_0_2 q3_0_1 q1_0_2 q3_0_0 q3_0_2 g4_0_1_1 u1_0 u0_0 hv_0_0_1 m4_0_0_2 pm_0_0 hv_0_0_2 m4_0_1_1 p2_0_2 p3_0_2 g4_0_2_0 hv_0_1_1 q4_0_0 hv_0_2_0 g4_0_1_0 pm_0_2 m4_0_1_0 pm_0_1 q4_0_1 own_0 tab1_0 tab0_0 arr_x1 hv_0_1_0
+g1_1_0_1 g1_1_1_0 g1_1_0_0 w1_1_0 c1_1_0 g2_1_0_1 g1_1_1_1 w1_1_1 hk_1_0 v1_1_0 dup_0_1 dup_0_0 dup_0_2 oc_0_2 g2_1_0_0 ms_1_0_1 ms_1_0_0 me_1_0_0 me_1_0_1 c1_1_1 q4_0_2 g1_1_2_0 w1_1_2 g2_1_1_0 bt_1_0_0 q5_0_1 c1_1_2 ab_1_0_0 ab_1_0_1 w2_1_0 ms_1_1_0 me_1_1_1 ms_1_1_1 g2_1_2_0 c2_1_0_0 bt_1_1_0 g3_1_0_0 ms_1_2_0 me_1_1_0 w3_1_0 ab_1_1_1 bt_1_1_1 bt_1_2_0 hk_1_2 ab_1_1_0 w2_1_1 g2_1_2_1 hk_1_1 ab_1_2_1 ms_1_2_1 me_1_2_0 p1_1_0 q2_1_0 q1_1_0 p2_1_0 q0_1_0 snd_t2 bt_1_2_1 p3_1_0 c2_1_1_0 q3_1_0 g3_1_1_0 ab_1_2_0 g4_1_0_0 w2_1_2 v1_1_2 v1_1_1 m4_1_0_0 c2_1_2_0 w3_1_1 g3_1_2_0 q5_0_2 p1_1_1 hv_1_0_0 g4_1_0_1 snd_x2 arr_t2 q1_1_1 p2_1_1 q2_1_1 p3_1_1 q3_1_1 w3_1_2 p1_1_2 q1_1_2 q2_1_2 q3_1_2 p2_1_2 p3_1_2 pm_1_0 pm_1_1 pm_1_2 m4_1_0_1 g4_1_2_1 q4_1_1 q4_1_0 q4_1_2 g4_1_2_0 hv_1_2_1 q5_1_0 u0_1 u1_1 own_1 tab0_1 tab1_1 g1_2_0_1 g4_1_1_0 hv_1_0_1 arr_x2 hv_1_2_0
+g1_2_0_0 m4_1_1_0 w1_2_0 hv_1_1_0 c1_2_0 g2_2_0_1 g1_2_1_0 w1_2_1 q5_1_1 c1_2_1 oc_1_2 dup_1_2 dup_1_1 dup_1_0 oc_1_1 hk_2_0 g2_2_0_0 v1_2_0 ms_2_0_1 me_2_0_1 ms_2_0_0 me_2_0_0 q5_1_2 g2_2_1_1 bt_2_0_1 g2_2_1_0 g1_2_2_0 w1_2_2 c1_2_2 g2_2_2_1 ms_2_1_1 bt_2_0_0 ms_2_1_0 w2_2_0 ab_2_0_0 bt_2_1_1 hk_2_1 me_2_1_1 g2_2_2_0 ab_2_1_1 ab_2_1_0 bt_2_1_0 c2_2_0_1 c2_2_0_0 g3_2_0_1 w2_2_1 c2_2_1_1 c2_2_1_0 g3_2_0_0 g3_2_1_0 ms_2_2_0 ms_2_2_1 me_2_2_0 me_2_2_1 w3_2_0 bt_2_2_0 bt_2_2_1 hk_2_2 ab_2_2_0 ab_2_2_1 p1_2_0 p2_2_0 w2_2_2 p3_2_0 c2_2_2_0 g4_2_0_1 v1_2_2 v1_2_1 w3_2_1 m4_2_0_1 q5_2_0 g3_2_2_0 p1_2_1 g4_2_0_0 hv_2_0_1 m4_2_0_0 w3_2_2 p2_2_1 p3_2_1 q5_2_1 hv_2_0_0 p1_2_2 g4_2_1_1 g4_2_1_0 hz_2_0_1 m4_2_1_0 p2_2_2 q5_2_2 p3_2_2 hv_2_1_0 hz_2_0_0 syq_1 syq_0 o_t hz_2_1_0 g4_2_2_0 hv_2_1_1 hz_2_1_1 syq_2 m4_2_2_0 o_p g4_2_2_1 hv_2_2_1 hv_2_2_0 syp syq_3 hz_2_2_0 hz_2_2_1 syq_4 syq_5
+"""
+CFG = {_a.split("=")[0]: (1 if _a.split("=")[1] == "1" else _a.split("=")[1]) for _a in CFGS.split()}
+ORDER = ORDERS.split()
+
+
+def build(g, T, topo, core, cfg):
+    A, AF, X = AluOpType, ActivationFunctionType, AxisListType.X
+    s = T.rank_of(core)
+    peers = [c for c in T.cores if c != core]
+    ops = []
+    vec, act, pe = g.vector, g.scalar, g.tensor
+    eng = cfg.get
+
+    def op(name, q, fn, rd, wr, cost):
+        ops.append((name, q, fn, rd, wr, cost))
+
+    def whole(n):
+        w = 1
+        for d in SCRATCH[n][1][1:]:
+            w *= d
+        return (n, 0, w)
+
+    def dma(name, q, out, in_, rd, wr, nbytes):
+        e = g.sync if q == "S" else g.scalar
+        op(name, q, lambda: e.dma_start(out(), in_()), rd, wr, ("dma", nbytes))
+
+    def ts(name, out, in0, s1, s2, o0, o1, rd, wr, n):
+        if o1 is None:
+            op(name, "V", lambda: vec.tensor_scalar(out(), in0(), s1(), None, o0), rd, wr, ("v", n))
+        else:
+            op(name, "V", lambda: vec.tensor_scalar(out(), in0(), s1(), s2(), o0, o1), rd, wr, ("v", n))
+
+    def tt(name, out, in0, in1, o, rd, wr, n):
+        op(name, "V", lambda: vec.tensor_tensor(out(), in0(), in1(), o), rd, wr, ("v", n))
+
+    def cp(name, out, in_, rd, wr, n):
+        op(name, "V", lambda: vec.tensor_copy(out(), in_()), rd, wr, ("v", n))
+
+    def ms(name, buf, lo, hi, val, n):
+        op(name, "V", lambda: vec.memset(T[buf][:, lo:hi], val), [], [(buf, lo, hi)], ("v", n))
+
+    def W(n):
+        return lambda: T[n][:]
+
+    def C(n, lo, hi):
+        return lambda: T[n][:, lo:hi]
+
+    def K(v):
+        return lambda: v
+
+    def tsw(name, out, in0, s1, s2, o0, o1):
+        ts(name, W(out), W(in0), K(s1), K(s2), o0, o1, [whole(in0)], [whole(out)], whole(out)[2])
+
+    def ttw(name, out, in0, in1, o):
+        tt(name, W(out), W(in0), W(in1), o, [whole(in0), whole(in1)], [whole(out)], 2 * whole(out)[2])
+
+    def send(tag, src, dst, rd, wr):
+        def fn():
+            m = topo.mask(core, peers[0])
+            for c in peers:
+                m &= topo.mask(core, c)
+            ids = [DstId(rid=topo.addr(c)[0], pnc=topo.addr(c)[1]) for c in peers]
+            g.remote_dma_fused([RemoteDMATransfer(dst_ids=ids, dma_engine_mask=m, remote_sem=T.sem["arr_" + tag],
+                                                  src=src(), dsts=[dst() for c in peers])], local_sem=T.sem["out_" + tag])
+            return bin(m).count("1")
+        op("snd_" + tag, "G", fn, rd, [("tok_" + tag, 0, 1)], ("send", 1))
+        op("arr_" + tag, "R", None, [("tok_" + tag, 0, 1)], wr, ("arr", 1))
+
+    def others(buf, w):
+        return [(buf, k * w, (k + 1) * w) for k in range(len(T.cores)) if k != s]
+
+    b0, b1 = s * B, s * B + B
+    ms("m_pb", "pb", 0, 128, 0, 128)
+    dma("lpb0", "S", lambda: T.pb[0:128:16, :], lambda: T.par[:, 0:8], [], [("pb", 0, 128)], 4096)
+    dma("lpb1", "A", lambda: T.pb[1:128:16, :], lambda: T.par[:, 0:8], [], [("pb1", 0, 128)], 4096)
+    dma("lpar", "S", W("pin"), lambda: T.par[:], [], [whole("pin")], 98304)
+    dma("lqb", "A", C("x0", b0, b1), lambda: T.q[:, 0:B], [], [("x0", b0, b1)], 32768)
+    dma("lam", "A", W("am"), lambda: T.amat[:], [], [whole("am")], 32768)
+    dma("lth", "A", C("thi", 0, 1), lambda: T.th[:], [], [whole("thi")], 512)
+    op("g_i16", "G", lambda: g.iota(T.i16[:], [[1, 16]], 128, -1), [], [whole("i16")], ("g", 16))
+    op("g_blk", "G", lambda: g.iota(T.blk[:], [[-16, 8]], 0, 1), [], [whole("blk")], ("g", 8))
+    op("g_eye", "G", lambda: g.iota(T.ieye[:], [[1, 128]], 0, -1, allow_small_or_imprecise_dtypes=True), [], [whole("ieye")], ("g", 128))
+    op("g_ki", "G", lambda: g.iota(T.ki[:, 0:1], [[1, 1]], 0, 1), [], [whole("ki")], ("g", 1))
+    op("g_vd", "G", lambda: g.iota(T.vd0[:], [[16, 192]], DUP, 0), [], [whole("vd0")], ("g", 192))
+    tsw("c_i16", "i16b", "i16", 15, None, A.bitwise_and, None)
+    tsw("c_msk", "msk", "i16b", 0.0, None, A.is_equal, None)
+    ms("m_tab", "tab", OWN, DUP, 0.0, 1536)
+    pbr = [whole("pb"), ("pb1", 0, 128)]
+    ts("b_t", W("pbt"), W("pb"), C("msk", 1, 2), None, A.mult, None, pbr + [whole("msk")], [whole("pbt")], 128)
+    tt("b_d", C("tab", b0, b1), W("pb"), W("pbt"), A.subtract, pbr + [whole("pbt")], [("tab", b0, b1)], 256)
+    send("t0", C("tab", b0, b1), C("tab", b0, b1), [("tab", b0, b1), ("tabr0", 0, 1), ("tabr1", 0, 1)], others("tab", B))
+    send("x0", C("x0", b0, b1), C("x0", b0, b1), [("x0", b0, b1)], others("x0", B))
+    for c in range(NC):
+        dma("lq%d" % c, "S", C("x0", OWN + c * CH, OWN + (c + 1) * CH), lambda c=c: T.q[:, c * CH:(c + 1) * CH],
+            [("tok_" + cfg["lq%d" % c], 0, 1)] if "lq%d" % c in cfg else [], [("x0", OWN + c * CH, OWN + (c + 1) * CH)], 262144)
+    dma("lclr", "S", W("clrs"), lambda: T.clr[:], [("tok_t0", 0, 1)], [whole("clrs")], 524288)
+    dma("ldup", "S", C("x0", DUP, DUP + V), lambda: T.q[:], [("tok_t0", 0, 1)], [("x0", DUP, DUP + V)], 786432)
+    tsw("i_t", "ta", "pin", float(OWN), float(B), A.is_ge, A.mult)
+    ttw("i_p", "p0", "pin", "ta", A.add)
+    cp("i_d0", W("d0"), W("p0"), [whole("p0")], [whole("d0")], 192)
+    ttw("i_d1", "d1", "p0", "d0", A.subtract)
+    dma("ltab0", "S", lambda: T.tab[0:128:16, OWN:DUP], W("d0"), [whole("d0"), ("tab", OWN, DUP)], [("tabr0", 1, 2)], 49152)
+    dma("ltab1", "A", lambda: T.tab[1:128:16, OWN:DUP], W("d1"), [whole("d1"), ("tab", OWN, DUP)], [("tabr1", 1, 2)], 49152)
+    tsw("i_hi", "tb", "p0", 4, None, A.arith_shift_right, None)
+    tsw("i_lo", "tc", "p0", 15, None, A.bitwise_and, None)
+    tsw("i_s", "td", "p0", 7, None, A.arith_shift_right, None)
+    tsw("i_s2", "te", "td", 8.0, 120.0, A.min, A.mult)
+    tsw("i_f", "tf", "ta", 184.0 / 128.0, 8.0, A.mult, A.add)
+    ttw("i_u", "tg", "tc", "tf", A.mult)
+    ttw("i_w", "th2", "tb", "te", A.add)
+    ttw("i_z", "ti", "tg", "th2", A.add)
+    cp("i_idx", W("idx0"), W("ti"), [whole("ti")], [whole("idx0")], 192)
+    for z in ("z1", "z2", "z3"):
+        ms("m_" + z, z, 0, 144, 0.0, 72)
+    ms("m_c32", "c32", 0, 64, 32.0, 32)
+    ms("m_two", "two", 0, 16, 2.0, 16)
+    tsw("c_blk", "blks", "blk", 4, None, A.arith_shift_right, None)
+    op("c_w1", "V", lambda: vec.tensor_reduce(T.w1[:, 0:1], T.msk[:, 0:2], X, A.add), [whole("msk")], [whole("w1")], ("v", 2))
+    op("c_pw", "V", lambda: vec.tensor_tensor_scan(T.pw[:], T.two[:], T.two[:], 2.0, A.mult, A.max), [whole("two")], [whole("pw")], ("v", 16))
+    ttw("c_pwm", "pwm", "pw", "msk", A.mult)
+    op("c_w2", "V", lambda: vec.tensor_reduce(T.w2[:, 0:1], T.pwm[:, 0:11], X, A.add), [whole("pwm")], [whole("w2")], ("v", 11))
+    for z, wt, rd in (("z1", C("w1", 0, 1), [whole("w1")]), ("z2", C("w2", 0, 1), [whole("w2")]), ("z3", K(-BIG), [])):
+        ts("c_" + z, lambda z=z: T[z][:, 15:143:16], W("blks"), K(0.0), wt, A.is_equal, A.mult, [whole("blks")] + rd, [whole(z)], 8)
+    tsw("c_eye", "eye", "ieye", 0.0, None, A.is_equal, None)
+    tsw("c_eyef", "eyef", "ieye", 0.0, None, A.is_equal, None)
+    for n, src, sc in (("eyen", "eye", -1.0), ("eyes", "eye", 1.0 / 16), ("eyeb", "eye", 256.0), ("am2", "am", 2.0)):
+        op("c_" + n, "A", lambda n=n, src=src, sc=sc: act.activation(T[n][:], T[src][:], AF.Identity, scale=sc),
+           [whole(src)], [whole(n)], ("a", 128))
+    ts("c_kj", C("kj", 0, 1), C("ki", 0, 1), K(15), None, A.bitwise_and, None, [whole("ki")], [whole("kj")], 1)
+    cp("c_kf", C("kf", 0, 1), C("kj", 0, 1), [whole("kj")], [whole("kf")], 1)
+    ts("c_vd", W("vd"), W("vd0"), C("kf", 0, 1), None, A.add, None, [whole("vd0"), whole("kf")], [whole("vd")], 192)
+    cp("c_thr0", C("thr0", 0, 1), C("thi", 0, 1), [whole("thi")], [whole("thr0")], 1)
+    ts("c_nb0", C("nb0", 0, 1), C("thi", 0, 1), K(-1.0), K(-0.5), A.mult, A.add, [whole("thi")], [whole("nb0")], 1)
+    op("c_cs", "P", lambda: pe.matmul(T.pc[:, 0:1], T.am[:], T.c32[:, 0:1], True, True), [whole("am"), whole("c32")], [whole("pc")], ("p", 64))
+    ts("c_thr1", C("thr1", 0, 1), C("pc", 0, 1), K(8.0), C("thr0", 0, 1), A.mult, A.add, [whole("pc"), whole("thr0")], [whole("thr1")], 1)
+    ts("c_nb1", C("nb1", 0, 1), C("thr1", 0, 1), K(-1.0), K(-0.5), A.mult, A.add, [whole("thr1")], [whole("nb1")], 1)
+
+    def wrap(name, bank, z, data, c, first):
+        def fn():
+            for i in range(16):
+                ins = pe.matmul(T[bank][:, 0:WC], T[z][:, 15 - i:143 - i], T[data][:, c * CH + i:(c + 1) * CH:16],
+                                first and i == 0, i == 15)
+            return ins
+        op(name, "P", fn, [whole(z), (data, c * CH, (c + 1) * CH)], [whole(bank)], ("p", 64 * 16))
+
+    def gather(name, e, out, lo, hi, win, whi, off, rd):
+        a, b = lo // 16, hi // 16
+        if e == "A":
+            op(name, "A", lambda: act.activation(T[out][:, lo:hi], T[win][:, 0:whi].indirect(T[off][:, a:b]), AF.Identity),
+               rd + [(off, a, b)], [(out, lo, hi)], ("ga", hi - lo))
+        else:
+            op(name, "V", lambda: vec.tensor_copy(T[out][:, lo:hi], T[win][:, 0:whi].indirect(T[off][:, a:b])),
+               rd + [(off, a, b)], [(out, lo, hi)], ("gv", hi - lo))
+
+    def gtt(name, out, lo, hi, win, whi, off, in1, l1, o):
+        a, b = lo // 16, hi // 16
+        op(name, "V", lambda: vec.tensor_tensor(T[out][:, lo:hi], T[win][:, 0:whi].indirect(T[off][:, a:b]), T[in1][:, l1:l1 + hi - lo], o),
+           [(win, 0, whi), (off, a, b), (in1, l1, l1 + hi - lo)], [(out, lo, hi)], ("gt", hi - lo))
+
+    def banks(b, lo, hi):
+        return (b, lo % CH // HF * HF, ((hi - 1) % CH // HF + 1) * HF)
+
+    def two(name, bank, l0, l1, data, lo, hi, x):
+        def fn():
+            for a, b in ((lo, min(hi, lo // HF * HF + HF)), (lo // HF * HF + HF, hi)):
+                if a < b:
+                    o = T[bank][:, a % CH:a % CH + b - a]
+                    pe.matmul(o, T[l1][:], T[x][:, OWN + a:OWN + b], True, False)
+                    ins = pe.matmul(o, T[l0][:], T[data][:, a:b], False, True)
+            return ins
+        op(name, "P", fn, [whole(l0), whole(l1), (data, lo, hi), (x, OWN + lo, OWN + hi)], [banks(bank, lo, hi)], ("p", 2 * (hi - lo)))
+
+    def cuts(tag, r, c):
+        lo = c * CH
+        return [(lo, lo + CH)] if cfg.get("%s_%d_%d" % (tag, r, c), 2) == 1 else [(lo, lo + HF), (lo + HF, lo + CH)]
+
+    def cuts4(r, c):
+        cs = cuts("n4", r, c)
+        return [(0, B), (B, cs[0][1])] + cs[1:] if c == 0 and r < RO - 1 else cs
+
+    def hull(r, chunks):
+        cs = [a for c in chunks for k, a in enumerate(cuts4(r, c)) if eng("g4_%d_%d_%d" % (r, c, k), "V") == "V"]
+        return (cs[0][0], cs[-1][1]) if cs else None
+
+    h0 = hull(0, range(NC))
+    if h0:
+        dma("loc", "S", C("oc", h0[0], h0[1]), lambda: T.q[:, h0[0]:h0[1]], [("tok_t0", 0, 1)], [("oc", h0[0], h0[1])], 256 * (h0[1] - h0[0]))
+    tabrd = [whole("tab"), ("tabr0", 0, 2), ("tabr1", 0, 2)]
+    for r in range(RO):
+        x, xn = "x%d" % r, "x%d" % (r + 1)
+        idx, hoff, coff, sel = "idx%d" % r, "hoff%d" % r, "coff%d" % r, "sel%d" % r
+        p, pn, pp, sf = "p%d" % r, "p%d" % (r + 1), "pp%d" % r, "sf%d" % r
+        thr, nb = ("thr0", "nb0") if r == 0 else ("thr1", "nb1")
+        last = r == RO - 1
+        for c in range(NC):
+            for k, (lo, hi) in enumerate(cuts("n1", r, c)):
+                t = "g1_%d_%d_%d" % (r, c, k)
+                gather(t, eng(t, "A"), "hg", lo, hi, "tab", 4096, idx, tabrd)
+            ph = "ph%d" % c
+            wrap("w1_%d_%d" % (r, c), ph, "z1", "hg", c, True)
+            cp("c1_%d_%d" % (r, c), C(hoff, c * WC, (c + 1) * WC), C(ph, 0, WC), [whole(ph)], [(hoff, c * WC, (c + 1) * WC)], WC)
+            hk = ("hk", c * WC, (c + 1) * WC)
+            op("hk_%d_%d" % (r, c), "A", lambda ph=ph, hk=hk: act.activation(T.hk[:, hk[1]:hk[2]], T[ph][:, 0:WC], AF.Identity, bias=BIG / 2),
+               [whole(ph)], [hk], ("a", WC))
+            op("v1_%d_%d" % (r, c), "P", lambda ph=ph, hk=hk: pe.matmul(T[ph][:, 0:WC], T.eyef[:], T.hk[:, hk[1]:hk[2]], True, False),
+               [hk, whole("eyef")], [whole(ph)], ("p", 4 * WC))
+        for c in range(NC):
+            ph = "ph%d" % c
+            form = []
+            for k, (lo, hi) in enumerate(cuts("n2", r, c)):
+                t = "g2_%d_%d_%d" % (r, c, k)
+                form += ["V" if eng(t, "A") == "V" else "A"] * ((hi - lo) // HF)
+                if eng(t, "A") != "V":
+                    gather(t, eng(t, "A"), "de", lo, hi, x, DUP, hoff, [(x, 0, DUP)])
+                else:
+                    gtt(t, "de", lo, hi, x, DUP, hoff, x, DUP + lo, A.subtract)
+            for k in range(2):
+                lo = c * CH + k * HF
+                two("ms_%d_%d_%d" % (r, c, k), "ps", "am", "am" if form[k] == "A" else "am2", "de", lo, lo + HF, x)
+                if form[k] == "A":
+                    two("me_%d_%d_%d" % (r, c, k), "pq", "eye", "eyen", "de", lo, lo + HF, x)
+            for k, (lo, hi) in enumerate(cuts("na" if form[0] == form[1] else "halves", r, c)):
+                src, a, b = ("pq", lo % CH, lo % CH + hi - lo) if form[k] == "A" else ("de", lo, hi)
+                op("ab_%d_%d_%d" % (r, c, k), "A", lambda src=src, a=a, b=b, lo=lo, hi=hi: act.activation(T.ab[:, lo:hi], T[src][:, a:b], AF.Abs),
+                   [(src, a, b)], [("ab", lo, hi)], ("a", hi - lo))
+            be = []
+            for k, (lo, hi) in enumerate(cuts("nb", r, c)):
+                t = "bt_%d_%d_%d" % (r, c, k)
+                a, b = lo % CH, lo % CH + hi - lo
+                be += [eng(t, "A")] * ((hi - lo) // HF)
+                if eng(t, "A") == "A":
+                    op(t, "A", lambda a=a, b=b, lo=lo, hi=hi, nb=nb: act.activation(T.bits[:, lo:hi], T.ps[:, a:b], AF.Sign, bias=T[nb][:, 0:1]),
+                       [("ps", a, b), whole(nb)], [("bits", lo, hi)], ("a", hi - lo))
+                else:
+                    ts(t, C("bits", lo, hi), C("ps", a, b), C(thr, 0, 1), K(2.0), A.is_gt, A.mult, [("ps", a, b), whole(thr)], [("bits", lo, hi)], hi - lo)
+            t = "%d_%d" % (r, c)
+            m0, m1 = c * WC, (c + 1) * WC
+            wrap("w2_" + t, "pc", "z2", "bits", c, True)
+            spans = [(0, WC, be[0])] if be[0] == be[1] else [(0, WC // 2, be[0]), (WC // 2, WC, be[1])]
+            for j, (a, b, e) in enumerate(spans):
+                ts("c2_%s_%d" % (t, j), C(coff, m0 + a, m0 + b), C("pc", a, b), K(0.125), K(1023.5 if e == "A" else 0.0), A.mult, A.add,
+                   [whole("pc")], [(coff, m0 + a, m0 + b)], b - a)
+            for k, (lo, hi) in enumerate(cuts("n3", r, c)):
+                gtt("g3_%s_%d" % (t, k), "vi", lo, hi, "clrs", 2048, coff, "ab", lo, A.is_lt)
+            wrap("w3_" + t, ph, "z3", "vi", c, False)
+            tt("p1_" + t, C(pp, m0, m1), C(ph, 0, WC), C(p, m0, m1), A.max, [whole(ph), (p, m0, m1)], [(pp, m0, m1)], WC)
+            tt("p2_" + t, C(sf, m0, m1), C(pp, m0, m1), C("vd", m0, m1), A.min, [(pp, m0, m1), ("vd", m0, m1)], [(sf, m0, m1)], 2 * WC)
+            cp("p3_" + t, C(sel, m0, m1), C(sf, m0, m1), [(sf, m0, m1)], [(sel, m0, m1)], WC)
+            ts("q5_" + t, C(pn, m0, m1), C(pp, m0, m1), K(4095), None, A.bitwise_and, None, [(pp, m0, m1)], [(pn, m0, m1)], WC)
+            if not last:
+                hl, dg, sg, idn = "hl%d" % r, "dg%d" % r, "sg%d" % r, "idx%d" % (r + 1)
+                for j, bitmask in enumerate((0xFF0, 15)):
+                    ts("q%d_%s" % (j + 1, t), lambda hl=hl, j=j, m0=m0, m1=m1: T[hl][:, j, m0:m1], C(pp, m0, m1), K(bitmask), None,
+                       A.bitwise_and, None, [(pp, m0, m1)], [(hl, 192 * j + m0, 192 * j + m1)], WC)
+                hr = [(hl, m0, m1), (hl, 192 + m0, 192 + m1)]
+                dw = [(dg, 64 + m0, 64 + m1), (dg, 320 + m0, 320 + m1)]
+                if c == 0:
+                    ow = [(sg, 16 * s, 16 * s + 16)]
+                    cp("q0_" + t, lambda sg=sg: T[sg][:, s, :, :], lambda hl=hl: T[hl][:, :, 0:8], hr, ow, 16)
+                    send("t%d" % (r + 1), lambda sg=sg: T[sg][:, s, :, :], lambda sg=sg: T[sg][:, s, :, :], ow, others(sg, 16))
+                    for j in range(2):
+                        op("u%d_%d" % (j, r), "A", lambda sg=sg, dg=dg, j=j: act.activation(T[dg][:, j, 0:64], T[sg][:, :, j, :], AF.Identity),
+                           [whole(sg)], [(dg, 256 * j, 256 * j + 64)], ("a", 64))
+                cp("q3_" + t, lambda dg=dg, m0=m0, m1=m1: T[dg][:, :, 64 + m0:64 + m1], lambda hl=hl, m0=m0, m1=m1: T[hl][:, :, m0:m1], hr, dw, 2 * WC)
+
+                def perm(ph=ph, dg=dg, m0=m0, m1=m1):
+                    pe.matmul(T[ph][:, 0:WC], T.eyes[:], T[dg][:, 0, 64 + m0:64 + m1], True, False)
+                    return pe.matmul(T[ph][:, 0:WC], T.eyeb[:], T[dg][:, 1, 64 + m0:64 + m1], False, True)
+                op("pm_" + t, "P", perm, dw + [whole("eyes"), whole("eyeb")], [whole(ph)], ("p", 128))
+                cp("q4_" + t, C(idn, m0, m1), C(ph, 0, WC), [whole(ph)], [(idn, m0, m1)], WC)
+        if not last:
+            dg = "dg%d" % r
+            dma("tab0_%d" % r, "S", lambda: T.tab[0:128:16, :], lambda dg=dg: T[dg][:, 0, :], [(dg, 0, 256)], [("tabr0", 0, 2)], 65536)
+            dma("tab1_%d" % r, "S", lambda: T.tab[1:128:16, :], lambda dg=dg: T[dg][:, 1, :], [(dg, 256, 512)], [("tabr1", 0, 2)], 65536)
+        else:
+            tsw("o_t", "pt", pn, float(OWN), float(B), A.is_ge, A.mult)
+            ttw("o_p", "po", pn, "pt", A.subtract)
+            dma("syp", "S", lambda: T.yp[:], W("po"), [whole("po")], [], 98304)
+        for c in range(NC):
+            for k, (lo, hi) in enumerate(cuts4(r, c)):
+                t = "%d_%d_%d" % (r, c, k)
+                e = eng("hv_" + t, "V")
+                n = hi - lo
+                if eng("g4_" + t, "V") == "A":
+                    gather("g4_" + t, "A", "bg", lo, hi, x, DUP + V, sel, [(x, 0, DUP + V)])
+                    two("m4_" + t, "pq", "eye", "eye", "bg", lo, hi, x)
+                    sb, a, rd, cyc = "pq", lo % CH, banks("pq", lo, hi), n
+                else:
+                    sb = "sbf" if r == 0 else ("s32" if e == "A" else "s16")
+                    gtt("g4_" + t, sb, lo, hi, x, DUP + V, sel, "oc", lo, A.add)
+                    a, rd, cyc = lo, (sb, lo, hi), n // 2
+                bias = 127.875 if r == 0 else -0.125
+                ob, o0 = ("y3", lo) if last else (xn, OWN + lo)
+                if e == "A":
+                    op("hv_" + t, "A", lambda ob=ob, o0=o0, sb=sb, a=a, n=n, bias=bias:
+                       act.activation(T[ob][:, o0:o0 + n], T[sb][:, a:a + n], AF.Identity, bias=bias, scale=0.5), [rd], [(ob, o0, o0 + n)], ("a", n))
+                else:
+                    ts("hv_" + t, C(ob, o0, o0 + n), C(sb, a, a + n), K(0.5), K(bias), A.mult, A.add, [rd], [(ob, o0, o0 + n)], cyc)
+                if last:
+                    if eng("hz_" + t, "A") == "A":
+                        op("hz_" + t, "A", lambda lo=lo, hi=hi: act.activation(T.yo[:, lo:hi], T.y3[:, lo:hi], AF.Identity, bias=-128.0),
+                           [("y3", lo, hi)], [("yo", lo, hi)], ("a", n))
+                    else:
+                        ts("hz_" + t, C("yo", lo, hi), C("y3", lo, hi), K(-128.0), None, A.add, None, [("y3", lo, hi)], [("yo", lo, hi)], n // 2)
+                    dma("syq_%d" % (2 * c + k), "S", lambda lo=lo, hi=hi: T.yq[:, lo:hi], C("yo", lo, hi), [("yo", lo, hi)], [], 256 * n)
+                elif c == 0 and k == 0:
+                    send("x%d" % (r + 1), C(xn, OWN, OWN + B), C(xn, b0, b1), [(xn, OWN, OWN + B)], others(xn, B))
+                    dma("own_%d" % r, "S", C(xn, b0, b1), C(xn, OWN, OWN + B), [(xn, OWN, OWN + B)], [(xn, b0, b1)], 32768)
+            if not last:
+                dma("dup_%d_%d" % (r, c), "S", C(xn, DUP + c * CH, DUP + (c + 1) * CH), C(xn, OWN + c * CH, OWN + (c + 1) * CH),
+                    [(xn, OWN + c * CH, OWN + (c + 1) * CH)], [(xn, DUP + c * CH, DUP + (c + 1) * CH)], 262144)
+                h = hull(r + 1, [c])
+                if h:
+                    dma("oc_%d_%d" % (r, c), "S", C("oc", h[0], h[1]), C(xn, OWN + h[0], OWN + h[1]),
+                        [(xn, OWN + h[0], OWN + h[1])], [("oc", h[0], h[1])], 256 * (h[1] - h[0]))
+    return ops
+
+
+def hazards(ops):
+    seen = {}
+    deps = {}
+    for o in ops:
+        name, q = o[0], o[1]
+        d = {"m_pb"} if name == "lpb1" else set()
+        acc = [(a, False) for a in o[3]] + [(a, True) for a in o[4]]
+        for (b, lo, hi), w in acc:
+            bank = b in SCRATCH and SCRATCH[b][0] == "psum"
+            for (n2, q2, l2, h2, w2) in seen.get(b, []):
+                if l2 < hi and lo < h2 and (w or w2 or (bank and q2 != q)):
+                    d.add(n2)
+        for (b, lo, hi), w in acc:
+            seen.setdefault(b, []).append((name, q, lo, hi, w))
+        deps[name] = d
+    return deps
+
+
+def rank_program(g, core, T, topo):
+    if T.rank_of(core) is None:
+        return
+    ops = build(g, T, topo, core, CFG)
+    deps = hazards(ops)
+    byname = {o[0]: o for o in ops}
+    order = list(ORDER)
+    queue = {"A": g.scalar, "V": g.vector, "P": g.tensor, "S": g.sync, "G": g}
+    npeer = len(T.cores) - 1
+    kind = {n: byname[n][5][0] for n in order}
+    pos = {n: i for i, n in enumerate(order)}
+
+    known = {q: set() for q in queue}
+    done_on = {q: [] for q in queue}
+    after = {}
+    waits = {}
+    for n in order:
+        q = byname[n][1]
+        if q == "R":
+            after[n] = {n}
+            continue
+        waits[n] = []
+        for d in sorted(deps[n], key=lambda a: -pos[a]):
+            if d not in known[q]:
+                waits[n].append(d)
+                known[q] |= after[d]
+        after[n] = known[q] | {n}
+        if kind[n] not in ("dma", "send"):
+            done_on[q].append(n)
+            after[n] |= set(done_on[q])
+    waited = set(done_on[q][-1] for q in done_on if done_on[q])
+    for n in waits:
+        waited |= set(waits[n])
+
+    count = {q: 0 for q in queue}
+    mark = {}
+    for n in order:
+        o = byname[n]
+        q = o[1]
+        if q == "R":
+            mark[n] = (n, mark["snd_" + n[4:]][1] * npeer)
+            continue
+        for d in waits[n]:
+            queue[q].wait_ge(T.sem[mark[d][0]], mark[d][1])
+        ins = o[2]()
+        if kind[n] == "dma":
+            ins.then_inc(T.sem[n], 16)
+            mark[n] = (n, 16)
+        elif kind[n] == "send":
+            mark[n] = ("out_" + n[4:], ins)
+        elif n in waited:
+            count[q] += 1
+            ins.then_inc(T.sem["q" + q], 1)
+            mark[n] = ("q" + q, count[q])
+    for n in order:
+        if kind[n] in ("dma", "send", "arr") and n not in waited:
+            g.wait_ge(T.sem[mark[n][0]], mark[n][1])
+    for q in ("A", "V", "P", "G"):
+        g.wait_ge(T.sem["q" + q], count[q])

@@ -2,56 +2,50 @@ from concourse.bass import DstId, RemoteDMATransfer
 from concourse.mybir import AluOpType, AxisListType, ActivationFunctionType
 
 V, B, RO = 3072, 128, 3
-CH, HF, NC = 1024, 512, 3
-WC = CH // 16
-OWN, DUP = 1024, 4096
-BIG = 16384.0
+M, NW, HF = 1024, 3968, 512
+TW = NW // 16
+BIG = 65536.0
+FLAG = (8192.0, 16384.0, 32768.0)
+MAGIC = 1.5 * 2 ** 23
 
-SCRATCH = {"tab": ("sbuf", [128, 4096], "bfloat16"), "clrs": ("sbuf", [128, 2048], "bfloat16"),
+SCRATCH = {"tab": ("sbuf", [128, NW], "bfloat16"), "clrs": ("sbuf", [128, 2048], "bfloat16"),
            "c32": ("sbuf", [128, 64], "bfloat16"), "ieye": ("sbuf", [128, 128], "float32"), "eyef": ("sbuf", [128, 128], "float32"),
-           "pb": ("sbuf", [128, 128], "int32"), "s16": ("sbuf", [128, V], "float16"), "s32": ("sbuf", [128, V], "float32")}
-for _names, _w, _t in (("am am2 eye eyen eyes eyeb pbt", 128, "bfloat16"), ("z1 z2 z3", 144, "bfloat16"),
+           "pb": ("sbuf", [128, 128], "int32"), "s16": ("sbuf", [128, V], "float16"), "s32": ("sbuf", [128, V], "float32"),
+           "hl": ("sbuf", [128, 2, 192], "int32"), "di": ("sbuf", [128, 2, 192], "bfloat16")}
+for _names, _w, _t in (("am am2 eye eyen eyes eyeb eye8 eyeu eyeh eyeg pbt", 128, "bfloat16"), ("z1 z2 z3", 144, "bfloat16"),
                        ("i16 i16b", 16, "int32"), ("msk two pw pwm", 16, "float32"), ("blk blks", 8, "int32"),
                        ("w1 w2 kf thr0 thr1 nb0 nb1", 4, "float32"), ("ki kj thi", 4, "int32"),
-                       ("vd0 vd pin ta tb tc td te tf tg th2 ti p0 p1 p2 p3 pp0 pp1 pp2 sf0 sf1 sf2", 192, "int32"),
-                       ("d0 d1", 192, "bfloat16"), ("pt po hk", 192, "float32"),
-                       ("hg de bits ab vi sbf bg y3 yo oc", V, "bfloat16"), ("x0 x1 x2", DUP + V, "bfloat16")):
+                       ("vd0 vd vd1 vd2 td p0 p3 pp0 pp1 pp2 sf0 sf1 sf2 sg0 sg1 sg2", 192, "int32"),
+                       ("te tf tg", 192, "bfloat16"), ("po hk", 192, "float32"),
+                       ("hg de bits ab vi sbf bg y3 yo", V, "bfloat16"), ("x0 x1 x2", NW + V, "bfloat16")):
     for _n in _names.split():
         SCRATCH[_n] = ("sbuf", [128, _w], _t)
 for _r in range(RO):
     for _n in ("idx", "hoff", "coff", "sel"):
         SCRATCH["%s%d" % (_n, _r)] = ("sbuf", [128, 192], "uint16")
 for _r in range(RO - 1):
-    SCRATCH["hl%d" % _r] = ("sbuf", [128, 2, 192], "int32")
-    SCRATCH["sg%d" % _r] = ("sbuf", [128, 8, 2, 8], "bfloat16")
+    SCRATCH["sb%d" % _r] = ("sbuf", [128, 8, 2, 8], "bfloat16")
     SCRATCH["dg%d" % _r] = ("sbuf", [128, 2, 256], "bfloat16")
-for _n in ("ph0", "ph1", "ph2", "pc"):
-    SCRATCH[_n] = ("psum", [128, 512], "float32")
-SCRATCH["ps"] = ("psum", [128, CH], "float32")
-SCRATCH["pq"] = ("psum", [128, CH], "float32")
+for _n in ("pa", "pz", "pc", "pd"):
+    SCRATCH[_n] = ("psum", [128, HF], "float32")
+SCRATCH["ps"] = ("psum", [128, 2 * HF], "float32")
+SCRATCH["pq"] = ("psum", [128, 2 * HF], "float32")
 
-DMAS = ["lpb0", "lpb1", "lpar", "lqb", "lq0", "lq1", "lq2", "lam", "lth", "lclr", "ldup", "ltab0", "ltab1", "syp", "loc"]
+DMAS = ["lpb0", "lpb1", "lpar", "lqb", "lq0", "lq1", "lq2", "lam", "lth", "lclr", "ldup0", "ldup1", "ldup2", "ltab0", "ltab1", "syp"]
 for _r in range(RO - 1):
-    DMAS += ["tab0_%d" % _r, "tab1_%d" % _r, "own_%d" % _r] + ["%s_%d_%d" % (_n, _r, _c) for _c in range(NC) for _n in ("dup", "oc")]
-DMAS += ["syq_%d" % _k for _k in range(2 * NC)]
+    DMAS += ["tab0_%d" % _r, "tab1_%d" % _r] + ["dup_%d_%d" % (_r, _c) for _c in range(5)]
+DMAS += ["syq_%d_%d" % (_c, _k) for _c in range(4) for _k in range(5)]
 SENDS = ["t0", "x0", "t1", "x1", "t2", "x2"]
 SEMAPHORES = ["qA", "qV", "qP", "qG"] + DMAS + ["arr_" + _s for _s in SENDS] + ["out_" + _s for _s in SENDS]
 
 CFGS = """
-bt_0_0_1=V bt_1_0_0=V bt_2_0_1=V bt_2_1_0=V g1_0_0_0=V g1_0_1_0=V g1_0_1_1=V g1_1_0_1=V g1_1_1_0=V g1_2_0_1=V g2_0_0_1=U
-g2_0_1_0=U g2_1_0_1=U g2_1_1_0=U g2_1_2_0=U g2_1_2_1=V g2_2_0_1=U g2_2_1_0=V g2_2_1_1=U g2_2_2_1=U g4_0_0_0=A g4_0_0_1=A
-g4_0_0_2=A g4_0_1_0=A g4_0_1_1=A g4_1_0_0=A g4_1_0_1=A g4_1_1_0=A g4_2_0_0=A g4_2_0_1=A g4_2_1_0=A g4_2_2_0=A hv_0_0_0=A
-hv_0_0_1=A hv_0_0_2=A hv_0_1_0=A hv_1_0_0=A hv_1_0_1=A hv_1_2_0=A hv_2_0_1=A hv_2_1_1=A hv_2_2_1=A hz_2_1_0=V hz_2_2_0=V
-lq1=x0 n1_1_2=1 n1_2_1=1 n1_2_2=1 n2_1_1=1 n3_0_0=1 n3_0_1=1 n3_1_0=1 n3_1_1=1 n3_1_2=1 n3_2_1=1 n3_2_2=1 n4_0_2=1
-n4_1_0=1 n4_1_1=1 na_0_1=1 na_1_2=1 na_2_0=1 nb_1_0=1
+Qdup_0_0=A Qdup_0_1=A Qlclr=A Qlq2=A Qtab0_0=A Wlclr=x0 Wldup0=t0 Wldup1=t0 Wldup2=t0 Wlq2=x0 bt_0_0_0=V bt_0_0_1=V bt_1_0_0=V bt_1_0_1=V bt_2_0_1=V bt_2_1_1=V cp_0_0=0 cp_0_1=0 cp_1_0=0 cp_1_1=0 cp_1_2=0 cp_2_1=0 cq_0_2=0 cq_2_2=0 em4_1_0_1=1 em4_1_0_2=1 em4_1_2_1=1 em4_2_0_1=1 em4_2_0_2=1 eme_0_0_1=1 eme_0_1_0=1 eme_1_0_0=1 eme_2_1_0=1 ems_0_0_0=1 ems_0_0_1=1 ems_1_0_0=1 ems_1_0_1=1 ems_1_1_1=1 ems_2_0_1=1 ems_2_1_1=1 fm_0_1=1 fm_2_0=1 g1_0_0_1=V g1_0_1_1=V g1_1_0_0=V g1_1_1_1=V g1_2_0_1=V g1_2_2_1=V g2_0_0_0=V g2_0_1_1=U g2_0_2_0=V g2_0_2_1=V g2_1_0_1=V g2_1_1_1=V g2_1_2_1=V g2_2_0_0=V g2_2_0_1=V g2_2_1_1=V g2_2_2_1=V g4_0_0_0=A g4_0_0_1=A g4_0_1_0=A g4_0_1_1=A g4_1_0_1=A g4_1_0_2=A g4_1_1_0=A g4_1_2_1=A g4_2_0_1=A g4_2_0_2=A g4_2_1_0=A g4_2_2_1=A hk_0_0=V hk_1_0=V hk_2_1=V hv_0_0_1=A hv_0_1_0=A hv_0_1_1=A hv_1_0_0=A hv_1_0_1=A hv_1_0_2=A hv_1_1_0=A hv_1_2_1=A hv_2_0_0=A hv_2_0_1=A hv_2_0_2=A hv_2_2_0=A hz_2_0_0=A hz_2_0_2=A hz_2_1_1=A n1_0_2=1 n1_1_2=1 n1_2_1=1 n3_0_0=1 n3_0_1=1 n3_1_1=1 n3_2_0=1 n3_2_2=1 n4_0_0=1 n4_0_2=1 na_0_0=1 na_0_1=1 na_1_2=1 na_2_0=1 na_2_2=1 nb_2_2=1 one=0
 """
 ORDERS = """
-m_pb lpb0 lpar lqb g_i16 g_ki g_blk g_eye g_vd snd_x0 lpb1 c_i16 m_tab m_z3 c_eye m_c32 m_two c_msk i_t b_t b_d lth lam c_eyes c_eyen lq0 c_nb0 c_thr0 i_p i_f c_kj m_z1 i_d0 i_s i_d1 ltab0 snd_t0 i_s2 i_lo c_pw i_hi c_kf i_u c_pwm i_w i_z c_w1 i_idx c_blk c_cs arr_t0 ltab1 arr_x0 lq2 lq1 m_z2 c_thr1 g1_0_0_0 c_z1 g1_0_0_1 w1_0_0 g1_0_1_0 g1_0_2_0 g1_0_2_1 loc lclr ldup w1_0_2 c1_0_0 g1_0_1_1 w1_0_1 g2_0_0_1 c_eyef c_nb1 c_w2 c1_0_1 ms_0_0_1 bt_0_0_1 g2_0_1_0 c_z3 c_am2 hk_0_0 c_eyeb g2_0_0_0 g2_0_1_1 me_0_0_1 ms_0_0_0 me_0_0_0 ab_0_0_1 bt_0_0_0 ab_0_0_0 c_vd c_z2 c1_0_2 me_0_1_1 w2_0_0 ms_0_1_0 c2_0_0_0 c2_0_0_1 g2_0_2_0 bt_0_1_0 g2_0_2_1 g3_0_0_0 v1_0_0 ms_0_1_1 me_0_1_0 bt_0_1_1 ms_0_2_0 w3_0_0 w2_0_1 ms_0_2_1 p1_0_0 ab_0_1_0 me_0_2_0 me_0_2_1 bt_0_2_0 bt_0_2_1 p2_0_0 p3_0_0 c2_0_1_0 q2_0_0 q1_0_0 q5_0_0 q0_0_0 g4_0_0_0 ab_0_2_0 hk_0_1 hk_0_2 ab_0_2_1 g3_0_1_0 snd_t1 w2_0_2 c2_0_2_0 g3_0_2_0 v1_0_1 m4_0_0_0 g3_0_2_1 hv_0_0_0 w3_0_1 v1_0_2 p1_0_1 g4_0_0_1 g4_0_0_2 snd_x1 arr_t1 p2_0_1 p3_0_1 q1_0_1 q2_0_1 w3_0_2 m4_0_0_1 p1_0_2 q2_0_2 q3_0_1 q1_0_2 q3_0_0 q3_0_2 g4_0_1_1 u1_0 u0_0 hv_0_0_1 m4_0_0_2 pm_0_0 hv_0_0_2 m4_0_1_1 p2_0_2 p3_0_2 g4_0_2_0 hv_0_1_1 q4_0_0 hv_0_2_0 g4_0_1_0 pm_0_2 m4_0_1_0 pm_0_1 q4_0_1 own_0 tab1_0 tab0_0 arr_x1 hv_0_1_0
-g1_1_0_1 g1_1_1_0 g1_1_0_0 w1_1_0 c1_1_0 g2_1_0_1 g1_1_1_1 w1_1_1 hk_1_0 v1_1_0 dup_0_1 dup_0_0 dup_0_2 oc_0_2 g2_1_0_0 ms_1_0_1 ms_1_0_0 me_1_0_0 me_1_0_1 c1_1_1 q4_0_2 g1_1_2_0 w1_1_2 g2_1_1_0 bt_1_0_0 q5_0_1 c1_1_2 ab_1_0_0 ab_1_0_1 w2_1_0 ms_1_1_0 me_1_1_1 ms_1_1_1 g2_1_2_0 c2_1_0_0 bt_1_1_0 g3_1_0_0 ms_1_2_0 me_1_1_0 w3_1_0 ab_1_1_1 bt_1_1_1 bt_1_2_0 hk_1_2 ab_1_1_0 w2_1_1 g2_1_2_1 hk_1_1 ab_1_2_1 ms_1_2_1 me_1_2_0 p1_1_0 q2_1_0 q1_1_0 p2_1_0 q0_1_0 snd_t2 bt_1_2_1 p3_1_0 c2_1_1_0 q3_1_0 g3_1_1_0 ab_1_2_0 g4_1_0_0 w2_1_2 v1_1_2 v1_1_1 m4_1_0_0 c2_1_2_0 w3_1_1 g3_1_2_0 q5_0_2 p1_1_1 hv_1_0_0 g4_1_0_1 snd_x2 arr_t2 q1_1_1 p2_1_1 q2_1_1 p3_1_1 q3_1_1 w3_1_2 p1_1_2 q1_1_2 q2_1_2 q3_1_2 p2_1_2 p3_1_2 pm_1_0 pm_1_1 pm_1_2 m4_1_0_1 g4_1_2_1 q4_1_1 q4_1_0 q4_1_2 g4_1_2_0 hv_1_2_1 q5_1_0 u0_1 u1_1 own_1 tab0_1 tab1_1 g1_2_0_1 g4_1_1_0 hv_1_0_1 arr_x2 hv_1_2_0
-g1_2_0_0 m4_1_1_0 w1_2_0 hv_1_1_0 c1_2_0 g2_2_0_1 g1_2_1_0 w1_2_1 q5_1_1 c1_2_1 oc_1_2 dup_1_2 dup_1_1 dup_1_0 oc_1_1 hk_2_0 g2_2_0_0 v1_2_0 ms_2_0_1 me_2_0_1 ms_2_0_0 me_2_0_0 q5_1_2 g2_2_1_1 bt_2_0_1 g2_2_1_0 g1_2_2_0 w1_2_2 c1_2_2 g2_2_2_1 ms_2_1_1 bt_2_0_0 ms_2_1_0 w2_2_0 ab_2_0_0 bt_2_1_1 hk_2_1 me_2_1_1 g2_2_2_0 ab_2_1_1 ab_2_1_0 bt_2_1_0 c2_2_0_1 c2_2_0_0 g3_2_0_1 w2_2_1 c2_2_1_1 c2_2_1_0 g3_2_0_0 g3_2_1_0 ms_2_2_0 ms_2_2_1 me_2_2_0 me_2_2_1 w3_2_0 bt_2_2_0 bt_2_2_1 hk_2_2 ab_2_2_0 ab_2_2_1 p1_2_0 p2_2_0 w2_2_2 p3_2_0 c2_2_2_0 g4_2_0_1 v1_2_2 v1_2_1 w3_2_1 m4_2_0_1 q5_2_0 g3_2_2_0 p1_2_1 g4_2_0_0 hv_2_0_1 m4_2_0_0 w3_2_2 p2_2_1 p3_2_1 q5_2_1 hv_2_0_0 p1_2_2 g4_2_1_1 g4_2_1_0 hz_2_0_1 m4_2_1_0 p2_2_2 q5_2_2 p3_2_2 hv_2_1_0 hz_2_0_0 syq_1 syq_0 o_t hz_2_1_0 g4_2_2_0 hv_2_1_1 hz_2_1_1 syq_2 m4_2_2_0 o_p g4_2_2_1 hv_2_2_1 hv_2_2_0 syp syq_3 hz_2_2_0 hz_2_2_1 syq_4 syq_5
+4 0 3 11 6 9 2 1 5 23 22 10 49 12 15 55 52 54 8 51 7 20 21 29 13 14 16 40 17 58 43 30 18 19 61 37 31 26 38 62 27 63 28 50 32 64 65 67 44 36 34 42 41 35 48 33 45 39 68 59 107 60 24 90 47 46 66 71 72 73 74 79 25 75 78 92 76 88 87 80 83 77 93 81 105 91 101 89 69 97 95 84 96 104 109 85 121 98 94 106 99 82 113 100 110 53 112 108 123 125 120 111 102 114 103 135 86 127 122 145 144 136 115 146 137 117 116 147 148 126 162 128 167 163 129 164 118 131 165 166 124 168 119 130 132 169 138 133 149 139 151 150 140 152 172 134 154 153 141 155 142 158 156 160 143 159 70 161 173 175 179 200 174 176 56 171 177 157 180 183 182 181 170 188 187 184 185 178 189 196 197 281 192 186 190 201 198 205 199 204 217 214 203 206 202 210 207 218 209 213 193 208 220 215 222 216 194 230 221 211 229 223 212 254 255 245 233 256 219 246 257 258 224 247 231 259 237 272 225 232 236 191 273 238 195 235 274 275 226 234 239 227 241 57 277 280 228 240 242 276 282 260 248 243 283 261 249 262 250 244 295 268 286 263 264 278 251 265 252 266 269 253 289 270 279 271 294 287 285 284 292 288 296 267 316 290 297 331 293 299 300 379 298 291 309 304 301 302 314 308 305 313 317 303 310 306 320 328 315 329 333 319 332 311 307 334 318 348 330 321 338 337 322 323 351 347 324 339 335 349 336 325 340 341 326 354 342 350 327 353 343 355 352 344 361 345 362 356 363 357 385 384 312 378 386 346 387 375 380 364 358 370 376 365 359 381 366 371 394 388 377 389 390 360 382 367 383 395 368 372 396 391 369 373 398 402 374 397 392 399 403 393 400 404 401 405
 """
-CFG = {_a.split("=")[0]: (1 if _a.split("=")[1] == "1" else _a.split("=")[1]) for _a in CFGS.split()}
-ORDER = ORDERS.split()
+CFG = dict(_a.split("=") for _a in CFGS.split())
+ORDER = [int(_a) for _a in ORDERS.split()]
 
 
 def build(g, T, topo, core, cfg):
@@ -61,6 +55,7 @@ def build(g, T, topo, core, cfg):
     ops = []
     vec, act, pe = g.vector, g.scalar, g.tensor
     eng = cfg.get
+    b0, b1 = s * B, s * B + B
 
     def op(name, q, fn, rd, wr, cost):
         ops.append((name, q, fn, rd, wr, cost))
@@ -72,7 +67,10 @@ def build(g, T, topo, core, cfg):
         return (n, 0, w)
 
     def dma(name, q, out, in_, rd, wr, nbytes):
+        q = eng("Q" + name, q)
         e = g.sync if q == "S" else g.scalar
+        if "W" + name in cfg:
+            rd = rd + [("tok_" + cfg["W" + name], 0, 1)]
         op(name, q, lambda: e.dma_start(out(), in_()), rd, wr, ("dma", nbytes))
 
     def ts(name, out, in0, s1, s2, o0, o1, rd, wr, n):
@@ -90,11 +88,17 @@ def build(g, T, topo, core, cfg):
     def ms(name, buf, lo, hi, val, n):
         op(name, "V", lambda: vec.memset(T[buf][:, lo:hi], val), [], [(buf, lo, hi)], ("v", n))
 
+    def ac(name, out, in_, f, rd, wr, n, bias=0.0, scale=1.0):
+        op(name, "A", lambda: act.activation(out(), in_(), f, bias=bias() if bias else 0.0, scale=scale), rd, wr, ("a", n))
+
     def W(n):
         return lambda: T[n][:]
 
     def C(n, lo, hi):
         return lambda: T[n][:, lo:hi]
+
+    def D(n, j, lo, hi):
+        return lambda: T[n][:, j, lo:hi]
 
     def K(v):
         return lambda: v
@@ -102,29 +106,40 @@ def build(g, T, topo, core, cfg):
     def tsw(name, out, in0, s1, s2, o0, o1):
         ts(name, W(out), W(in0), K(s1), K(s2), o0, o1, [whole(in0)], [whole(out)], whole(out)[2])
 
-    def ttw(name, out, in0, in1, o):
-        tt(name, W(out), W(in0), W(in1), o, [whole(in0), whole(in1)], [whole(out)], 2 * whole(out)[2])
+    def own(lo, hi):
+        return [(a, b, a + (b0 if a < B else M - B)) for a, b in ((lo, min(hi, B)), (max(lo, B), hi)) if a < b]
 
-    def send(tag, src, dst, rd, wr):
+    def ownr(x, lo, hi):
+        return [(x, w, w + b - a) for a, b, w in own(lo, hi)]
+
+    def send(tags, aps, rd, wr, nbytes):
         def fn():
-            m = topo.mask(core, peers[0])
-            for c in peers:
-                m &= topo.mask(core, c)
+            es = [e for e in topo.engines(core, peers[0]) if all(e in topo.engines(core, c) for c in peers)]
+            es = es[:int(eng("E" + tags[0], len(es)))]
+            n = len(es) // len(tags)
             ids = [DstId(rid=topo.addr(c)[0], pnc=topo.addr(c)[1]) for c in peers]
-            g.remote_dma_fused([RemoteDMATransfer(dst_ids=ids, dma_engine_mask=m, remote_sem=T.sem["arr_" + tag],
-                                                  src=src(), dsts=[dst() for c in peers])], local_sem=T.sem["out_" + tag])
-            return bin(m).count("1")
-        op("snd_" + tag, "G", fn, rd, [("tok_" + tag, 0, 1)], ("send", 1))
-        op("arr_" + tag, "R", None, [("tok_" + tag, 0, 1)], wr, ("arr", 1))
+            g.remote_dma_fused([RemoteDMATransfer(dst_ids=ids, dma_engine_mask=sum(1 << e for e in es[k * n:(k + 1) * n]),
+                                                  remote_sem=T.sem["arr_" + t], src=aps[k](), dsts=[aps[k]() for c in peers])
+                                for k, t in enumerate(tags)], local_sem=T.sem["out_" + tags[0]])
+            return (n * len(tags), n)
+        op("snd_" + tags[0], "G", fn, rd, [("tok_" + t, 0, 1) for t in tags], ("send", nbytes))
+        for k, t in enumerate(tags):
+            op("arr_" + t, "R", "snd_" + tags[0], [("tok_" + t, 0, 1)], wr[k], ("arr", 1))
 
     def others(buf, w):
         return [(buf, k * w, (k + 1) * w) for k in range(len(T.cores)) if k != s]
 
-    b0, b1 = s * B, s * B + B
+    def mm(name, bank, n, terms, rd, cyc):
+        def fn():
+            for k, (l, r_) in enumerate(terms):
+                ins = pe.matmul(T[bank][:, 0:n], T[l][:], r_(), k == 0, k == len(terms) - 1)
+            return ins
+        op(name, "P", fn, rd + [whole(l) for l, r_ in terms], [whole(bank)], ("p", cyc))
+
     ms("m_pb", "pb", 0, 128, 0, 128)
     dma("lpb0", "S", lambda: T.pb[0:128:16, :], lambda: T.par[:, 0:8], [], [("pb", 0, 128)], 4096)
     dma("lpb1", "A", lambda: T.pb[1:128:16, :], lambda: T.par[:, 0:8], [], [("pb1", 0, 128)], 4096)
-    dma("lpar", "S", W("pin"), lambda: T.par[:], [], [whole("pin")], 98304)
+    dma("lpar", "S", W("p0"), lambda: T.par[:], [], [whole("p0")], 98304)
     dma("lqb", "A", C("x0", b0, b1), lambda: T.q[:, 0:B], [], [("x0", b0, b1)], 32768)
     dma("lam", "A", W("am"), lambda: T.amat[:], [], [whole("am")], 32768)
     dma("lth", "A", C("thi", 0, 1), lambda: T.th[:], [], [whole("thi")], 512)
@@ -132,35 +147,33 @@ def build(g, T, topo, core, cfg):
     op("g_blk", "G", lambda: g.iota(T.blk[:], [[-16, 8]], 0, 1), [], [whole("blk")], ("g", 8))
     op("g_eye", "G", lambda: g.iota(T.ieye[:], [[1, 128]], 0, -1, allow_small_or_imprecise_dtypes=True), [], [whole("ieye")], ("g", 128))
     op("g_ki", "G", lambda: g.iota(T.ki[:, 0:1], [[1, 1]], 0, 1), [], [whole("ki")], ("g", 1))
-    op("g_vd", "G", lambda: g.iota(T.vd0[:], [[16, 192]], DUP, 0), [], [whole("vd0")], ("g", 192))
+    op("g_vb", "G", lambda: g.iota(T.vd0[:, 0:8], [[16, 8]], 4096 + b0, 0), [], [("vd0", 0, 8)], ("g", 8))
+    op("g_vd", "G", lambda: g.iota(T.vd0[:, 8:192], [[16, 184]], 4096 + M, 0), [], [("vd0", 8, 192)], ("g", 184))
     tsw("c_i16", "i16b", "i16", 15, None, A.bitwise_and, None)
     tsw("c_msk", "msk", "i16b", 0.0, None, A.is_equal, None)
-    ms("m_tab", "tab", OWN, DUP, 0.0, 1536)
+    ms("m_tab", "tab", M, NW, 0.0, (NW - M) // 2)
     pbr = [whole("pb"), ("pb1", 0, 128)]
     ts("b_t", W("pbt"), W("pb"), C("msk", 1, 2), None, A.mult, None, pbr + [whole("msk")], [whole("pbt")], 128)
     tt("b_d", C("tab", b0, b1), W("pb"), W("pbt"), A.subtract, pbr + [whole("pbt")], [("tab", b0, b1)], 256)
-    send("t0", C("tab", b0, b1), C("tab", b0, b1), [("tab", b0, b1), ("tabr0", 0, 1), ("tabr1", 0, 1)], others("tab", B))
-    send("x0", C("x0", b0, b1), C("x0", b0, b1), [("x0", b0, b1)], others("x0", B))
-    for c in range(NC):
-        dma("lq%d" % c, "S", C("x0", OWN + c * CH, OWN + (c + 1) * CH), lambda c=c: T.q[:, c * CH:(c + 1) * CH],
-            [("tok_" + cfg["lq%d" % c], 0, 1)] if "lq%d" % c in cfg else [], [("x0", OWN + c * CH, OWN + (c + 1) * CH)], 262144)
-    dma("lclr", "S", W("clrs"), lambda: T.clr[:], [("tok_t0", 0, 1)], [whole("clrs")], 524288)
-    dma("ldup", "S", C("x0", DUP, DUP + V), lambda: T.q[:], [("tok_t0", 0, 1)], [("x0", DUP, DUP + V)], 786432)
-    tsw("i_t", "ta", "pin", float(OWN), float(B), A.is_ge, A.mult)
-    ttw("i_p", "p0", "pin", "ta", A.add)
-    cp("i_d0", W("d0"), W("p0"), [whole("p0")], [whole("d0")], 192)
-    ttw("i_d1", "d1", "p0", "d0", A.subtract)
-    dma("ltab0", "S", lambda: T.tab[0:128:16, OWN:DUP], W("d0"), [whole("d0"), ("tab", OWN, DUP)], [("tabr0", 1, 2)], 49152)
-    dma("ltab1", "A", lambda: T.tab[1:128:16, OWN:DUP], W("d1"), [whole("d1"), ("tab", OWN, DUP)], [("tabr1", 1, 2)], 49152)
-    tsw("i_hi", "tb", "p0", 4, None, A.arith_shift_right, None)
-    tsw("i_lo", "tc", "p0", 15, None, A.bitwise_and, None)
+    trd = [("tab", b0, b1), ("tabr0", 0, 1), ("tabr1", 0, 1)]
+    if eng("one", "1") == "1":
+        send(["t0", "x0"], [C("tab", b0, b1), C("x0", b0, b1)], trd + [("x0", b0, b1)], [others("tab", B), others("x0", B)], 65536)
+    else:
+        send(["t0"], [C("tab", b0, b1)], trd, [others("tab", B)], 32768)
+        send(["x0"], [C("x0", b0, b1)], [("x0", b0, b1)], [others("x0", B)], 32768)
+    for c in range(3):
+        lo, hi = max(B, c * 1024), (c + 1) * 1024
+        dma("lq%d" % c, "S", C("x0", lo + M - B, hi + M - B), lambda lo=lo, hi=hi: T.q[:, lo:hi], [], ownr("x0", lo, hi), 256 * (hi - lo))
+    dma("lclr", "S", W("clrs"), lambda: T.clr[:], [], [whole("clrs")], 524288)
+    for j, bitmask in enumerate((0xFF0, 15)):
+        ts("i_q%d" % j, D("hl", j, 0, 192), W("p0"), K(bitmask), None, A.bitwise_and, None, [whole("p0")], [("hl", 192 * j, 192 * j + 192)], 192)
+        cp("i_d%d" % j, D("di", j, 0, 192), D("hl", j, 0, 192), [("hl", 192 * j, 192 * j + 192)], [("di", 192 * j, 192 * j + 192)], 192)
+        dma("ltab%d" % j, "SA"[j], lambda j=j: T.tab[j:128:16, M:NW], D("di", j, 8, 192), [("di", 192 * j, 192 * j + 192), ("tab", M, NW)],
+            [("tabr%d" % j, 1, 2)], 47104)
     tsw("i_s", "td", "p0", 7, None, A.arith_shift_right, None)
     tsw("i_s2", "te", "td", 8.0, 120.0, A.min, A.mult)
-    tsw("i_f", "tf", "ta", 184.0 / 128.0, 8.0, A.mult, A.add)
-    ttw("i_u", "tg", "tc", "tf", A.mult)
-    ttw("i_w", "th2", "tb", "te", A.add)
-    ttw("i_z", "ti", "tg", "th2", A.add)
-    cp("i_idx", W("idx0"), W("ti"), [whole("ti")], [whole("idx0")], 192)
+    ts("i_f", W("tf"), D("di", 0, 0, 192), K(float(M)), K(16.0), A.is_ge, A.mult, [("di", 0, 192)], [whole("tf")], 96)
+    tt("i_u", W("tg"), W("tf"), D("di", 1, 0, 192), A.min, [whole("tf"), ("di", 192, 384)], [whole("tg")], 384)
     for z in ("z1", "z2", "z3"):
         ms("m_" + z, z, 0, 144, 0.0, 72)
     ms("m_c32", "c32", 0, 64, 32.0, 32)
@@ -168,31 +181,40 @@ def build(g, T, topo, core, cfg):
     tsw("c_blk", "blks", "blk", 4, None, A.arith_shift_right, None)
     op("c_w1", "V", lambda: vec.tensor_reduce(T.w1[:, 0:1], T.msk[:, 0:2], X, A.add), [whole("msk")], [whole("w1")], ("v", 2))
     op("c_pw", "V", lambda: vec.tensor_tensor_scan(T.pw[:], T.two[:], T.two[:], 2.0, A.mult, A.max), [whole("two")], [whole("pw")], ("v", 16))
-    ttw("c_pwm", "pwm", "pw", "msk", A.mult)
+    tt("c_pwm", W("pwm"), W("pw"), W("msk"), A.mult, [whole("pw"), whole("msk")], [whole("pwm")], 32)
     op("c_w2", "V", lambda: vec.tensor_reduce(T.w2[:, 0:1], T.pwm[:, 0:11], X, A.add), [whole("pwm")], [whole("w2")], ("v", 11))
     for z, wt, rd in (("z1", C("w1", 0, 1), [whole("w1")]), ("z2", C("w2", 0, 1), [whole("w2")]), ("z3", K(-BIG), [])):
         ts("c_" + z, lambda z=z: T[z][:, 15:143:16], W("blks"), K(0.0), wt, A.is_equal, A.mult, [whole("blks")] + rd, [whole(z)], 8)
     tsw("c_eye", "eye", "ieye", 0.0, None, A.is_equal, None)
     tsw("c_eyef", "eyef", "ieye", 0.0, None, A.is_equal, None)
-    for n, src, sc in (("eyen", "eye", -1.0), ("eyes", "eye", 1.0 / 16), ("eyeb", "eye", 256.0), ("am2", "am", 2.0)):
-        op("c_" + n, "A", lambda n=n, src=src, sc=sc: act.activation(T[n][:], T[src][:], AF.Identity, scale=sc),
-           [whole(src)], [whole(n)], ("a", 128))
+    for n, src, sc in (("eyen", "eye", -1.0), ("eyes", "eye", 1.0 / 16), ("eyeb", "eye", float(TW)), ("eye8", "eye", 8.0), ("eyeu", "eye", 176.0),
+                       ("eyeh", "eye", 0.5), ("eyeg", "eye", 255.0 / 512), ("am2", "am", 2.0)):
+        ac("c_" + n, W(n), W(src), AF.Identity, [whole(src)], [whole(n)], 128, scale=sc)
+    mm("i_m", "pa", 192, [("eyes", D("di", 0, 0, 192)), ("eye8", D("di", 1, 0, 192)), ("eye", W("te")), ("eyeu", W("tg"))],
+       [whole("di"), whole("te"), whole("tg")], 768)
+    cp("i_idx", W("idx0"), C("pa", 0, 192), [whole("pa")], [whole("idx0")], 192)
     ts("c_kj", C("kj", 0, 1), C("ki", 0, 1), K(15), None, A.bitwise_and, None, [whole("ki")], [whole("kj")], 1)
     cp("c_kf", C("kf", 0, 1), C("kj", 0, 1), [whole("kj")], [whole("kf")], 1)
     ts("c_vd", W("vd"), W("vd0"), C("kf", 0, 1), None, A.add, None, [whole("vd0"), whole("kf")], [whole("vd")], 192)
+    for r in (1, 2):
+        tsw("c_vd%d" % r, "vd%d" % r, "vd", FLAG[r] - FLAG[0], None, A.add, None)
     cp("c_thr0", C("thr0", 0, 1), C("thi", 0, 1), [whole("thi")], [whole("thr0")], 1)
     ts("c_nb0", C("nb0", 0, 1), C("thi", 0, 1), K(-1.0), K(-0.5), A.mult, A.add, [whole("thi")], [whole("nb0")], 1)
-    op("c_cs", "P", lambda: pe.matmul(T.pc[:, 0:1], T.am[:], T.c32[:, 0:1], True, True), [whole("am"), whole("c32")], [whole("pc")], ("p", 64))
+    mm("c_cs", "pc", 1, [("am", C("c32", 0, 1))], [whole("c32")], 64)
     ts("c_thr1", C("thr1", 0, 1), C("pc", 0, 1), K(8.0), C("thr0", 0, 1), A.mult, A.add, [whole("pc"), whole("thr0")], [whole("thr1")], 1)
     ts("c_nb1", C("nb1", 0, 1), C("thr1", 0, 1), K(-1.0), K(-0.5), A.mult, A.add, [whole("thr1")], [whole("nb1")], 1)
 
-    def wrap(name, bank, z, data, c, first):
+    def wrap(name, bank, z, data, lo, hi, names):
+        n = (hi - lo) // 16
+
         def fn():
             for i in range(16):
-                ins = pe.matmul(T[bank][:, 0:WC], T[z][:, 15 - i:143 - i], T[data][:, c * CH + i:(c + 1) * CH:16],
-                                first and i == 0, i == 15)
+                ins = pe.matmul(T[bank][:, 0:n], T[z][:, 15 - i:143 - i], T[data][:, lo + i:hi:16], i == 0 and not names, i == 15)
             return ins
-        op(name, "P", fn, [whole(z), (data, c * CH, (c + 1) * CH)], [whole(bank)], ("p", 64 * 16))
+        if names:
+            op("v1" + name[2:], "P", lambda: pe.matmul(T[bank][:, 0:n], T.eyef[:], T.hk[:, lo // 16:hi // 16], True, False),
+               [whole("eyef"), ("hk", lo // 16, hi // 16)], [whole(bank)], ("p", 4 * max(64, n)))
+        op(name, "P", fn, [whole(z), (data, lo, hi)], [whole(bank)], ("p", max(64, n) * 16))
 
     def gather(name, e, out, lo, hi, win, whi, off, rd):
         a, b = lo // 16, hi // 16
@@ -203,167 +225,226 @@ def build(g, T, topo, core, cfg):
             op(name, "V", lambda: vec.tensor_copy(T[out][:, lo:hi], T[win][:, 0:whi].indirect(T[off][:, a:b])),
                rd + [(off, a, b)], [(out, lo, hi)], ("gv", hi - lo))
 
-    def gtt(name, out, lo, hi, win, whi, off, in1, l1, o):
-        a, b = lo // 16, hi // 16
-        op(name, "V", lambda: vec.tensor_tensor(T[out][:, lo:hi], T[win][:, 0:whi].indirect(T[off][:, a:b]), T[in1][:, l1:l1 + hi - lo], o),
-           [(win, 0, whi), (off, a, b), (in1, l1, l1 + hi - lo)], [(out, lo, hi)], ("gt", hi - lo))
+    def gtt(name, out, win, whi, off, in1, lo, hi, w, o):
+        op(name, "V", lambda: vec.tensor_tensor(T[out][:, lo:hi], T[win][:, 0:whi].indirect(T[off][:, lo // 16:hi // 16]), T[in1][:, w:w + hi - lo], o),
+           [(win, 0, whi), (off, lo // 16, hi // 16), (in1, w, w + hi - lo)], [(out, lo, hi)], ("gt", hi - lo))
 
-    def banks(b, lo, hi):
-        return (b, lo % CH // HF * HF, ((hi - 1) % CH // HF + 1) * HF)
+    def two(name, bank, o0, l0, l1, data, lo, hi, x):
+        if lo >= B and hi - lo <= HF and eng("e" + name, "0") == "1":
+            w0 = lo + M - B
+            op("e" + name, "P", lambda: pe.matmul(T[bank][:, o0:o0 + hi - lo], T[l1][:], T[x][:, w0:w0 + hi - lo], True, False),
+               [whole(l1)] + ownr(x, lo, hi), [banks(bank, o0, hi - lo)], ("p", hi - lo))
+            op(name, "P", lambda: pe.matmul(T[bank][:, o0:o0 + hi - lo], T[l0][:], T[data][:, lo:hi], False, True),
+               [whole(l0), (data, lo, hi)], [banks(bank, o0, hi - lo)], ("p", hi - lo))
+            return
 
-    def two(name, bank, l0, l1, data, lo, hi, x):
         def fn():
-            for a, b in ((lo, min(hi, lo // HF * HF + HF)), (lo // HF * HF + HF, hi)):
-                if a < b:
-                    o = T[bank][:, a % CH:a % CH + b - a]
-                    pe.matmul(o, T[l1][:], T[x][:, OWN + a:OWN + b], True, False)
-                    ins = pe.matmul(o, T[l0][:], T[data][:, a:b], False, True)
+            for a, b, w in own(lo, hi):
+                while a < b:
+                    o = o0 + a - lo
+                    n = min(b - a, HF - o % HF)
+                    pe.matmul(T[bank][:, o:o + n], T[l1][:], T[x][:, w:w + n], True, False)
+                    ins = pe.matmul(T[bank][:, o:o + n], T[l0][:], T[data][:, a:a + n], False, True)
+                    a, w = a + n, w + n
             return ins
-        op(name, "P", fn, [whole(l0), whole(l1), (data, lo, hi), (x, OWN + lo, OWN + hi)], [banks(bank, lo, hi)], ("p", 2 * (hi - lo)))
+        op(name, "P", fn, [whole(l0), whole(l1), (data, lo, hi)] + ownr(x, lo, hi), [banks(bank, o0, hi - lo)], ("p", 2 * (hi - lo)))
 
-    def cuts(tag, r, c):
-        lo = c * CH
-        return [(lo, lo + CH)] if cfg.get("%s_%d_%d" % (tag, r, c), 2) == 1 else [(lo, lo + HF), (lo + HF, lo + CH)]
+    def banks(b, o, n):
+        return (b, o // HF * HF, ((o + n - 1) // HF + 1) * HF)
 
-    def cuts4(r, c):
-        cs = cuts("n4", r, c)
-        return [(0, B), (B, cs[0][1])] + cs[1:] if c == 0 and r < RO - 1 else cs
+    def chunks(tag, r):
+        e = [0] + [256 * int(a) for a in eng("%s%d" % (tag, r), "4,8").split(",") if a] + [V]
+        return list(zip(e[:-1], e[1:]))
 
-    def hull(r, chunks):
-        cs = [a for c in chunks for k, a in enumerate(cuts4(r, c)) if eng("g4_%d_%d_%d" % (r, c, k), "V") == "V"]
-        return (cs[0][0], cs[-1][1]) if cs else None
+    def cuts(tag, lo, hi, fl=None, form=None):
+        ps = [(a, min(hi, a + HF)) for a in range(lo, hi, HF)]
+        if eng(tag, "2") != "1":
+            return ps
+        if fl is None:
+            return [(lo, hi)]
+        out = []
+        for k, (a, b) in enumerate(ps):
+            if out and (k + fl) % 2 and (not form or form[k] == form[k - 1]):
+                out[-1] = (out[-1][0], b)
+            else:
+                out.append((a, b))
+        return out
 
-    h0 = hull(0, range(NC))
-    if h0:
-        dma("loc", "S", C("oc", h0[0], h0[1]), lambda: T.q[:, h0[0]:h0[1]], [("tok_t0", 0, 1)], [("oc", h0[0], h0[1])], 256 * (h0[1] - h0[0]))
+    def place(lo, c0, fl):
+        return ((lo - c0) // HF + fl) % 2 * HF + (lo - c0) % HF
+
+    def cuts4(r, c, c0, c1):
+        cs = cuts("n4_%d_%d" % (r, c), c0, c1, int(eng("fm_%d_%d" % (r, c), "0")))
+        return [(0, B), (B, cs[0][1])] + cs[1:] if c == 0 else cs
+
+    def copied(r, lo, hi):
+        cs = [(max(a, lo), min(b, hi)) for c, (c0, c1) in enumerate(chunks("cb", r))
+              for t, d, ps in (("g4", "V", cuts4(r, c, c0, c1)), ("g2", "A", cuts("n2_%d_%d" % (r, c), c0, c1)))
+              for k, (a, b) in enumerate(ps) if eng("%s_%d_%d_%d" % (t, r, c, k), d) == "V" and a < hi and lo < b]
+        return (min(cs)[0], max(b for a, b in cs)) if cs else None
+
+    for c in range(3):
+        h = copied(0, c * 1024, c * 1024 + 1024)
+        if h:
+            dma("ldup%d" % c, "S", C("x0", NW + h[0], NW + h[1]), lambda h=h: T.q[:, h[0]:h[1]], [], [("x0", NW + h[0], NW + h[1])], 256 * (h[1] - h[0]))
     tabrd = [whole("tab"), ("tabr0", 0, 2), ("tabr1", 0, 2)]
     for r in range(RO):
         x, xn = "x%d" % r, "x%d" % (r + 1)
         idx, hoff, coff, sel = "idx%d" % r, "hoff%d" % r, "coff%d" % r, "sel%d" % r
-        p, pn, pp, sf = "p%d" % r, "p%d" % (r + 1), "pp%d" % r, "sf%d" % r
+        p, pn, pp, sf, sg = ("p0", "pp0", "pp1")[r], "p3", "pp%d" % r, "sf%d" % r, "sg%d" % r
         thr, nb = ("thr0", "nb0") if r == 0 else ("thr1", "nb1")
-        last = r == RO - 1
-        for c in range(NC):
-            for k, (lo, hi) in enumerate(cuts("n1", r, c)):
-                t = "g1_%d_%d_%d" % (r, c, k)
-                gather(t, eng(t, "A"), "hg", lo, hi, "tab", 4096, idx, tabrd)
-            ph = "ph%d" % c
-            wrap("w1_%d_%d" % (r, c), ph, "z1", "hg", c, True)
-            cp("c1_%d_%d" % (r, c), C(hoff, c * WC, (c + 1) * WC), C(ph, 0, WC), [whole(ph)], [(hoff, c * WC, (c + 1) * WC)], WC)
-            hk = ("hk", c * WC, (c + 1) * WC)
-            op("hk_%d_%d" % (r, c), "A", lambda ph=ph, hk=hk: act.activation(T.hk[:, hk[1]:hk[2]], T[ph][:, 0:WC], AF.Identity, bias=BIG / 2),
-               [whole(ph)], [hk], ("a", WC))
-            op("v1_%d_%d" % (r, c), "P", lambda ph=ph, hk=hk: pe.matmul(T[ph][:, 0:WC], T.eyef[:], T.hk[:, hk[1]:hk[2]], True, False),
-               [hk, whole("eyef")], [whole(ph)], ("p", 4 * WC))
-        for c in range(NC):
-            ph = "ph%d" % c
-            form = []
-            for k, (lo, hi) in enumerate(cuts("n2", r, c)):
-                t = "g2_%d_%d_%d" % (r, c, k)
-                form += ["V" if eng(t, "A") == "V" else "A"] * ((hi - lo) // HF)
-                if eng(t, "A") != "V":
-                    gather(t, eng(t, "A"), "de", lo, hi, x, DUP, hoff, [(x, 0, DUP)])
-                else:
-                    gtt(t, "de", lo, hi, x, DUP, hoff, x, DUP + lo, A.subtract)
-            for k in range(2):
-                lo = c * CH + k * HF
-                two("ms_%d_%d_%d" % (r, c, k), "ps", "am", "am" if form[k] == "A" else "am2", "de", lo, lo + HF, x)
-                if form[k] == "A":
-                    two("me_%d_%d_%d" % (r, c, k), "pq", "eye", "eyen", "de", lo, lo + HF, x)
-            for k, (lo, hi) in enumerate(cuts("na" if form[0] == form[1] else "halves", r, c)):
-                src, a, b = ("pq", lo % CH, lo % CH + hi - lo) if form[k] == "A" else ("de", lo, hi)
-                op("ab_%d_%d_%d" % (r, c, k), "A", lambda src=src, a=a, b=b, lo=lo, hi=hi: act.activation(T.ab[:, lo:hi], T[src][:, a:b], AF.Abs),
-                   [(src, a, b)], [("ab", lo, hi)], ("a", hi - lo))
-            be = []
-            for k, (lo, hi) in enumerate(cuts("nb", r, c)):
-                t = "bt_%d_%d_%d" % (r, c, k)
-                a, b = lo % CH, lo % CH + hi - lo
-                be += [eng(t, "A")] * ((hi - lo) // HF)
-                if eng(t, "A") == "A":
-                    op(t, "A", lambda a=a, b=b, lo=lo, hi=hi, nb=nb: act.activation(T.bits[:, lo:hi], T.ps[:, a:b], AF.Sign, bias=T[nb][:, 0:1]),
-                       [("ps", a, b), whole(nb)], [("bits", lo, hi)], ("a", hi - lo))
-                else:
-                    ts(t, C("bits", lo, hi), C("ps", a, b), C(thr, 0, 1), K(2.0), A.is_gt, A.mult, [("ps", a, b), whole(thr)], [("bits", lo, hi)], hi - lo)
+        last, vd = r == RO - 1, ("vd", "vd1", "vd2")[r]
+        for c, (c0, c1) in enumerate(chunks("ca", r)):
             t = "%d_%d" % (r, c)
-            m0, m1 = c * WC, (c + 1) * WC
-            wrap("w2_" + t, "pc", "z2", "bits", c, True)
-            spans = [(0, WC, be[0])] if be[0] == be[1] else [(0, WC // 2, be[0]), (WC // 2, WC, be[1])]
+            for k, (lo, hi) in enumerate(cuts("n1_" + t, c0, c1)):
+                gather("g1_%s_%d" % (t, k), eng("g1_%s_%d" % (t, k), "A"), "hg", lo, hi, "tab", NW, idx, tabrd)
+            ph, m0, m1 = ("pz", "pa")[c % 2], c0 // 16, c1 // 16
+            wrap("w1_" + t, ph, "z1", "hg", c0, c1, False)
+            cp("c1_" + t, C(hoff, m0, m1), C(ph, 0, m1 - m0), [whole(ph)], [(hoff, m0, m1)], m1 - m0)
+            if eng("hk_" + t, "A") == "A":
+                ac("hk_" + t, C("hk", m0, m1), C(ph, 0, m1 - m0), AF.Identity, [whole(ph)], [("hk", m0, m1)], m1 - m0, bias=K(FLAG[r]))
+            else:
+                ts("hk_" + t, C("hk", m0, m1), C(hoff, m0, m1), K(FLAG[r]), None, A.add, None, [(hoff, m0, m1)], [("hk", m0, m1)], m1 - m0)
+        cb = chunks("cb", r)
+        for c, (c0, c1) in enumerate(cb):
+            t = "%d_%d" % (r, c)
+            m0, m1 = c0 // 16, c1 // 16
+            n = m1 - m0
+            fl = int(eng("fl_" + t, "0"))
+            form = []
+            for k, (lo, hi) in enumerate(cuts("n2_" + t, c0, c1)):
+                e = eng("g2_%s_%d" % (t, k), "A")
+                form += ["V" if e == "V" else "A"] * ((hi - lo + HF - 1) // HF)
+                if e != "V":
+                    gather("g2_%s_%d" % (t, k), e, "de", lo, hi, x, NW, hoff, [(x, 0, NW)])
+                else:
+                    gtt("g2_%s_%d" % (t, k), "de", x, NW, hoff, x, lo, hi, NW + lo, A.subtract)
+            abs_, bts = cuts("na_" + t, c0, c1, fl, form), cuts("nb_" + t, c0, c1, fl)
+            spans = []
+            for p0_ in range(c0 - fl * HF, c1, 2 * HF):
+                for k, (lo, hi) in enumerate(cuts("pieces", c0, c1)):
+                    if p0_ <= lo < p0_ + 2 * HF:
+                        two("ms_%s_%d" % (t, k), "ps", place(lo, c0, fl), "am", "am" if form[k] == "A" else "am2", "de", lo, hi, x)
+                        if form[k] == "A":
+                            two("me_%s_%d" % (t, k), "pq", place(lo, c0, fl), "eye", "eyen", "de", lo, hi, x)
+                for k, (lo, hi) in enumerate(abs_):
+                    if p0_ <= lo < p0_ + 2 * HF:
+                        a = place(lo, c0, fl)
+                        if form[(lo - c0) // HF] == "A":
+                            ac("ab_%s_%d" % (t, k), C("ab", lo, hi), C("pq", a, a + hi - lo), AF.Abs, [banks("pq", a, hi - lo)], [("ab", lo, hi)], hi - lo)
+                        else:
+                            ac("ab_%s_%d" % (t, k), C("ab", lo, hi), C("de", lo, hi), AF.Abs, [("de", lo, hi)], [("ab", lo, hi)], hi - lo)
+                for k, (lo, hi) in enumerate(bts):
+                    if p0_ <= lo < p0_ + 2 * HF:
+                        nm, a = "bt_%s_%d" % (t, k), place(lo, c0, fl)
+                        e, rd = eng(nm, "A"), banks("ps", a, hi - lo)
+                        if spans and spans[-1][2] == e:
+                            spans[-1][1] = hi // 16
+                        else:
+                            spans.append([lo // 16, hi // 16, e])
+                        if e == "A":
+                            ac(nm, C("bits", lo, hi), C("ps", a, a + hi - lo), AF.Sign, [rd, whole(nb)], [("bits", lo, hi)], hi - lo, bias=C(nb, 0, 1))
+                        else:
+                            ts(nm, C("bits", lo, hi), C("ps", a, a + hi - lo), C(thr, 0, 1), K(2.0), A.is_gt, A.mult, [rd, whole(thr)],
+                               [("bits", lo, hi)], hi - lo)
+            wrap("w2_" + t, "pc", "z2", "bits", c0, c1, False)
             for j, (a, b, e) in enumerate(spans):
-                ts("c2_%s_%d" % (t, j), C(coff, m0 + a, m0 + b), C("pc", a, b), K(0.125), K(1023.5 if e == "A" else 0.0), A.mult, A.add,
-                   [whole("pc")], [(coff, m0 + a, m0 + b)], b - a)
-            for k, (lo, hi) in enumerate(cuts("n3", r, c)):
-                gtt("g3_%s_%d" % (t, k), "vi", lo, hi, "clrs", 2048, coff, "ab", lo, A.is_lt)
-            wrap("w3_" + t, ph, "z3", "vi", c, False)
-            tt("p1_" + t, C(pp, m0, m1), C(ph, 0, WC), C(p, m0, m1), A.max, [whole(ph), (p, m0, m1)], [(pp, m0, m1)], WC)
-            tt("p2_" + t, C(sf, m0, m1), C(pp, m0, m1), C("vd", m0, m1), A.min, [(pp, m0, m1), ("vd", m0, m1)], [(sf, m0, m1)], 2 * WC)
-            cp("p3_" + t, C(sel, m0, m1), C(sf, m0, m1), [(sf, m0, m1)], [(sel, m0, m1)], WC)
-            ts("q5_" + t, C(pn, m0, m1), C(pp, m0, m1), K(4095), None, A.bitwise_and, None, [(pp, m0, m1)], [(pn, m0, m1)], WC)
-            if not last:
-                hl, dg, sg, idn = "hl%d" % r, "dg%d" % r, "sg%d" % r, "idx%d" % (r + 1)
-                for j, bitmask in enumerate((0xFF0, 15)):
-                    ts("q%d_%s" % (j + 1, t), lambda hl=hl, j=j, m0=m0, m1=m1: T[hl][:, j, m0:m1], C(pp, m0, m1), K(bitmask), None,
-                       A.bitwise_and, None, [(pp, m0, m1)], [(hl, 192 * j + m0, 192 * j + m1)], WC)
-                hr = [(hl, m0, m1), (hl, 192 + m0, 192 + m1)]
-                dw = [(dg, 64 + m0, 64 + m1), (dg, 320 + m0, 320 + m1)]
-                if c == 0:
-                    ow = [(sg, 16 * s, 16 * s + 16)]
-                    cp("q0_" + t, lambda sg=sg: T[sg][:, s, :, :], lambda hl=hl: T[hl][:, :, 0:8], hr, ow, 16)
-                    send("t%d" % (r + 1), lambda sg=sg: T[sg][:, s, :, :], lambda sg=sg: T[sg][:, s, :, :], ow, others(sg, 16))
-                    for j in range(2):
-                        op("u%d_%d" % (j, r), "A", lambda sg=sg, dg=dg, j=j: act.activation(T[dg][:, j, 0:64], T[sg][:, :, j, :], AF.Identity),
-                           [whole(sg)], [(dg, 256 * j, 256 * j + 64)], ("a", 64))
-                cp("q3_" + t, lambda dg=dg, m0=m0, m1=m1: T[dg][:, :, 64 + m0:64 + m1], lambda hl=hl, m0=m0, m1=m1: T[hl][:, :, m0:m1], hr, dw, 2 * WC)
+                ts("c2_%s_%d" % (t, j), C(coff, a, b), C("pc", a - m0, b - m0), K(0.125), K(1023.5 if e == "A" else 0.0), A.mult, A.add,
+                   [whole("pc")], [(coff, a, b)], b - a)
+            for k, (lo, hi) in enumerate(cuts("n3_" + t, c0, c1)):
+                gtt("g3_%s_%d" % (t, k), "vi", "clrs", 2048, coff, "ab", lo, hi, lo, A.is_lt)
+            wrap("w3_" + t, "pd", "z3", "vi", c0, c1, True)
+            tt("p1_" + t, C(pp, m0, m1), C("pd", 0, n), C(p, m0, m1), A.max, [whole("pd"), (p, m0, m1)], [(pp, m0, m1)], n)
+        for tag in ("cs", "cq", "cp"):
+            ends = [b // 16 for c, (a, b) in enumerate(cb) if b == V or eng("%s_%d_%d" % (tag, r, c), "1") == "1"]
+            for c, (m0, m1) in enumerate(zip([0] + ends[:-1], ends)):
+                t, n = "%d_%d" % (r, m1), m1 - m0
+                if tag == "cs":
+                    tt("p2_" + t, C(sf, m0, m1), C(pp, m0, m1), C(vd, m0, m1), A.min, [(pp, m0, m1), (vd, m0, m1)], [(sf, m0, m1)], 2 * n)
+                    ts("p4_" + t, C(sg, m0, m1), C(sf, m0, m1), K(4095), None, A.bitwise_and, None, [(sf, m0, m1)], [(sg, m0, m1)], n)
+                    cp("p3_" + t, C(sel, m0, m1), C(sg, m0, m1), [(sg, m0, m1)], [(sel, m0, m1)], n)
+                elif tag == "cp":
+                    if last:
+                        ts("q5_" + t, C(pn, m0, m1), C(pp, m0, m1), K(4095), None, A.bitwise_and, None, [(pp, m0, m1)], [(pn, m0, m1)], n)
+                        cp("o_" + t, C("po", m0, m1), C(pn, m0, m1), [(pn, m0, m1)], [("po", m0, m1)], n)
+                    else:
+                        ph, dg = ("pa", "pz")[c % 2], "dg%d" % r
+                        sb = "sb%d" % r
 
-                def perm(ph=ph, dg=dg, m0=m0, m1=m1):
-                    pe.matmul(T[ph][:, 0:WC], T.eyes[:], T[dg][:, 0, 64 + m0:64 + m1], True, False)
-                    return pe.matmul(T[ph][:, 0:WC], T.eyeb[:], T[dg][:, 1, 64 + m0:64 + m1], False, True)
-                op("pm_" + t, "P", perm, dw + [whole("eyes"), whole("eyeb")], [whole(ph)], ("p", 128))
-                cp("q4_" + t, C(idn, m0, m1), C(ph, 0, WC), [whole(ph)], [(idn, m0, m1)], WC)
+                        def perm(ph=ph, dg=dg, sb=sb, m0=m0, m1=m1):
+                            a = max(m0, 8)
+                            for j in range(2 if m0 == 0 else 0):
+                                pe.matmul(T[ph][:, 0:8], T[("eyes", "eyeb")[j]][:], T[sb][:, s, j, :], j == 0, j == 1)
+                            for j in range(2):
+                                ins = pe.matmul(T[ph][:, a - m0:m1 - m0], T[("eyes", "eyeb")[j]][:], T[dg][:, j, 56 + a:56 + m1], j == 0, j == 1)
+                            return ins
+                        op("pm_" + t, "P", perm, [(dg + "o", m0, m1), whole("eyes"), whole("eyeb")] + ([(sb, 16 * s, 16 * s + 16)] if m0 == 0 else []),
+                           [whole(ph)], ("p", 2 * max(64, n) + (128 if m0 == 0 else 0)))
+                        cp("q4_" + t, C("idx%d" % (r + 1), m0, m1), C(ph, 0, n), [whole(ph)], [("idx%d" % (r + 1), m0, m1)], n)
+                elif not last:
+                    dg, sb = "dg%d" % r, "sb%d" % r
+                    for j, bitmask in enumerate((0xFF0, 15)):
+                        ts("q%d_%s" % (j + 1, t), D("hl", j, m0, m1), C(pp, m0, m1), K(bitmask), None,
+                           A.bitwise_and, None, [(pp, m0, m1)], [("hl", 192 * j + m0, 192 * j + m1)], n)
+                    hr = [("hl", m0, m1), ("hl", 192 + m0, 192 + m1)]
+                    if c == 0:
+                        ow = [(sb, 16 * s, 16 * s + 16)]
+                        cp("q0_" + t, lambda sb=sb: T[sb][:, s, :, :], lambda: T.hl[:, :, 0:8], hr, ow, 16)
+                        send(["t%d" % (r + 1)], [lambda sb=sb: T[sb][:, s, :, :]], ow, [others(sb, 16)], 4096)
+                    m0 = max(m0, 8)
+                    cp("q3_" + t, lambda dg=dg, m0=m0, m1=m1: T[dg][:, :, 56 + m0:56 + m1], lambda m0=m0, m1=m1: T.hl[:, :, m0:m1], hr,
+                       [(dg + "o", m0, m1)], 2 * n)
         if not last:
-            dg = "dg%d" % r
-            dma("tab0_%d" % r, "S", lambda: T.tab[0:128:16, :], lambda dg=dg: T[dg][:, 0, :], [(dg, 0, 256)], [("tabr0", 0, 2)], 65536)
-            dma("tab1_%d" % r, "S", lambda: T.tab[1:128:16, :], lambda dg=dg: T[dg][:, 1, :], [(dg, 256, 512)], [("tabr1", 0, 2)], 65536)
+            dg, sb = "dg%d" % r, "sb%d" % r
+            for j in range(2):
+                ac("u%d_%d" % (j, r), D(dg, j, 0, 64), lambda sb=sb, j=j: T[sb][:, :, j, :], AF.Identity, [whole(sb)], [(dg, j, j + 1)], 64)
+                dma("tab%d_%d" % (j, r), "S", lambda j=j: T.tab[j:128:16, :], D(dg, j, 0, TW), [(dg, j, j + 1), (dg + "o", 0, 192)],
+                    [("tabr%d" % j, 0, 2)], 63488)
         else:
-            tsw("o_t", "pt", pn, float(OWN), float(B), A.is_ge, A.mult)
-            ttw("o_p", "po", pn, "pt", A.subtract)
             dma("syp", "S", lambda: T.yp[:], W("po"), [whole("po")], [], 98304)
-        for c in range(NC):
-            for k, (lo, hi) in enumerate(cuts4(r, c)):
+        for c, (c0, c1) in enumerate(cb):
+            cs = cuts4(r, c, c0, c1)
+            fl = int(eng("fm_%d_%d" % (r, c), "0"))
+            for k, (lo, hi) in enumerate(cs):
                 t = "%d_%d_%d" % (r, c, k)
-                e = eng("hv_" + t, "V")
-                n = hi - lo
+                e, n = eng("hv_" + t, "V"), hi - lo
+                magic = False
                 if eng("g4_" + t, "V") == "A":
-                    gather("g4_" + t, "A", "bg", lo, hi, x, DUP + V, sel, [(x, 0, DUP + V)])
-                    two("m4_" + t, "pq", "eye", "eye", "bg", lo, hi, x)
-                    sb, a, rd, cyc = "pq", lo % CH, banks("pq", lo, hi), n
+                    magic = last and e == "V"
+                    a = place(lo, c0, fl)
+                    gather("g4_" + t, "A", "bg", lo, hi, x, NW, sel, [(x, 0, NW)])
+                    two("m4_" + t, "pq", a, "eyeg" if magic else "eye", "eyeh" if magic else "eye", "bg", lo, hi, x)
+                    sb, rd, cyc = "pq", banks("pq", a, n), n
                 else:
                     sb = "sbf" if r == 0 else ("s32" if e == "A" else "s16")
-                    gtt("g4_" + t, sb, lo, hi, x, DUP + V, sel, "oc", lo, A.add)
+                    gtt("g4_" + t, sb, x, NW, sel, x, lo, hi, NW + lo, A.add)
                     a, rd, cyc = lo, (sb, lo, hi), n // 2
                 bias = 127.875 if r == 0 else -0.125
-                ob, o0 = ("y3", lo) if last else (xn, OWN + lo)
-                if e == "A":
-                    op("hv_" + t, "A", lambda ob=ob, o0=o0, sb=sb, a=a, n=n, bias=bias:
-                       act.activation(T[ob][:, o0:o0 + n], T[sb][:, a:a + n], AF.Identity, bias=bias, scale=0.5), [rd], [(ob, o0, o0 + n)], ("a", n))
+                ob, o0 = ("y3", lo) if last else (xn, own(lo, hi)[0][2])
+                if magic:
+                    ts("hv_" + t, C("yo", lo, hi), C(sb, a, a + n), K(MAGIC), K(MAGIC + 128.0), A.add, A.subtract, [rd], [("yo", lo, hi)], n)
+                elif e == "A":
+                    ac("hv_" + t, C(ob, o0, o0 + n), C(sb, a, a + n), AF.Identity, [rd], [(ob, o0, o0 + n)], n, bias=K(bias), scale=0.5)
                 else:
                     ts("hv_" + t, C(ob, o0, o0 + n), C(sb, a, a + n), K(0.5), K(bias), A.mult, A.add, [rd], [(ob, o0, o0 + n)], cyc)
                 if last:
-                    if eng("hz_" + t, "A") == "A":
-                        op("hz_" + t, "A", lambda lo=lo, hi=hi: act.activation(T.yo[:, lo:hi], T.y3[:, lo:hi], AF.Identity, bias=-128.0),
-                           [("y3", lo, hi)], [("yo", lo, hi)], ("a", n))
+                    if magic:
+                        pass
+                    elif eng("hz_" + t, "V") == "A":
+                        ac("hz_" + t, C("yo", lo, hi), C("y3", lo, hi), AF.Identity, [("y3", lo, hi)], [("yo", lo, hi)], n, bias=K(-128.0))
                     else:
                         ts("hz_" + t, C("yo", lo, hi), C("y3", lo, hi), K(-128.0), None, A.add, None, [("y3", lo, hi)], [("yo", lo, hi)], n // 2)
-                    dma("syq_%d" % (2 * c + k), "S", lambda lo=lo, hi=hi: T.yq[:, lo:hi], C("yo", lo, hi), [("yo", lo, hi)], [], 256 * n)
+                    if (c, k) != (0, 0):
+                        l2 = 0 if lo == B else lo
+                        dma("syq_%d_%d" % (c, k), "S", lambda l2=l2, hi=hi: T.yq[:, l2:hi], C("yo", l2, hi), [("yo", l2, hi)], [], 256 * (hi - l2))
                 elif c == 0 and k == 0:
-                    send("x%d" % (r + 1), C(xn, OWN, OWN + B), C(xn, b0, b1), [(xn, OWN, OWN + B)], others(xn, B))
-                    dma("own_%d" % r, "S", C(xn, b0, b1), C(xn, OWN, OWN + B), [(xn, OWN, OWN + B)], [(xn, b0, b1)], 32768)
+                    send(["x%d" % (r + 1)], [C(xn, b0, b1)], [(xn, b0, b1)], [others(xn, B)], 32768)
             if not last:
-                dma("dup_%d_%d" % (r, c), "S", C(xn, DUP + c * CH, DUP + (c + 1) * CH), C(xn, OWN + c * CH, OWN + (c + 1) * CH),
-                    [(xn, OWN + c * CH, OWN + (c + 1) * CH)], [(xn, DUP + c * CH, DUP + (c + 1) * CH)], 262144)
-                h = hull(r + 1, [c])
-                if h:
-                    dma("oc_%d_%d" % (r, c), "S", C("oc", h[0], h[1]), C(xn, OWN + h[0], OWN + h[1]),
-                        [(xn, OWN + h[0], OWN + h[1])], [("oc", h[0], h[1])], 256 * (h[1] - h[0]))
+                for k, (a, b, w) in enumerate(own(c0, c1)):
+                    h = copied(r + 1, a, b)
+                    if h:
+                        dma("dup_%d_%d" % (r, 4 if a == 0 else c), "S", C(xn, NW + h[0], NW + h[1]), C(xn, w + h[0] - a, w + h[1] - a),
+                            [(xn, w + h[0] - a, w + h[1] - a)], [(xn, NW + h[0], NW + h[1])], 256 * (h[1] - h[0]))
     return ops
 
 
@@ -391,7 +472,7 @@ def rank_program(g, core, T, topo):
     ops = build(g, T, topo, core, CFG)
     deps = hazards(ops)
     byname = {o[0]: o for o in ops}
-    order = list(ORDER)
+    order = [ops[i][0] for i in ORDER]
     queue = {"A": g.scalar, "V": g.vector, "P": g.tensor, "S": g.sync, "G": g}
     npeer = len(T.cores) - 1
     kind = {n: byname[n][5][0] for n in order}
@@ -425,7 +506,7 @@ def rank_program(g, core, T, topo):
         o = byname[n]
         q = o[1]
         if q == "R":
-            mark[n] = (n, mark["snd_" + n[4:]][1] * npeer)
+            mark[n] = (n, mark[o[2]][2] * npeer)
             continue
         for d in waits[n]:
             queue[q].wait_ge(T.sem[mark[d][0]], mark[d][1])
@@ -434,7 +515,7 @@ def rank_program(g, core, T, topo):
             ins.then_inc(T.sem[n], 16)
             mark[n] = (n, 16)
         elif kind[n] == "send":
-            mark[n] = ("out_" + n[4:], ins)
+            mark[n] = ("out_" + n[4:], ins[0], ins[1])
         elif n in waited:
             count[q] += 1
             ins.then_inc(T.sem["q" + q], 1)

@@ -7,17 +7,20 @@ TW = NW // 16
 BIG = 65536.0
 FLAG = (8192.0, 16384.0, 32768.0)
 MAGIC = 1.5 * 2 ** 23
+LOW = (255.5, -1.0, -2.0)
 
 SCRATCH = {"tab": ("sbuf", [128, NW], "bfloat16"), "clrs": ("sbuf", [128, 2048], "bfloat16"),
            "c32": ("sbuf", [128, 64], "bfloat16"), "ieye": ("sbuf", [128, 128], "float32"), "eyef": ("sbuf", [128, 128], "float32"),
-           "pb": ("sbuf", [128, 128], "int32"), "s16": ("sbuf", [128, V], "float16"), "s32": ("sbuf", [128, V], "float32"),
-           "hl": ("sbuf", [128, 2, 192], "int32"), "di": ("sbuf", [128, 2, 192], "bfloat16")}
+           "pb": ("sbuf", [128, 128], "int32"), "cmg": ("sbuf", [128, HF], "bfloat16"),
+           "hl": ("sbuf", [128, 2, 192], "int32"), "di": ("sbuf", [128, 2, 192], "bfloat16"),
+           "ps": ("psum", [128, 8 * HF], "float32")}
 for _names, _w, _t in (("am am2 eye eyen eyes eyeb eye8 eyeu eyeh eyeg pbt", 128, "bfloat16"), ("z1 z2 z3", 144, "bfloat16"),
                        ("i16 i16b", 16, "int32"), ("msk two pw pwm", 16, "float32"), ("blk blks", 8, "int32"),
-                       ("w1 w2 kf thr0 thr1 nb0 nb1", 4, "float32"), ("ki kj thi", 4, "int32"),
+                       ("w1 w2 kf thr0 thr1 thr2 thr1s thr2s th2 nb0 nb1 nb1s", 4, "float32"), ("ki kj thi", 4, "int32"),
                        ("vd0 vd vd1 vd2 td p0 p3 pp0 pp1 pp2 sf0 sf1 sf2 sg0 sg1 sg2", 192, "int32"),
                        ("te tf tg", 192, "bfloat16"), ("po hk", 192, "float32"),
-                       ("hg de bits ab vi sbf bg y3 yo", V, "bfloat16"), ("x0 x1 x2", NW + V, "bfloat16")):
+                       ("hg de bits ab vi bg y3 yo d0", V, "bfloat16"), ("x0 x1 x2", NW, "bfloat16"),
+                       ("lV0 lV1 lV2", V, "float16"), ("lA0 lA1 lA2", V, "float32")):
     for _n in _names.split():
         SCRATCH[_n] = ("sbuf", [128, _w], _t)
 for _r in range(RO):
@@ -26,32 +29,27 @@ for _r in range(RO):
 for _r in range(RO - 1):
     SCRATCH["sb%d" % _r] = ("sbuf", [128, 8, 2, 8], "bfloat16")
     SCRATCH["dg%d" % _r] = ("sbuf", [128, 2, 256], "bfloat16")
-for _n in ("pa", "pz", "pc", "pd"):
-    SCRATCH[_n] = ("psum", [128, HF], "float32")
-SCRATCH["ps"] = ("psum", [128, 2 * HF], "float32")
-SCRATCH["pq"] = ("psum", [128, 2 * HF], "float32")
 
-DMAS = ["lpb0", "lpb1", "lpar", "lqb", "lq0", "lq1", "lq2", "lam", "lth", "lclr", "ldup0", "ldup1", "ldup2", "ltab0", "ltab1", "syp"]
+DMAS = ["lpb0", "lpb1", "lpar", "lqb", "lq0", "lq1", "lq2", "lam", "lth", "lclr", "ltab0", "ltab1", "syp"]
 for _r in range(RO - 1):
-    DMAS += ["tab0_%d" % _r, "tab1_%d" % _r] + ["dup_%d_%d" % (_r, _c) for _c in range(5)]
-DMAS += ["syq_%d_%d" % (_c, _k) for _c in range(4) for _k in range(5)]
-SENDS = ["t0", "x0", "t1", "x1", "t2", "x2"]
+    DMAS += ["tab0_%d" % _r, "tab1_%d" % _r]
+DMAS += ["syq_%d" % _k for _k in range(24)]
+SENDS = ["xa", "t0", "x0", "t1", "x1", "t2", "x2"]
 SEMAPHORES = ["qA", "qV", "qP", "qG"] + DMAS + ["arr_" + _s for _s in SENDS] + ["out_" + _s for _s in SENDS]
 
 CFGS = """
-Qdup_0_0=A Qdup_0_1=A Qlclr=A Qlq2=A Qtab0_0=A Wlclr=x0 Wldup0=t0 Wldup1=t0 Wldup2=t0 Wlq2=x0 bt_0_0_0=V bt_0_0_1=V bt_1_0_0=V bt_1_0_1=V bt_2_0_1=V bt_2_1_1=V cp_0_0=0 cp_0_1=0 cp_1_0=0 cp_1_1=0 cp_1_2=0 cp_2_1=0 cq_0_2=0 cq_2_2=0 em4_1_0_1=1 em4_1_0_2=1 em4_1_2_1=1 em4_2_0_1=1 em4_2_0_2=1 eme_0_0_1=1 eme_0_1_0=1 eme_1_0_0=1 eme_2_1_0=1 ems_0_0_0=1 ems_0_0_1=1 ems_1_0_0=1 ems_1_0_1=1 ems_1_1_1=1 ems_2_0_1=1 ems_2_1_1=1 fm_0_1=1 fm_2_0=1 g1_0_0_1=V g1_0_1_1=V g1_1_0_0=V g1_1_1_1=V g1_2_0_1=V g1_2_2_1=V g2_0_0_0=V g2_0_1_1=U g2_0_2_0=V g2_0_2_1=V g2_1_0_1=V g2_1_1_1=V g2_1_2_1=V g2_2_0_0=V g2_2_0_1=V g2_2_1_1=V g2_2_2_1=V g4_0_0_0=A g4_0_0_1=A g4_0_1_0=A g4_0_1_1=A g4_1_0_1=A g4_1_0_2=A g4_1_1_0=A g4_1_2_1=A g4_2_0_1=A g4_2_0_2=A g4_2_1_0=A g4_2_2_1=A hk_0_0=V hk_1_0=V hk_2_1=V hv_0_0_1=A hv_0_1_0=A hv_0_1_1=A hv_1_0_0=A hv_1_0_1=A hv_1_0_2=A hv_1_1_0=A hv_1_2_1=A hv_2_0_0=A hv_2_0_1=A hv_2_0_2=A hv_2_2_0=A hz_2_0_0=A hz_2_0_2=A hz_2_1_1=A n1_0_2=1 n1_1_2=1 n1_2_1=1 n3_0_0=1 n3_0_1=1 n3_1_1=1 n3_2_0=1 n3_2_2=1 n4_0_0=1 n4_0_2=1 na_0_0=1 na_0_1=1 na_1_2=1 na_2_0=1 na_2_2=1 nb_2_2=1 one=0
+Qlclr=A Qlq1=A Qlq2=A Qsyq_16=A Wlclr=t0 Wlq2=xa bt_0_0=V bt_0_8=V bt_1_0=V bt_1_12=V bt_1_4=V bt_2_0=V bt_2_12=V bt_2_4=V c40=1,4,8,12,16,20 c41=1,4,8,12,16,20 c42=4,8,12,16,20 c_eye8=V c_eyeb=V cp_0_0=0 cp_0_8=0 cp_1_0=0 cp_1_8=0 cp_2_0=0 cq_0_8=0 cq_1_8=0 dc_0_12=A dc_0_20=A dc_0_4=A em4_0_1=1 em4_1_1=1 em4_1_16=1 em4_1_8=1 em4_2_16=1 eme_0_8=1 eme_1_16=1 eme_1_8=1 eme_2_8=1 ems_0_12=1 ems_0_16=1 ems_0_20=1 ems_0_4=1 ems_1_12=1 ems_1_16=1 ems_1_20=1 ems_1_4=1 ems_1_8=1 ems_2_12=1 ems_2_16=1 ems_2_4=1 ems_2_8=1 g1_0_0=V g1_0_20=V g1_1_20=V g1_1_4=V g1_2_20=V g1_2_4=V g2_0_12=S g2_0_20=S g2_0_4=S g2_1_12=S g2_1_20=S g2_1_4=S g2_2_12=S g2_2_20=S g2_2_4=S g4_0_1=A g4_0_16=A g4_0_4=A g4_0_8=A g4_1_1=A g4_1_16=A g4_1_8=A g4_2_0=A g4_2_16=A g4_2_8=A hk_0_8=V hk_2_8=V hv_0_1=A hv_0_4=A hv_0_8=A hv_1_1=A hv_1_16=A hv_1_8=A hv_2_0=A hv_2_20=A hv_2_4=A lw_1_0=A lw_1_12=A lw_1_4=A n1_0_0=1 n1_0_8=1 n1_1_8=1 n1_2_8=1 n3_1_0=1 n3_1_16=1 n3_2_0=1 n3_2_16=1 u0_1=V u1_0=G
 """
 ORDERS = """
-4 0 3 11 6 9 2 1 5 23 22 10 49 12 15 55 52 54 8 51 7 20 21 29 13 14 16 40 17 58 43 30 18 19 61 37 31 26 38 62 27 63 28 50 32 64 65 67 44 36 34 42 41 35 48 33 45 39 68 59 107 60 24 90 47 46 66 71 72 73 74 79 25 75 78 92 76 88 87 80 83 77 93 81 105 91 101 89 69 97 95 84 96 104 109 85 121 98 94 106 99 82 113 100 110 53 112 108 123 125 120 111 102 114 103 135 86 127 122 145 144 136 115 146 137 117 116 147 148 126 162 128 167 163 129 164 118 131 165 166 124 168 119 130 132 169 138 133 149 139 151 150 140 152 172 134 154 153 141 155 142 158 156 160 143 159 70 161 173 175 179 200 174 176 56 171 177 157 180 183 182 181 170 188 187 184 185 178 189 196 197 281 192 186 190 201 198 205 199 204 217 214 203 206 202 210 207 218 209 213 193 208 220 215 222 216 194 230 221 211 229 223 212 254 255 245 233 256 219 246 257 258 224 247 231 259 237 272 225 232 236 191 273 238 195 235 274 275 226 234 239 227 241 57 277 280 228 240 242 276 282 260 248 243 283 261 249 262 250 244 295 268 286 263 264 278 251 265 252 266 269 253 289 270 279 271 294 287 285 284 292 288 296 267 316 290 297 331 293 299 300 379 298 291 309 304 301 302 314 308 305 313 317 303 310 306 320 328 315 329 333 319 332 311 307 334 318 348 330 321 338 337 322 323 351 347 324 339 335 349 336 325 340 341 326 354 342 350 327 353 343 355 352 344 361 345 362 356 363 357 385 384 312 378 386 346 387 375 380 364 358 370 376 365 359 381 366 371 394 388 377 389 390 360 382 367 383 395 368 372 396 391 369 373 398 402 374 397 392 399 403 393 400 404 401 405
+4 3 9 7 10 8 0 42 15 45 63 13 40 51 28 43 14 29 2 5 1 25 6 24 54 30 20 16 64 17 36 31 34 52 46 56 44 38 32 12 18 60 70 35 71 41 82 37 57 79 33 68 22 11 53 26 23 19 21 65 69 47 50 39 118 61 105 72 124 67 49 48 66 62 80 89 27 93 85 94 86 90 95 87 76 99 106 91 84 117 96 88 98 103 81 116 104 100 107 125 101 126 122 108 136 123 109 92 110 111 127 113 119 143 144 140 129 102 112 121 135 120 145 114 141 142 97 139 132 137 138 131 115 163 162 153 128 164 146 181 154 130 155 55 147 177 165 184 178 179 166 180 133 150 185 182 149 148 151 134 156 73 157 167 152 158 159 168 169 75 160 78 175 186 183 196 173 170 161 83 174 176 187 191 188 171 190 189 197 172 199 204 194 192 200 193 235 220 238 201 255 209 202 74 205 198 214 208 213 210 221 218 203 206 77 230 222 211 219 250 215 258 239 223 229 217 216 234 236 224 240 225 231 237 195 212 259 232 233 241 251 226 227 242 244 249 260 207 256 257 252 305 261 295 300 246 254 253 228 243 277 276 267 278 268 245 269 279 294 296 247 59 58 297 264 262 291 263 248 281 270 265 292 271 266 272 273 282 283 274 280 293 284 287 275 299 289 288 290 301 285 303 298 286 308 313 322 304 306 302 307 312 317 348 314 333 318 351 315 309 326 310 327 319 311 331 334 321 323 343 335 324 332 316 342 330 347 328 349 352 336 329 350 362 363 337 353 344 345 370 338 371 346 339 354 367 356 368 369 366 340 358 341 355 378 357 364 372 365 379 373 320 380 325 392 359 375 360 374 361 396 376 407 393 381 387 377 382 388 389 384 383 390 385 403 397 398 391 399 394 386 404 411 405 395 406 400 408 401 409 412 402 413 410
 """
 CFG = dict(_a.split("=") for _a in CFGS.split())
 ORDER = [int(_a) for _a in ORDERS.split()]
 
 
-def build(g, T, topo, core, cfg):
+def build(g, T, topo, core, cfg, bank):
     A, AF, X = AluOpType, ActivationFunctionType, AxisListType.X
     s = T.rank_of(core)
-    peers = [c for c in T.cores if c != core]
     ops = []
     vec, act, pe = g.vector, g.scalar, g.tensor
     eng = cfg.get
@@ -69,7 +67,7 @@ def build(g, T, topo, core, cfg):
     def dma(name, q, out, in_, rd, wr, nbytes):
         q = eng("Q" + name, q)
         e = g.sync if q == "S" else g.scalar
-        if "W" + name in cfg:
+        if eng("W" + name, "0") != "0":
             rd = rd + [("tok_" + cfg["W" + name], 0, 1)]
         op(name, q, lambda: e.dma_start(out(), in_()), rd, wr, ("dma", nbytes))
 
@@ -97,6 +95,12 @@ def build(g, T, topo, core, cfg):
     def C(n, lo, hi):
         return lambda: T[n][:, lo:hi]
 
+    def P(n, lo, hi):
+        return lambda: T.ps[:, bank[n] * HF + lo:bank[n] * HF + hi]
+
+    def PB(n, lo=0, hi=1):
+        return (n, lo // HF * HF, ((hi - 1) // HF + 1) * HF)
+
     def D(n, j, lo, hi):
         return lambda: T[n][:, j, lo:hi]
 
@@ -112,29 +116,25 @@ def build(g, T, topo, core, cfg):
     def ownr(x, lo, hi):
         return [(x, w, w + b - a) for a, b, w in own(lo, hi)]
 
-    def send(tags, aps, rd, wr, nbytes):
+    def send(t, ap, rd, buf, w, nbytes, steps):
+        n = len(T.cores)
+        to = [T.cores[(s + k) % n] for k in steps]
+
         def fn():
-            es = [e for e in topo.engines(core, peers[0]) if all(e in topo.engines(core, c) for c in peers)]
-            es = es[:int(eng("E" + tags[0], len(es)))]
-            n = len(es) // len(tags)
-            ids = [DstId(rid=topo.addr(c)[0], pnc=topo.addr(c)[1]) for c in peers]
-            g.remote_dma_fused([RemoteDMATransfer(dst_ids=ids, dma_engine_mask=sum(1 << e for e in es[k * n:(k + 1) * n]),
-                                                  remote_sem=T.sem["arr_" + t], src=aps[k](), dsts=[aps[k]() for c in peers])
-                                for k, t in enumerate(tags)], local_sem=T.sem["out_" + tags[0]])
-            return (n * len(tags), n)
-        op("snd_" + tags[0], "G", fn, rd, [("tok_" + t, 0, 1) for t in tags], ("send", nbytes))
-        for k, t in enumerate(tags):
-            op("arr_" + t, "R", "snd_" + tags[0], [("tok_" + t, 0, 1)], wr[k], ("arr", 1))
+            es = [e for e in topo.engines(core, to[0]) if all(e in topo.engines(core, c) for c in to)]
+            ids = [DstId(rid=topo.addr(c)[0], pnc=topo.addr(c)[1]) for c in to]
+            g.remote_dma_fused([RemoteDMATransfer(dst_ids=ids, dma_engine_mask=sum(1 << e for e in es), remote_sem=T.sem["arr_" + t],
+                                                  src=ap(), dsts=[ap() for c in to])], local_sem=T.sem["out_" + t])
+            return (len(es), len(es) * len(to))
+        op("snd_" + t, "G", fn, rd, [("tok_" + t, 0, 1)], ("send", nbytes, len(to)))
+        op("arr_" + t, "R", "snd_" + t, [("tok_" + t, 0, 1)], [(buf, (s - k) % n * w, (s - k) % n * w + w) for k in steps], ("arr", 1))
 
-    def others(buf, w):
-        return [(buf, k * w, (k + 1) * w) for k in range(len(T.cores)) if k != s]
-
-    def mm(name, bank, n, terms, rd, cyc):
+    def mm(name, pn, n, terms, rd, cyc):
         def fn():
             for k, (l, r_) in enumerate(terms):
-                ins = pe.matmul(T[bank][:, 0:n], T[l][:], r_(), k == 0, k == len(terms) - 1)
+                ins = pe.matmul(P(pn, 0, n)(), T[l][:], r_(), k == 0, k == len(terms) - 1)
             return ins
-        op(name, "P", fn, rd + [whole(l) for l, r_ in terms], [whole(bank)], ("p", cyc))
+        op(name, "P", fn, rd + [whole(l) for l, r_ in terms], [PB(pn)], ("p", cyc))
 
     ms("m_pb", "pb", 0, 128, 0, 128)
     dma("lpb0", "S", lambda: T.pb[0:128:16, :], lambda: T.par[:, 0:8], [], [("pb", 0, 128)], 4096)
@@ -156,11 +156,11 @@ def build(g, T, topo, core, cfg):
     ts("b_t", W("pbt"), W("pb"), C("msk", 1, 2), None, A.mult, None, pbr + [whole("msk")], [whole("pbt")], 128)
     tt("b_d", C("tab", b0, b1), W("pb"), W("pbt"), A.subtract, pbr + [whole("pbt")], [("tab", b0, b1)], 256)
     trd = [("tab", b0, b1), ("tabr0", 0, 1), ("tabr1", 0, 1)]
-    if eng("one", "1") == "1":
-        send(["t0", "x0"], [C("tab", b0, b1), C("x0", b0, b1)], trd + [("x0", b0, b1)], [others("tab", B), others("x0", B)], 65536)
-    else:
-        send(["t0"], [C("tab", b0, b1)], trd, [others("tab", B)], 32768)
-        send(["x0"], [C("x0", b0, b1)], [("x0", b0, b1)], [others("x0", B)], 32768)
+    every, ka = range(1, len(T.cores)), int(eng("ka", "1"))
+    send("t0", C("tab", b0, b1), trd, "tab", B, 32768, every)
+    if ka:
+        send("xa", C("x0", b0, b1), [("x0", b0, b1)], "x0", B, 32768, every[:ka])
+    send("x0", C("x0", b0, b1), [("x0", b0, b1)], "x0", B, 32768, every[ka:])
     for c in range(3):
         lo, hi = max(B, c * 1024), (c + 1) * 1024
         dma("lq%d" % c, "S", C("x0", lo + M - B, hi + M - B), lambda lo=lo, hi=hi: T.q[:, lo:hi], [], ownr("x0", lo, hi), 256 * (hi - lo))
@@ -187,34 +187,37 @@ def build(g, T, topo, core, cfg):
         ts("c_" + z, lambda z=z: T[z][:, 15:143:16], W("blks"), K(0.0), wt, A.is_equal, A.mult, [whole("blks")] + rd, [whole(z)], 8)
     tsw("c_eye", "eye", "ieye", 0.0, None, A.is_equal, None)
     tsw("c_eyef", "eyef", "ieye", 0.0, None, A.is_equal, None)
-    for n, src, sc in (("eyen", "eye", -1.0), ("eyes", "eye", 1.0 / 16), ("eyeb", "eye", float(TW)), ("eye8", "eye", 8.0), ("eyeu", "eye", 176.0),
-                       ("eyeh", "eye", 0.5), ("eyeg", "eye", 255.0 / 512), ("am2", "am", 2.0)):
-        ac("c_" + n, W(n), W(src), AF.Identity, [whole(src)], [whole(n)], 128, scale=sc)
-    mm("i_m", "pa", 192, [("eyes", D("di", 0, 0, 192)), ("eye8", D("di", 1, 0, 192)), ("eye", W("te")), ("eyeu", W("tg"))],
+    four = [[128 * int(a) for a in ("0," + eng("c4%d" % r, ("1,8,16", "1,8,16", "8,16")[r]) + ",24").split(",")] for r in range(RO)]
+    onA = [eng("hv_2_%d" % (lo // 128), "V") for lo in four[2][:-1] if eng("g4_2_%d" % (lo // 128), "V") == "A"]
+    for n, sc in [("eyen", -1.0), ("eyes", 1.0 / 16), ("eyeb", float(TW)), ("eye8", 8.0), ("eyeu", 176.0)] + (
+            [("eyeh", 0.125), ("eyeg", 255.0 / 2048)] if onA else []):
+        if eng("c_" + n, "A") == "A":
+            ac("c_" + n, W(n), W("eye"), AF.Identity, [whole("eye")], [whole(n)], 128, scale=sc)
+        else:
+            ts("c_" + n, W(n), W("eye"), K(sc), None, A.mult, None, [whole("eye")], [whole(n)], 64)
+    if "A" in onA:
+        ms("m_cmg", "cmg", 0, HF, MAGIC, HF // 2)
+    mm("i_m", "@i", 192, [("eyes", D("di", 0, 0, 192)), ("eye8", D("di", 1, 0, 192)), ("eye", W("te")), ("eyeu", W("tg"))],
        [whole("di"), whole("te"), whole("tg")], 768)
-    cp("i_idx", W("idx0"), C("pa", 0, 192), [whole("pa")], [whole("idx0")], 192)
+    cp("i_idx", W("idx0"), P("@i", 0, 192), [PB("@i")], [whole("idx0")], 192)
     ts("c_kj", C("kj", 0, 1), C("ki", 0, 1), K(15), None, A.bitwise_and, None, [whole("ki")], [whole("kj")], 1)
     cp("c_kf", C("kf", 0, 1), C("kj", 0, 1), [whole("kj")], [whole("kf")], 1)
     ts("c_vd", W("vd"), W("vd0"), C("kf", 0, 1), None, A.add, None, [whole("vd0"), whole("kf")], [whole("vd")], 192)
     for r in (1, 2):
         tsw("c_vd%d" % r, "vd%d" % r, "vd", FLAG[r] - FLAG[0], None, A.add, None)
-    cp("c_thr0", C("thr0", 0, 1), C("thi", 0, 1), [whole("thi")], [whole("thr0")], 1)
-    ts("c_nb0", C("nb0", 0, 1), C("thi", 0, 1), K(-1.0), K(-0.5), A.mult, A.add, [whole("thi")], [whole("nb0")], 1)
-    mm("c_cs", "pc", 1, [("am", C("c32", 0, 1))], [whole("c32")], 64)
-    ts("c_thr1", C("thr1", 0, 1), C("pc", 0, 1), K(8.0), C("thr0", 0, 1), A.mult, A.add, [whole("pc"), whole("thr0")], [whole("thr1")], 1)
-    ts("c_nb1", C("nb1", 0, 1), C("thr1", 0, 1), K(-1.0), K(-0.5), A.mult, A.add, [whole("thr1")], [whole("nb1")], 1)
+    late, need = len(ops), set()
 
-    def wrap(name, bank, z, data, lo, hi, names):
+    def wrap(name, pn, z, data, lo, hi, names):
         n = (hi - lo) // 16
 
         def fn():
             for i in range(16):
-                ins = pe.matmul(T[bank][:, 0:n], T[z][:, 15 - i:143 - i], T[data][:, lo + i:hi:16], i == 0 and not names, i == 15)
+                ins = pe.matmul(P(pn, 0, n)(), T[z][:, 15 - i:143 - i], T[data][:, lo + i:hi:16], i == 0 and not names, i == 15)
             return ins
         if names:
-            op("v1" + name[2:], "P", lambda: pe.matmul(T[bank][:, 0:n], T.eyef[:], T.hk[:, lo // 16:hi // 16], True, False),
-               [whole("eyef"), ("hk", lo // 16, hi // 16)], [whole(bank)], ("p", 4 * max(64, n)))
-        op(name, "P", fn, [whole(z), (data, lo, hi)], [whole(bank)], ("p", max(64, n) * 16))
+            op("v1" + name[2:], "P", lambda: pe.matmul(P(pn, 0, n)(), T.eyef[:], T.hk[:, lo // 16:hi // 16], True, False),
+               [whole("eyef"), ("hk", lo // 16, hi // 16)], [PB(pn)], ("p", 4 * max(64, n)))
+        op(name, "P", fn, [whole(z), (data, lo, hi)], [PB(pn)], ("p", max(64, n) * 16))
 
     def gather(name, e, out, lo, hi, win, whi, off, rd):
         a, b = lo // 16, hi // 16
@@ -225,140 +228,157 @@ def build(g, T, topo, core, cfg):
             op(name, "V", lambda: vec.tensor_copy(T[out][:, lo:hi], T[win][:, 0:whi].indirect(T[off][:, a:b])),
                rd + [(off, a, b)], [(out, lo, hi)], ("gv", hi - lo))
 
-    def gtt(name, out, win, whi, off, in1, lo, hi, w, o):
-        op(name, "V", lambda: vec.tensor_tensor(T[out][:, lo:hi], T[win][:, 0:whi].indirect(T[off][:, lo // 16:hi // 16]), T[in1][:, w:w + hi - lo], o),
-           [(win, 0, whi), (off, lo // 16, hi // 16), (in1, w, w + hi - lo)], [(out, lo, hi)], ("gt", hi - lo))
+    def gtt(name, out, o0, win, whi, off, in1, lo, hi, o):
+        op(name, "V", lambda: vec.tensor_tensor(T[out][:, o0:o0 + hi - lo], T[win][:, 0:whi].indirect(T[off][:, lo // 16:hi // 16]), T[in1][:, lo:hi], o),
+           [(win, 0, whi), (off, lo // 16, hi // 16), (in1, lo, hi)], [(out, o0, o0 + hi - lo)], ("gt", hi - lo))
 
-    def two(name, bank, o0, l0, l1, data, lo, hi, x):
-        if lo >= B and hi - lo <= HF and eng("e" + name, "0") == "1":
+    def two(name, pn, o0, l0, l1, data, lo, hi, x, rnd=False):
+        early = lo >= B and hi - lo <= HF and eng("e" + name, "0") == "1"
+        if early:
             w0 = lo + M - B
-            op("e" + name, "P", lambda: pe.matmul(T[bank][:, o0:o0 + hi - lo], T[l1][:], T[x][:, w0:w0 + hi - lo], True, False),
-               [whole(l1)] + ownr(x, lo, hi), [banks(bank, o0, hi - lo)], ("p", hi - lo))
-            op(name, "P", lambda: pe.matmul(T[bank][:, o0:o0 + hi - lo], T[l0][:], T[data][:, lo:hi], False, True),
-               [whole(l0), (data, lo, hi)], [banks(bank, o0, hi - lo)], ("p", hi - lo))
-            return
+            op("e" + name, "P", lambda: pe.matmul(P(pn, o0, o0 + hi - lo)(), T[l1][:], T[x][:, w0:w0 + hi - lo], True, False),
+               [whole(l1)] + ownr(x, lo, hi), [PB(pn, o0, o0 + hi - lo)], ("p", hi - lo))
 
         def fn():
             for a, b, w in own(lo, hi):
                 while a < b:
                     o = o0 + a - lo
                     n = min(b - a, HF - o % HF)
-                    pe.matmul(T[bank][:, o:o + n], T[l1][:], T[x][:, w:w + n], True, False)
-                    ins = pe.matmul(T[bank][:, o:o + n], T[l0][:], T[data][:, a:a + n], False, True)
+                    if not early:
+                        pe.matmul(P(pn, o, o + n)(), T[l1][:], T[x][:, w:w + n], True, False)
+                    ins = pe.matmul(P(pn, o, o + n)(), T[l0][:], T[data][:, a:a + n], False, not rnd)
+                    if rnd:
+                        pe.matmul(P(pn, o, o + n)(), T.eye[:], T.cmg[:, 0:n], False, False)
+                        ins = pe.matmul(P(pn, o, o + n)(), T.eyen[:], T.cmg[:, 0:n], False, True)
                     a, w = a + n, w + n
             return ins
-        op(name, "P", fn, [whole(l0), whole(l1), (data, lo, hi)] + ownr(x, lo, hi), [banks(bank, o0, hi - lo)], ("p", 2 * (hi - lo)))
-
-    def banks(b, o, n):
-        return (b, o // HF * HF, ((o + n - 1) // HF + 1) * HF)
+        op(name, "P", fn, [whole(l0), whole(l1), (data, lo, hi)] + ownr(x, lo, hi) + ([whole("cmg"), whole("eye"), whole("eyen")] if rnd else []),
+           [PB(pn, o0, o0 + hi - lo)], ("p", (2 - early + 2 * rnd) * (hi - lo)))
 
     def chunks(tag, r):
-        e = [0] + [256 * int(a) for a in eng("%s%d" % (tag, r), "4,8").split(",") if a] + [V]
+        e = [0] + [128 * int(a) for a in eng("%s%d" % (tag, r), "8,16").split(",")] + [V]
         return list(zip(e[:-1], e[1:]))
 
-    def cuts(tag, lo, hi, fl=None, form=None):
-        ps = [(a, min(hi, a + HF)) for a in range(lo, hi, HF)]
-        if eng(tag, "2") != "1":
-            return ps
-        if fl is None:
-            return [(lo, hi)]
+    def cuts(tag, lo, hi):
+        return [(lo, hi)] if eng(tag, "2") == "1" else [(a, min(hi, a + HF)) for a in range(lo, hi, HF)]
+
+    def calls2(r):
+        return [(lo, hi, eng("g2_%d_%d" % (r, lo // 128), "A")) for c0, c1 in chunks("cb", r) for lo, hi in cuts("n2_%d_%d" % (r, c0 // 128), c0, c1)]
+
+    def runs(r, lo, hi):
+        out = []
+        for a in range(lo // HF * HF, hi, HF):
+            lb = "l%s%d" % (eng("lw_%d_%d" % (r, a // 128), "V"), r)
+            if out and out[-1][2] == lb:
+                out[-1][1] = min(hi, a + HF)
+            else:
+                out.append([max(lo, a), min(hi, a + HF), lb])
+        return out
+
+    def groups(tag, c0, c1, sub):
+        ps = [(a, min(c1, a + HF)) for a in range(c0, c1, HF)]
         out = []
         for k, (a, b) in enumerate(ps):
-            if out and (k + fl) % 2 and (not form or form[k] == form[k - 1]):
+            if out and eng(tag, "2") == "1" and sub[a] == sub[out[-1][0]] and out[-1][1] - out[-1][0] == HF:
                 out[-1] = (out[-1][0], b)
             else:
                 out.append((a, b))
         return out
 
-    def place(lo, c0, fl):
-        return ((lo - c0) // HF + fl) % 2 * HF + (lo - c0) % HF
-
-    def cuts4(r, c, c0, c1):
-        cs = cuts("n4_%d_%d" % (r, c), c0, c1, int(eng("fm_%d_%d" % (r, c), "0")))
-        return [(0, B), (B, cs[0][1])] + cs[1:] if c == 0 else cs
-
-    def copied(r, lo, hi):
-        cs = [(max(a, lo), min(b, hi)) for c, (c0, c1) in enumerate(chunks("cb", r))
-              for t, d, ps in (("g4", "V", cuts4(r, c, c0, c1)), ("g2", "A", cuts("n2_%d_%d" % (r, c), c0, c1)))
-              for k, (a, b) in enumerate(ps) if eng("%s_%d_%d_%d" % (t, r, c, k), d) == "V" and a < hi and lo < b]
-        return (min(cs)[0], max(b for a, b in cs)) if cs else None
-
-    for c in range(3):
-        h = copied(0, c * 1024, c * 1024 + 1024)
-        if h:
-            dma("ldup%d" % c, "S", C("x0", NW + h[0], NW + h[1]), lambda h=h: T.q[:, h[0]:h[1]], [], [("x0", NW + h[0], NW + h[1])], 256 * (h[1] - h[0]))
+    for lo, hi, e in calls2(0):
+        if e == "S":
+            for a, b, w in own(lo, hi):
+                nm = "dc_0_%d" % (a // 128)
+                if eng(nm, "V") == "A":
+                    ac(nm, C("d0", a, b), C("x0", w, w + b - a), AF.Identity, [("x0", w, w + b - a)], [("d0", a, b)], b - a)
+                else:
+                    cp(nm, C("d0", a, b), C("x0", w, w + b - a), [("x0", w, w + b - a)], [("d0", a, b)], (b - a) // 2)
     tabrd = [whole("tab"), ("tabr0", 0, 2), ("tabr1", 0, 2)]
     for r in range(RO):
         x, xn = "x%d" % r, "x%d" % (r + 1)
         idx, hoff, coff, sel = "idx%d" % r, "hoff%d" % r, "coff%d" % r, "sel%d" % r
         p, pn, pp, sf, sg = ("p0", "pp0", "pp1")[r], "p3", "pp%d" % r, "sf%d" % r, "sg%d" % r
-        thr, nb = ("thr0", "nb0") if r == 0 else ("thr1", "nb1")
         last, vd = r == RO - 1, ("vd", "vd1", "vd2")[r]
-        for c, (c0, c1) in enumerate(chunks("ca", r)):
-            t = "%d_%d" % (r, c)
-            for k, (lo, hi) in enumerate(cuts("n1_" + t, c0, c1)):
-                gather("g1_%s_%d" % (t, k), eng("g1_%s_%d" % (t, k), "A"), "hg", lo, hi, "tab", NW, idx, tabrd)
-            ph, m0, m1 = ("pz", "pa")[c % 2], c0 // 16, c1 // 16
+        used = [(lo, hi) for lo, hi in zip(four[r][:-1], four[r][1:]) if eng("g4_%d_%d" % (r, lo // 128), "V") == "V"]
+        used += [(lo, hi) for lo, hi, e in calls2(r) if e == "S" and r]
+        for u in range(0, V, HF):
+            cs = [(max(a, u), min(b, u + HF)) for a, b in used if a < u + HF and b > u]
+            if cs:
+                e = eng("lw_%d_%d" % (r, u // 128), "V")
+                for a, b, w in own(min(cs)[0], max(b for a, b in cs)):
+                    nm, lb = "lw_%d_%d" % (r, 1 if u == 0 < a else u // 128), "l%s%d" % (e, r)
+                    if e == "A":
+                        ac(nm, C(lb, a, b), C(x, w, w + b - a), AF.Identity, [(x, w, w + b - a)], [(lb, a, b)], b - a, bias=K(LOW[r]))
+                    else:
+                        ts(nm, C(lb, a, b), C(x, w, w + b - a), K(LOW[r]), None, A.add, None, [(x, w, w + b - a)], [(lb, a, b)], (b - a) // 2)
+        for c0, c1 in chunks("ca", r):
+            t = "%d_%d" % (r, c0 // 128)
+            for lo, hi in cuts("n1_" + t, c0, c1):
+                nm = "g1_%d_%d" % (r, lo // 128)
+                gather(nm, eng(nm, "A"), "hg", lo, hi, "tab", NW, idx, tabrd)
+            ph, m0, m1 = "@w1_" + t, c0 // 16, c1 // 16
             wrap("w1_" + t, ph, "z1", "hg", c0, c1, False)
-            cp("c1_" + t, C(hoff, m0, m1), C(ph, 0, m1 - m0), [whole(ph)], [(hoff, m0, m1)], m1 - m0)
+            cp("c1_" + t, C(hoff, m0, m1), P(ph, 0, m1 - m0), [PB(ph)], [(hoff, m0, m1)], m1 - m0)
             if eng("hk_" + t, "A") == "A":
-                ac("hk_" + t, C("hk", m0, m1), C(ph, 0, m1 - m0), AF.Identity, [whole(ph)], [("hk", m0, m1)], m1 - m0, bias=K(FLAG[r]))
+                ac("hk_" + t, C("hk", m0, m1), P(ph, 0, m1 - m0), AF.Identity, [PB(ph)], [("hk", m0, m1)], m1 - m0, bias=K(FLAG[r]))
             else:
                 ts("hk_" + t, C("hk", m0, m1), C(hoff, m0, m1), K(FLAG[r]), None, A.add, None, [(hoff, m0, m1)], [("hk", m0, m1)], m1 - m0)
         cb = chunks("cb", r)
-        for c, (c0, c1) in enumerate(cb):
-            t = "%d_%d" % (r, c)
+        for c0, c1 in cb:
+            t = "%d_%d" % (r, c0 // 128)
             m0, m1 = c0 // 16, c1 // 16
             n = m1 - m0
-            fl = int(eng("fl_" + t, "0"))
-            form = []
-            for k, (lo, hi) in enumerate(cuts("n2_" + t, c0, c1)):
-                e = eng("g2_%s_%d" % (t, k), "A")
-                form += ["V" if e == "V" else "A"] * ((hi - lo + HF - 1) // HF)
-                if e != "V":
-                    gather("g2_%s_%d" % (t, k), e, "de", lo, hi, x, NW, hoff, [(x, 0, NW)])
-                else:
-                    gtt("g2_%s_%d" % (t, k), "de", x, NW, hoff, x, lo, hi, NW + lo, A.subtract)
-            abs_, bts = cuts("na_" + t, c0, c1, fl, form), cuts("nb_" + t, c0, c1, fl)
+            sub = {}
+            for lo, hi, e in calls2(r):
+                if c0 <= lo < c1:
+                    for a in range(lo, hi, HF):
+                        sub[a] = e == "S"
+                    if e != "S":
+                        gather("g2_%d_%d" % (r, lo // 128), e, "de", lo, hi, x, NW, hoff, [(x, 0, NW)])
+                    else:
+                        for a, b, lb in runs(r, lo, hi) if r else [(lo, hi, "d0")]:
+                            gtt("g2_%d_%d" % (r, a // 128), "de", a, x, NW, hoff, lb, a, b, A.subtract)
+            for lo, hi in groups("na_" + t, c0, c1, sub):
+                u = "%d_%d" % (r, lo // 128)
+                if sub[lo]:
+                    ac("ab_" + u, C("ab", lo, hi), C("de", lo, hi), AF.Abs, [("de", lo, hi)], [("ab", lo, hi)], hi - lo, scale=0.5 ** r,
+                       bias=K(-0.5) if r else 0.0)
+                    continue
+                for a in range(lo, hi, HF):
+                    two("me_%d_%d" % (r, a // 128), "@e" + u, a - lo, "eye", "eyen", "de", a, min(hi, a + HF), x)
+                ac("ab_" + u, C("ab", lo, hi), P("@e" + u, 0, hi - lo), AF.Abs, [PB("@e" + u, 0, hi - lo)], [("ab", lo, hi)], hi - lo, scale=0.5 ** r)
             spans = []
-            for p0_ in range(c0 - fl * HF, c1, 2 * HF):
-                for k, (lo, hi) in enumerate(cuts("pieces", c0, c1)):
-                    if p0_ <= lo < p0_ + 2 * HF:
-                        two("ms_%s_%d" % (t, k), "ps", place(lo, c0, fl), "am", "am" if form[k] == "A" else "am2", "de", lo, hi, x)
-                        if form[k] == "A":
-                            two("me_%s_%d" % (t, k), "pq", place(lo, c0, fl), "eye", "eyen", "de", lo, hi, x)
-                for k, (lo, hi) in enumerate(abs_):
-                    if p0_ <= lo < p0_ + 2 * HF:
-                        a = place(lo, c0, fl)
-                        if form[(lo - c0) // HF] == "A":
-                            ac("ab_%s_%d" % (t, k), C("ab", lo, hi), C("pq", a, a + hi - lo), AF.Abs, [banks("pq", a, hi - lo)], [("ab", lo, hi)], hi - lo)
-                        else:
-                            ac("ab_%s_%d" % (t, k), C("ab", lo, hi), C("de", lo, hi), AF.Abs, [("de", lo, hi)], [("ab", lo, hi)], hi - lo)
-                for k, (lo, hi) in enumerate(bts):
-                    if p0_ <= lo < p0_ + 2 * HF:
-                        nm, a = "bt_%s_%d" % (t, k), place(lo, c0, fl)
-                        e, rd = eng(nm, "A"), banks("ps", a, hi - lo)
-                        if spans and spans[-1][2] == e:
-                            spans[-1][1] = hi // 16
-                        else:
-                            spans.append([lo // 16, hi // 16, e])
-                        if e == "A":
-                            ac(nm, C("bits", lo, hi), C("ps", a, a + hi - lo), AF.Sign, [rd, whole(nb)], [("bits", lo, hi)], hi - lo, bias=C(nb, 0, 1))
-                        else:
-                            ts(nm, C("bits", lo, hi), C("ps", a, a + hi - lo), C(thr, 0, 1), K(2.0), A.is_gt, A.mult, [rd, whole(thr)],
-                               [("bits", lo, hi)], hi - lo)
-            wrap("w2_" + t, "pc", "z2", "bits", c0, c1, False)
-            for j, (a, b, e) in enumerate(spans):
-                ts("c2_%s_%d" % (t, j), C(coff, a, b), C("pc", a - m0, b - m0), K(0.125), K(1023.5 if e == "A" else 0.0), A.mult, A.add,
-                   [whole("pc")], [(coff, a, b)], b - a)
-            for k, (lo, hi) in enumerate(cuts("n3_" + t, c0, c1)):
-                gtt("g3_%s_%d" % (t, k), "vi", "clrs", 2048, coff, "ab", lo, hi, lo, A.is_lt)
-            wrap("w3_" + t, "pd", "z3", "vi", c0, c1, True)
-            tt("p1_" + t, C(pp, m0, m1), C("pd", 0, n), C(p, m0, m1), A.max, [whole("pd"), (p, m0, m1)], [(pp, m0, m1)], n)
+            for lo, hi in groups("nb_" + t, c0, c1, sub):
+                u = "%d_%d" % (r, lo // 128)
+                for a in range(lo, hi, HF):
+                    two("ms_%d_%d" % (r, a // 128), "@s" + u, a - lo, "am", "am2" if sub[lo] else "am", "de", a, min(hi, a + HF), x)
+                nm = "bt_" + u
+                e, rd = eng(nm, "A"), PB("@s" + u, 0, hi - lo)
+                sx = "s" if sub[lo] and r else ""
+                thr, nb = "thr%d%s" % (r, sx), "nb%d%s" % (min(r, 1), sx)
+                need |= {nb if e == "A" else thr, "am2" if sub[lo] else "am"}
+                if spans and spans[-1][2] == e:
+                    spans[-1][1] = hi // 16
+                else:
+                    spans.append([lo // 16, hi // 16, e])
+                if e == "A":
+                    ac(nm, C("bits", lo, hi), P("@s" + u, 0, hi - lo), AF.Sign, [rd, whole(nb)], [("bits", lo, hi)], hi - lo, bias=C(nb, 0, 1),
+                       scale=0.5 if last else 1.0)
+                else:
+                    ts(nm, C("bits", lo, hi), P("@s" + u, 0, hi - lo), C(thr, 0, 1), K(2.0), A.is_gt, A.mult, [rd, whole(thr)],
+                       [("bits", lo, hi)], hi - lo)
+            wrap("w2_" + t, "@w2_" + t, "z2", "bits", c0, c1, False)
+            for a, b, e in spans:
+                ts("c2_%d_%d" % (r, a // 8), C(coff, a, b), P("@w2_" + t, a - m0, b - m0), K(0.125), K(1023.5 if e == "A" else 0.0), A.mult, A.add,
+                   [PB("@w2_" + t)], [(coff, a, b)], b - a)
+            for lo, hi in cuts("n3_" + t, c0, c1):
+                gtt("g3_%d_%d" % (r, lo // 128), "vi", lo, "clrs", 2048, coff, "ab", lo, hi, A.is_lt)
+            wrap("w3_" + t, "@w3_" + t, "z3", "vi", c0, c1, True)
+            tt("p1_" + t, C(pp, m0, m1), P("@w3_" + t, 0, n), C(p, m0, m1), A.max, [PB("@w3_" + t), (p, m0, m1)], [(pp, m0, m1)], n)
         for tag in ("cs", "cq", "cp"):
-            ends = [b // 16 for c, (a, b) in enumerate(cb) if b == V or eng("%s_%d_%d" % (tag, r, c), "1") == "1"]
+            ends = [b // 16 for a, b in cb if b == V or eng("%s_%d_%d" % (tag, r, a // 128), "1") == "1"]
             for c, (m0, m1) in enumerate(zip([0] + ends[:-1], ends)):
-                t, n = "%d_%d" % (r, m1), m1 - m0
+                t, n = "%d_%d" % (r, m1 // 8), m1 - m0
                 if tag == "cs":
                     tt("p2_" + t, C(sf, m0, m1), C(pp, m0, m1), C(vd, m0, m1), A.min, [(pp, m0, m1), (vd, m0, m1)], [(sf, m0, m1)], 2 * n)
                     ts("p4_" + t, C(sg, m0, m1), C(sf, m0, m1), K(4095), None, A.bitwise_and, None, [(sf, m0, m1)], [(sg, m0, m1)], n)
@@ -368,19 +388,18 @@ def build(g, T, topo, core, cfg):
                         ts("q5_" + t, C(pn, m0, m1), C(pp, m0, m1), K(4095), None, A.bitwise_and, None, [(pp, m0, m1)], [(pn, m0, m1)], n)
                         cp("o_" + t, C("po", m0, m1), C(pn, m0, m1), [(pn, m0, m1)], [("po", m0, m1)], n)
                     else:
-                        ph, dg = ("pa", "pz")[c % 2], "dg%d" % r
-                        sb = "sb%d" % r
+                        ph, dg, sb = "@pm_" + t, "dg%d" % r, "sb%d" % r
 
                         def perm(ph=ph, dg=dg, sb=sb, m0=m0, m1=m1):
                             a = max(m0, 8)
                             for j in range(2 if m0 == 0 else 0):
-                                pe.matmul(T[ph][:, 0:8], T[("eyes", "eyeb")[j]][:], T[sb][:, s, j, :], j == 0, j == 1)
+                                pe.matmul(P(ph, 0, 8)(), T[("eyes", "eyeb")[j]][:], T[sb][:, s, j, :], j == 0, j == 1)
                             for j in range(2):
-                                ins = pe.matmul(T[ph][:, a - m0:m1 - m0], T[("eyes", "eyeb")[j]][:], T[dg][:, j, 56 + a:56 + m1], j == 0, j == 1)
+                                ins = pe.matmul(P(ph, a - m0, m1 - m0)(), T[("eyes", "eyeb")[j]][:], T[dg][:, j, 56 + a:56 + m1], j == 0, j == 1)
                             return ins
                         op("pm_" + t, "P", perm, [(dg + "o", m0, m1), whole("eyes"), whole("eyeb")] + ([(sb, 16 * s, 16 * s + 16)] if m0 == 0 else []),
-                           [whole(ph)], ("p", 2 * max(64, n) + (128 if m0 == 0 else 0)))
-                        cp("q4_" + t, C("idx%d" % (r + 1), m0, m1), C(ph, 0, n), [whole(ph)], [("idx%d" % (r + 1), m0, m1)], n)
+                           [PB(ph)], ("p", 2 * max(64, n) + (128 if m0 == 0 else 0)))
+                        cp("q4_" + t, C("idx%d" % (r + 1), m0, m1), P(ph, 0, n), [PB(ph)], [("idx%d" % (r + 1), m0, m1)], n)
                 elif not last:
                     dg, sb = "dg%d" % r, "sb%d" % r
                     for j, bitmask in enumerate((0xFF0, 15)):
@@ -390,62 +409,69 @@ def build(g, T, topo, core, cfg):
                     if c == 0:
                         ow = [(sb, 16 * s, 16 * s + 16)]
                         cp("q0_" + t, lambda sb=sb: T[sb][:, s, :, :], lambda: T.hl[:, :, 0:8], hr, ow, 16)
-                        send(["t%d" % (r + 1)], [lambda sb=sb: T[sb][:, s, :, :]], ow, [others(sb, 16)], 4096)
+                        send("t%d" % (r + 1), lambda sb=sb: T[sb][:, s, :, :], ow, sb, 16, 4096, every)
                     m0 = max(m0, 8)
                     cp("q3_" + t, lambda dg=dg, m0=m0, m1=m1: T[dg][:, :, 56 + m0:56 + m1], lambda m0=m0, m1=m1: T.hl[:, :, m0:m1], hr,
                        [(dg + "o", m0, m1)], 2 * n)
         if not last:
             dg, sb = "dg%d" % r, "sb%d" % r
             for j in range(2):
-                ac("u%d_%d" % (j, r), D(dg, j, 0, 64), lambda sb=sb, j=j: T[sb][:, :, j, :], AF.Identity, [whole(sb)], [(dg, j, j + 1)], 64)
+                nm, src = "u%d_%d" % (j, r), lambda sb=sb, j=j: T[sb][:, :, j, :]
+                if eng(nm, "A") == "A":
+                    ac(nm, D(dg, j, 0, 64), src, AF.Identity, [whole(sb)], [(dg, j, j + 1)], 64)
+                elif eng(nm, "A") == "V":
+                    cp(nm, D(dg, j, 0, 64), src, [whole(sb)], [(dg, j, j + 1)], 32)
+                else:
+                    op(nm, "G", lambda dg=dg, j=j, src=src: g.affine_select(T[dg][:, j, 0:64], src(), [[0, 64]], A.is_ge, 0.0, 0, 0),
+                       [whole(sb)], [(dg, j, j + 1)], ("g", 88))
                 dma("tab%d_%d" % (j, r), "S", lambda j=j: T.tab[j:128:16, :], D(dg, j, 0, TW), [(dg, j, j + 1), (dg + "o", 0, 192)],
                     [("tabr%d" % j, 0, 2)], 63488)
         else:
             dma("syp", "S", lambda: T.yp[:], W("po"), [whole("po")], [], 98304)
-        for c, (c0, c1) in enumerate(cb):
-            cs = cuts4(r, c, c0, c1)
-            fl = int(eng("fm_%d_%d" % (r, c), "0"))
-            for k, (lo, hi) in enumerate(cs):
-                t = "%d_%d_%d" % (r, c, k)
-                e, n = eng("hv_" + t, "V"), hi - lo
-                magic = False
-                if eng("g4_" + t, "V") == "A":
-                    magic = last and e == "V"
-                    a = place(lo, c0, fl)
-                    gather("g4_" + t, "A", "bg", lo, hi, x, NW, sel, [(x, 0, NW)])
-                    two("m4_" + t, "pq", a, "eyeg" if magic else "eye", "eyeh" if magic else "eye", "bg", lo, hi, x)
-                    sb, rd, cyc = "pq", banks("pq", a, n), n
+        for lo, hi in zip(four[r][:-1], four[r][1:]):
+            t = "%d_%d" % (r, lo // 128)
+            e, n = eng("hv_" + t, "V"), hi - lo
+            ob, o0 = ("yo", lo) if last else (xn, own(lo, hi)[0][2])
+            if eng("g4_" + t, "V") == "A":
+                pq = "@m" + t
+                gather("g4_" + t, "A", "bg", lo, hi, x, NW, sel, [(x, 0, NW)])
+                two("m4_" + t, pq, 0, "eyeg" if last else "eye", "eyeh" if last else "eye", "bg", lo, hi, x, last and e == "A")
+                if e == "A":
+                    ac("hv_" + t, C(ob, o0, o0 + n), P(pq, 0, n), AF.Identity, [PB(pq, 0, n)], [(ob, o0, o0 + n)], n, bias=K(-128.0 if last else LOW[r]))
+                elif last:
+                    ts("hv_" + t, C(ob, o0, o0 + n), P(pq, 0, n), K(MAGIC), K(MAGIC + 128.0), A.add, A.subtract, [PB(pq, 0, n)], [(ob, o0, o0 + n)], n)
                 else:
-                    sb = "sbf" if r == 0 else ("s32" if e == "A" else "s16")
-                    gtt("g4_" + t, sb, x, NW, sel, x, lo, hi, NW + lo, A.add)
-                    a, rd, cyc = lo, (sb, lo, hi), n // 2
-                bias = 127.875 if r == 0 else -0.125
-                ob, o0 = ("y3", lo) if last else (xn, own(lo, hi)[0][2])
-                if magic:
-                    ts("hv_" + t, C("yo", lo, hi), C(sb, a, a + n), K(MAGIC), K(MAGIC + 128.0), A.add, A.subtract, [rd], [("yo", lo, hi)], n)
-                elif e == "A":
-                    ac("hv_" + t, C(ob, o0, o0 + n), C(sb, a, a + n), AF.Identity, [rd], [(ob, o0, o0 + n)], n, bias=K(bias), scale=0.5)
-                else:
-                    ts("hv_" + t, C(ob, o0, o0 + n), C(sb, a, a + n), K(0.5), K(bias), A.mult, A.add, [rd], [(ob, o0, o0 + n)], cyc)
-                if last:
-                    if magic:
-                        pass
-                    elif eng("hz_" + t, "V") == "A":
-                        ac("hz_" + t, C("yo", lo, hi), C("y3", lo, hi), AF.Identity, [("y3", lo, hi)], [("yo", lo, hi)], n, bias=K(-128.0))
-                    else:
-                        ts("hz_" + t, C("yo", lo, hi), C("y3", lo, hi), K(-128.0), None, A.add, None, [("y3", lo, hi)], [("yo", lo, hi)], n // 2)
-                    if (c, k) != (0, 0):
-                        l2 = 0 if lo == B else lo
-                        dma("syq_%d_%d" % (c, k), "S", lambda l2=l2, hi=hi: T.yq[:, l2:hi], C("yo", l2, hi), [("yo", l2, hi)], [], 256 * (hi - l2))
-                elif c == 0 and k == 0:
-                    send(["x%d" % (r + 1)], [C(xn, b0, b1)], [(xn, b0, b1)], [others(xn, B)], 32768)
-            if not last:
-                for k, (a, b, w) in enumerate(own(c0, c1)):
-                    h = copied(r + 1, a, b)
-                    if h:
-                        dma("dup_%d_%d" % (r, 4 if a == 0 else c), "S", C(xn, NW + h[0], NW + h[1]), C(xn, w + h[0] - a, w + h[1] - a),
-                            [(xn, w + h[0] - a, w + h[1] - a)], [(xn, NW + h[0], NW + h[1])], 256 * (h[1] - h[0]))
-    return ops
+                    ts("hv_" + t, C(ob, o0, o0 + n), P(pq, 0, n), K(LOW[r]), None, A.add, None, [PB(pq, 0, n)], [(ob, o0, o0 + n)], n)
+            else:
+                for a, b, lb in runs(r, lo, hi):
+                    gtt("g4_%d_%d" % (r, a // 128), "y3" if last else ob, o0 + a - lo, x, NW, sel, lb, a, b, A.add)
+                if last and e == "A":
+                    ac("hv_" + t, C("yo", lo, hi), C("y3", lo, hi), AF.Identity, [("y3", lo, hi)], [("yo", lo, hi)], n, bias=K(-128.0), scale=0.125)
+                elif last:
+                    ts("hv_" + t, C("yo", lo, hi), C("y3", lo, hi), K(0.125), K(-128.0), A.mult, A.add, [("y3", lo, hi)], [("yo", lo, hi)], n // 2)
+            if last:
+                dma("syq_%d" % (lo // 128), "S", lambda lo=lo, hi=hi: T.yq[:, lo:hi], C("yo", lo, hi), [("yo", lo, hi)], [], 256 * n)
+            elif lo == 0:
+                send("x%d" % (r + 1), C(xn, b0, b1), [(xn, b0, b1)], xn, B, 32768, every)
+    rounds = ops[late:]
+    del ops[late:]
+    if "am2" in need:
+        ac("c_am2", W("am2"), W("am"), AF.Identity, [whole("am")], [whole("am2")], 128, scale=2.0)
+    if "thr0" in need:
+        cp("c_thr0", C("thr0", 0, 1), C("thi", 0, 1), [whole("thi")], [whole("thr0")], 1)
+    if "nb0" in need:
+        ts("c_nb0", C("nb0", 0, 1), C("thi", 0, 1), K(-1.0), K(-0.5), A.mult, A.add, [whole("thi")], [whole("nb0")], 1)
+    ts("c_th2", C("th2", 0, 1), C("thi", 0, 1), K(2.0), None, A.mult, None, [whole("thi")], [whole("th2")], 1)
+    mm("c_cs", "@c", 1, [("am", C("c32", 0, 1))], [whole("c32")], 64)
+    for sx, f in (("", 16.0), ("s", 513.0 / 32)):
+        t1 = "thr1" + sx
+        if need & {t1, "thr2" + sx, "nb1" + sx}:
+            ts("c_" + t1, C(t1, 0, 1), P("@c", 0, 1), K(f), C("th2", 0, 1), A.mult, A.add, [PB("@c"), whole("th2")], [whole(t1)], 1)
+        if "thr2" + sx in need:
+            ts("c_thr2" + sx, C("thr2" + sx, 0, 1), C(t1, 0, 1), K(2.0), None, A.mult, None, [whole(t1)], [whole("thr2" + sx)], 1)
+        if "nb1" + sx in need:
+            ts("c_nb1" + sx, C("nb1" + sx, 0, 1), C(t1, 0, 1), K(-1.0), K(-0.25), A.mult, A.add, [whole(t1)], [whole("nb1" + sx)], 1)
+    return ops + rounds
 
 
 def hazards(ops):
@@ -456,9 +482,8 @@ def hazards(ops):
         d = {"m_pb"} if name == "lpb1" else set()
         acc = [(a, False) for a in o[3]] + [(a, True) for a in o[4]]
         for (b, lo, hi), w in acc:
-            bank = b in SCRATCH and SCRATCH[b][0] == "psum"
             for (n2, q2, l2, h2, w2) in seen.get(b, []):
-                if l2 < hi and lo < h2 and (w or w2 or (bank and q2 != q)):
+                if l2 < hi and lo < h2 and (w or w2 or (b[0] == "@" and q2 != q)):
                     d.add(n2)
         for (b, lo, hi), w in acc:
             seen.setdefault(b, []).append((name, q, lo, hi, w))
@@ -466,15 +491,39 @@ def hazards(ops):
     return deps
 
 
+def pieces(ops):
+    al = {}
+    for o in ops:
+        for b, lo, hi in o[3] + o[4]:
+            if b[0] == "@":
+                n, us = al.get(b, (0, []))
+                al[b] = (max(n, hi // HF), us if o[0] in us else us + [o[0]])
+    return al
+
+
+def allocate(al, order, deps, bank):
+    pos = {n: i for i, n in enumerate(order)}
+    held = [(-1, [])] * 8
+    for b in sorted(al, key=lambda a: min(pos[n] for n in al[a][1])):
+        n, us = al[b]
+        k = min(range(9 - n), key=lambda j: max(h[0] for h in held[j:j + n]))
+        for j in range(k, k + n):
+            for u in us:
+                deps[u] = deps[u] | set(held[j][1])
+            held[j] = (max(pos[u] for u in us), us)
+        bank[b] = k
+
+
 def rank_program(g, core, T, topo):
     if T.rank_of(core) is None:
         return
-    ops = build(g, T, topo, core, CFG)
+    bank = {}
+    ops = build(g, T, topo, core, CFG, bank)
     deps = hazards(ops)
     byname = {o[0]: o for o in ops}
     order = [ops[i][0] for i in ORDER]
+    allocate(pieces(ops), order, deps, bank)
     queue = {"A": g.scalar, "V": g.vector, "P": g.tensor, "S": g.sync, "G": g}
-    npeer = len(T.cores) - 1
     kind = {n: byname[n][5][0] for n in order}
     pos = {n: i for i, n in enumerate(order)}
 
@@ -489,7 +538,7 @@ def rank_program(g, core, T, topo):
             continue
         waits[n] = []
         for d in sorted(deps[n], key=lambda a: -pos[a]):
-            if d not in known[q]:
+            if d not in known[q] and (q != "P" or byname[d][1] != "P"):
                 waits[n].append(d)
                 known[q] |= after[d]
         after[n] = known[q] | {n}
@@ -506,7 +555,7 @@ def rank_program(g, core, T, topo):
         o = byname[n]
         q = o[1]
         if q == "R":
-            mark[n] = (n, mark[o[2]][2] * npeer)
+            mark[n] = (n, mark[o[2]][2])
             continue
         for d in waits[n]:
             queue[q].wait_ge(T.sem[mark[d][0]], mark[d][1])

from concourse.bass import DstId, RemoteDMATransfer
from concourse.mybir import AluOpType, AxisListType, ActivationFunctionType

V, B, RO = 3072, 128, 3
M, NW, HF = 1024, 3968, 512
TW = NW // 16
BIG = 65536.0
FLAG = (8192.0, 16384.0, 32768.0)
MAGIC = 1.5 * 2 ** 23
LOW = (255.5, -1.0, -2.0)

SCRATCH = {"tab": ("sbuf", [128, NW], "bfloat16"), "clrs": ("sbuf", [128, 2048], "bfloat16"),
           "c32": ("sbuf", [128, 64], "bfloat16"), "ieye": ("sbuf", [128, 128], "float32"), "eyef": ("sbuf", [128, 128], "float32"),
           "pb": ("sbuf", [128, 128], "int32"), "cmg": ("sbuf", [128, HF], "bfloat16"),
           "hl": ("sbuf", [128, 2, 192], "int32"), "di": ("sbuf", [128, 2, 192], "bfloat16"),
           "ps": ("psum", [128, 8 * HF], "float32")}
for _names, _w, _t in (("am am2 eye eyen eyes eyeb eye8 eyeu eyeh eyeg pbt", 128, "bfloat16"), ("z1 z2 z3", 144, "bfloat16"),
                       ("i16 i16b", 16, "int32"), ("msk two pw pwm", 16, "float32"), ("blk blks", 8, "int32"),
                       ("w1 w2 kf thr0 thr1 thr2 thr1s thr2s th2 nb0 nb1 nb1s", 4, "float32"), ("ki kj thi", 4, "int32"),
                       ("vd0 vd vd1 vd2 td p0 p3 pp0 pp1 pp2 sf0 sf1 sf2 sg0 sg1 sg2", 192, "int32"),
                       ("te tf tg", 192, "bfloat16"), ("po hk", 192, "float32"),
                       ("hg de bits ab vi bg y3 yo d0", V, "bfloat16"), ("x0 x1 x2", NW, "bfloat16"),
                       ("lV0 lV1 lV2", V, "float16"), ("lA0 lA1 lA2", V, "float32")):
    for _n in _names.split():
        SCRATCH[_n] = ("sbuf", [128, _w], _t)
for _r in range(RO):
    for _n in ("idx", "hoff", "coff", "sel"):
        SCRATCH["%s%d" % (_n, _r)] = ("sbuf", [128, 192], "uint16")
for _r in range(RO - 1):
    SCRATCH["sb%d" % _r] = ("sbuf", [128, 8, 2, 8], "bfloat16")
    SCRATCH["dg%d" % _r] = ("sbuf", [128, 2, 256], "bfloat16")

DMAS = ["lpb0", "lpb1", "lpar", "lqb", "lq0", "lq1", "lq2", "lam", "lth", "lclr", "ltab0", "ltab1", "syp"]
for _r in range(RO - 1):
    DMAS += ["tab0_%d" % _r, "tab1_%d" % _r]
DMAS += ["syq_%d" % _k for _k in range(24)]
SENDS = ["xa", "t0", "x0", "t1", "x1", "t2", "x2"]
SEMAPHORES = ["qA", "qV", "qP", "qG"] + DMAS + ["arr_" + _s for _s in SENDS] + ["out_" + _s for _s in SENDS]

CFGS = """
Qlclr=A Qlq1=A Qlq2=A Qsyq_16=A Wlclr=t0 Wlq2=xa bt_0_0=V bt_0_8=V bt_1_0=V bt_1_12=V bt_1_4=V bt_2_0=V bt_2_12=V bt_2_4=V c40=1,4,8,12,16,20 c41=1,4,8,12,16,20 c42=4,8,12,16,20 c_eye8=V c_eyeb=V cp_0_0=0 cp_0_8=0 cp_1_0=0 cp_1_8=0 cp_2_0=0 cq_0_8=0 cq_1_8=0 dc_0_12=A dc_0_20=A dc_0_4=A em4_0_1=1 em4_1_1=1 em4_1_16=1 em4_1_8=1 em4_2_16=1 eme_0_8=1 eme_1_16=1 eme_1_8=1 eme_2_8=1 ems_0_12=1 ems_0_16=1 ems_0_20=1 ems_0_4=1 ems_1_12=1 ems_1_16=1 ems_1_20=1 ems_1_4=1 ems_1_8=1 ems_2_12=1 ems_2_16=1 ems_2_4=1 ems_2_8=1 g1_0_0=V g1_0_20=V g1_1_20=V g1_1_4=V g1_2_20=V g1_2_4=V g2_0_12=S g2_0_20=S g2_0_4=S g2_1_12=S g2_1_20=S g2_1_4=S g2_2_12=S g2_2_20=S g2_2_4=S g4_0_1=A g4_0_16=A g4_0_4=A g4_0_8=A g4_1_1=A g4_1_16=A g4_1_8=A g4_2_0=A g4_2_16=A g4_2_8=A hk_0_8=V hk_2_8=V hv_0_1=A hv_0_4=A hv_0_8=A hv_1_1=A hv_1_16=A hv_1_8=A hv_2_0=A hv_2_20=A hv_2_4=A lw_1_0=A lw_1_12=A lw_1_4=A n1_0_0=1 n1_0_8=1 n1_1_8=1 n1_2_8=1 n3_1_0=1 n3_1_16=1 n3_2_0=1 n3_2_16=1 u0_1=V u1_0=G
"""
ORDERS = """
4 3 9 7 10 8 0 42 15 45 63 13 40 51 28 43 14 29 2 5 1 25 6 24 54 30 20 16 64 17 36 31 34 52 46 56 44 38 32 12 18 60 70 35 71 41 82 37 57 79 33 68 22 11 53 26 23 19 21 65 69 47 50 39 118 61 105 72 124 67 49 48 66 62 80 89 27 93 85 94 86 90 95 87 76 99 106 91 84 117 96 88 98 103 81 116 104 100 107 125 101 126 122 108 136 123 109 92 110 111 127 113 119 143 144 140 129 102 112 121 135 120 145 114 141 142 97 139 132 137 138 131 115 163 162 153 128 164 146 181 154 130 155 55 147 177 165 184 178 179 166 180 133 150 185 182 149 148 151 134 156 73 157 167 152 158 159 168 169 75 160 78 175 186 183 196 173 170 161 83 174 176 187 191 188 171 190 189 197 172 199 204 194 192 200 193 235 220 238 201 255 209 202 74 205 198 214 208 213 210 221 218 203 206 77 230 222 211 219 250 215 258 239 223 229 217 216 234 236 224 240 225 231 237 195 212 259 232 233 241 251 226 227 242 244 249 260 207 256 257 252 305 261 295 300 246 254 253 228 243 277 276 267 278 268 245 269 279 294 296 247 59 58 297 264 262 291 263 248 281 270 265 292 271 266 272 273 282 283 274 280 293 284 287 275 299 289 288 290 301 285 303 298 286 308 313 322 304 306 302 307 312 317 348 314 333 318 351 315 309 326 310 327 319 311 331 334 321 323 343 335 324 332 316 342 330 347 328 349 352 336 329 350 362 363 337 353 344 345 370 338 371 346 339 354 367 356 368 369 366 340 358 341 355 378 357 364 372 365 379 373 320 380 325 392 359 375 360 374 361 396 376 407 393 381 387 377 382 388 389 384 383 390 385 403 397 398 391 399 394 386 404 411 405 395 406 400 408 401 409 412 402 413 410
"""
CFG = dict(_a.split("=") for _a in CFGS.split())
ORDER = [int(_a) for _a in ORDERS.split()]


def build(g, T, topo, core, cfg, bank):
    A, AF, X = AluOpType, ActivationFunctionType, AxisListType.X
    s = T.rank_of(core)
    ops = []
    vec, act, pe = g.vector, g.scalar, g.tensor
    eng = cfg.get
    b0, b1 = s * B, s * B + B

    def op(name, q, fn, rd, wr, cost):
        ops.append((name, q, fn, rd, wr, cost))

    def whole(n):
        w = 1
        for d in SCRATCH[n][1][1:]:
            w *= d
        return (n, 0, w)

    def dma(name, q, out, in_, rd, wr, nbytes):
        q = eng("Q" + name, q)
        e = g.sync if q == "S" else g.scalar
        if eng("W" + name, "0") != "0":
            rd = rd + [("tok_" + cfg["W" + name], 0, 1)]
        op(name, q, lambda: e.dma_start(out(), in_()), rd, wr, ("dma", nbytes))

    def ts(name, out, in0, s1, s2, o0, o1, rd, wr, n):
        if o1 is None:
            op(name, "V", lambda: vec.tensor_scalar(out(), in0(), s1(), None, o0), rd, wr, ("v", n))
        else:
            op(name, "V", lambda: vec.tensor_scalar(out(), in0(), s1(), s2(), o0, o1), rd, wr, ("v", n))

    def tt(name, out, in0, in1, o, rd, wr, n):
        op(name, "V", lambda: vec.tensor_tensor(out(), in0(), in1(), o), rd, wr, ("v", n))

    def cp(name, out, in_, rd, wr, n):
        op(name, "V", lambda: vec.tensor_copy(out(), in_()), rd, wr, ("v", n))

    def ms(name, buf, lo, hi, val, n):
        op(name, "V", lambda: vec.memset(T[buf][:, lo:hi], val), [], [(buf, lo, hi)], ("v", n))

    def ac(name, out, in_, f, rd, wr, n, bias=0.0, scale=1.0):
        op(name, "A", lambda: act.activation(out(), in_(), f, bias=bias() if bias else 0.0, scale=scale), rd, wr, ("a", n))

    def W(n):
        return lambda: T[n][:]

    def C(n, lo, hi):
        return lambda: T[n][:, lo:hi]

    def P(n, lo, hi):
        return lambda: T.ps[:, bank[n] * HF + lo:bank[n] * HF + hi]

    def PB(n, lo=0, hi=1):
        return (n, lo // HF * HF, ((hi - 1) // HF + 1) * HF)

    def D(n, j, lo, hi):
        return lambda: T[n][:, j, lo:hi]

    def K(v):
        return lambda: v

    def tsw(name, out, in0, s1, s2, o0, o1):
        ts(name, W(out), W(in0), K(s1), K(s2), o0, o1, [whole(in0)], [whole(out)], whole(out)[2])

    def own(lo, hi):
        return [(a, b, a + (b0 if a < B else M - B)) for a, b in ((lo, min(hi, B)), (max(lo, B), hi)) if a < b]

    def ownr(x, lo, hi):
        return [(x, w, w + b - a) for a, b, w in own(lo, hi)]

    def send(t, ap, rd, buf, w, nbytes, steps):
        n = len(T.cores)
        to = [T.cores[(s + k) % n] for k in steps]

        def fn():
            es = [e for e in topo.engines(core, to[0]) if all(e in topo.engines(core, c) for c in to)]
            ids = [DstId(rid=topo.addr(c)[0], pnc=topo.addr(c)[1]) for c in to]
            g.remote_dma_fused([RemoteDMATransfer(dst_ids=ids, dma_engine_mask=sum(1 << e for e in es), remote_sem=T.sem["arr_" + t],
                                                  src=ap(), dsts=[ap() for c in to])], local_sem=T.sem["out_" + t])
            return (len(es), len(es) * len(to))
        op("snd_" + t, "G", fn, rd, [("tok_" + t, 0, 1)], ("send", nbytes, len(to)))
        op("arr_" + t, "R", "snd_" + t, [("tok_" + t, 0, 1)], [(buf, (s - k) % n * w, (s - k) % n * w + w) for k in steps], ("arr", 1))

    def mm(name, pn, n, terms, rd, cyc):
        def fn():
            for k, (l, r_) in enumerate(terms):
                ins = pe.matmul(P(pn, 0, n)(), T[l][:], r_(), k == 0, k == len(terms) - 1)
            return ins
        op(name, "P", fn, rd + [whole(l) for l, r_ in terms], [PB(pn)], ("p", cyc))

    ms("m_pb", "pb", 0, 128, 0, 128)
    dma("lpb0", "S", lambda: T.pb[0:128:16, :], lambda: T.par[:, 0:8], [], [("pb", 0, 128)], 4096)
    dma("lpb1", "A", lambda: T.pb[1:128:16, :], lambda: T.par[:, 0:8], [], [("pb1", 0, 128)], 4096)
    dma("lpar", "S", W("p0"), lambda: T.par[:], [], [whole("p0")], 98304)
    dma("lqb", "A", C("x0", b0, b1), lambda: T.q[:, 0:B], [], [("x0", b0, b1)], 32768)
    dma("lam", "A", W("am"), lambda: T.amat[:], [], [whole("am")], 32768)
    dma("lth", "A", C("thi", 0, 1), lambda: T.th[:], [], [whole("thi")], 512)
    op("g_i16", "G", lambda: g.iota(T.i16[:], [[1, 16]], 128, -1), [], [whole("i16")], ("g", 16))
    op("g_blk", "G", lambda: g.iota(T.blk[:], [[-16, 8]], 0, 1), [], [whole("blk")], ("g", 8))
    op("g_eye", "G", lambda: g.iota(T.ieye[:], [[1, 128]], 0, -1, allow_small_or_imprecise_dtypes=True), [], [whole("ieye")], ("g", 128))
    op("g_ki", "G", lambda: g.iota(T.ki[:, 0:1], [[1, 1]], 0, 1), [], [whole("ki")], ("g", 1))
    op("g_vb", "G", lambda: g.iota(T.vd0[:, 0:8], [[16, 8]], 4096 + b0, 0), [], [("vd0", 0, 8)], ("g", 8))
    op("g_vd", "G", lambda: g.iota(T.vd0[:, 8:192], [[16, 184]], 4096 + M, 0), [], [("vd0", 8, 192)], ("g", 184))
    tsw("c_i16", "i16b", "i16", 15, None, A.bitwise_and, None)
    tsw("c_msk", "msk", "i16b", 0.0, None, A.is_equal, None)
    ms("m_tab", "tab", M, NW, 0.0, (NW - M) // 2)
    pbr = [whole("pb"), ("pb1", 0, 128)]
    ts("b_t", W("pbt"), W("pb"), C("msk", 1, 2), None, A.mult, None, pbr + [whole("msk")], [whole("pbt")], 128)
    tt("b_d", C("tab", b0, b1), W("pb"), W("pbt"), A.subtract, pbr + [whole("pbt")], [("tab", b0, b1)], 256)
    trd = [("tab", b0, b1), ("tabr0", 0, 1), ("tabr1", 0, 1)]
    every, ka = range(1, len(T.cores)), int(eng("ka", "1"))
    send("t0", C("tab", b0, b1), trd, "tab", B, 32768, every)
    if ka:
        send("xa", C("x0", b0, b1), [("x0", b0, b1)], "x0", B, 32768, every[:ka])
    send("x0", C("x0", b0, b1), [("x0", b0, b1)], "x0", B, 32768, every[ka:])
    for c in range(3):
        lo, hi = max(B, c * 1024), (c + 1) * 1024
        dma("lq%d" % c, "S", C("x0", lo + M - B, hi + M - B), lambda lo=lo, hi=hi: T.q[:, lo:hi], [], ownr("x0", lo, hi), 256 * (hi - lo))
    dma("lclr", "S", W("clrs"), lambda: T.clr[:], [], [whole("clrs")], 524288)
    for j, bitmask in enumerate((0xFF0, 15)):
        ts("i_q%d" % j, D("hl", j, 0, 192), W("p0"), K(bitmask), None, A.bitwise_and, None, [whole("p0")], [("hl", 192 * j, 192 * j + 192)], 192)
        cp("i_d%d" % j, D("di", j, 0, 192), D("hl", j, 0, 192), [("hl", 192 * j, 192 * j + 192)], [("di", 192 * j, 192 * j + 192)], 192)
        dma("ltab%d" % j, "SA"[j], lambda j=j: T.tab[j:128:16, M:NW], D("di", j, 8, 192), [("di", 192 * j, 192 * j + 192), ("tab", M, NW)],
            [("tabr%d" % j, 1, 2)], 47104)
    tsw("i_s", "td", "p0", 7, None, A.arith_shift_right, None)
    tsw("i_s2", "te", "td", 8.0, 120.0, A.min, A.mult)
    ts("i_f", W("tf"), D("di", 0, 0, 192), K(float(M)), K(16.0), A.is_ge, A.mult, [("di", 0, 192)], [whole("tf")], 96)
    tt("i_u", W("tg"), W("tf"), D("di", 1, 0, 192), A.min, [whole("tf"), ("di", 192, 384)], [whole("tg")], 384)
    for z in ("z1", "z2", "z3"):
        ms("m_" + z, z, 0, 144, 0.0, 72)
    ms("m_c32", "c32", 0, 64, 32.0, 32)
    ms("m_two", "two", 0, 16, 2.0, 16)
    tsw("c_blk", "blks", "blk", 4, None, A.arith_shift_right, None)
    op("c_w1", "V", lambda: vec.tensor_reduce(T.w1[:, 0:1], T.msk[:, 0:2], X, A.add), [whole("msk")], [whole("w1")], ("v", 2))
    op("c_pw", "V", lambda: vec.tensor_tensor_scan(T.pw[:], T.two[:], T.two[:], 2.0, A.mult, A.max), [whole("two")], [whole("pw")], ("v", 16))
    tt("c_pwm", W("pwm"), W("pw"), W("msk"), A.mult, [whole("pw"), whole("msk")], [whole("pwm")], 32)
    op("c_w2", "V", lambda: vec.tensor_reduce(T.w2[:, 0:1], T.pwm[:, 0:11], X, A.add), [whole("pwm")], [whole("w2")], ("v", 11))
    for z, wt, rd in (("z1", C("w1", 0, 1), [whole("w1")]), ("z2", C("w2", 0, 1), [whole("w2")]), ("z3", K(-BIG), [])):
        ts("c_" + z, lambda z=z: T[z][:, 15:143:16], W("blks"), K(0.0), wt, A.is_equal, A.mult, [whole("blks")] + rd, [whole(z)], 8)
    tsw("c_eye", "eye", "ieye", 0.0, None, A.is_equal, None)
    tsw("c_eyef", "eyef", "ieye", 0.0, None, A.is_equal, None)
    four = [[128 * int(a) for a in ("0," + eng("c4%d" % r, ("1,8,16", "1,8,16", "8,16")[r]) + ",24").split(",")] for r in range(RO)]
    onA = [eng("hv_2_%d" % (lo // 128), "V") for lo in four[2][:-1] if eng("g4_2_%d" % (lo // 128), "V") == "A"]
    for n, sc in [("eyen", -1.0), ("eyes", 1.0 / 16), ("eyeb", float(TW)), ("eye8", 8.0), ("eyeu", 176.0)] + (
            [("eyeh", 0.125), ("eyeg", 255.0 / 2048)] if onA else []):
        if eng("c_" + n, "A") == "A":
            ac("c_" + n, W(n), W("eye"), AF.Identity, [whole("eye")], [whole(n)], 128, scale=sc)
        else:
            ts("c_" + n, W(n), W("eye"), K(sc), None, A.mult, None, [whole("eye")], [whole(n)], 64)
    if "A" in onA:
        ms("m_cmg", "cmg", 0, HF, MAGIC, HF // 2)
    mm("i_m", "@i", 192, [("eyes", D("di", 0, 0, 192)), ("eye8", D("di", 1, 0, 192)), ("eye", W("te")), ("eyeu", W("tg"))],
       [whole("di"), whole("te"), whole("tg")], 768)
    cp("i_idx", W("idx0"), P("@i", 0, 192), [PB("@i")], [whole("idx0")], 192)
    ts("c_kj", C("kj", 0, 1), C("ki", 0, 1), K(15), None, A.bitwise_and, None, [whole("ki")], [whole("kj")], 1)
    cp("c_kf", C("kf", 0, 1), C("kj", 0, 1), [whole("kj")], [whole("kf")], 1)
    ts("c_vd", W("vd"), W("vd0"), C("kf", 0, 1), None, A.add, None, [whole("vd0"), whole("kf")], [whole("vd")], 192)
    for r in (1, 2):
        tsw("c_vd%d" % r, "vd%d" % r, "vd", FLAG[r] - FLAG[0], None, A.add, None)
    late, need = len(ops), set()

    def wrap(name, pn, z, data, lo, hi, names):
        n = (hi - lo) // 16

        def fn():
            for i in range(16):
                ins = pe.matmul(P(pn, 0, n)(), T[z][:, 15 - i:143 - i], T[data][:, lo + i:hi:16], i == 0 and not names, i == 15)
            return ins
        if names:
            op("v1" + name[2:], "P", lambda: pe.matmul(P(pn, 0, n)(), T.eyef[:], T.hk[:, lo // 16:hi // 16], True, False),
               [whole("eyef"), ("hk", lo // 16, hi // 16)], [PB(pn)], ("p", 4 * max(64, n)))
        op(name, "P", fn, [whole(z), (data, lo, hi)], [PB(pn)], ("p", max(64, n) * 16))

    def gather(name, e, out, lo, hi, win, whi, off, rd):
        a, b = lo // 16, hi // 16
        if e == "A":
            op(name, "A", lambda: act.activation(T[out][:, lo:hi], T[win][:, 0:whi].indirect(T[off][:, a:b]), AF.Identity),
               rd + [(off, a, b)], [(out, lo, hi)], ("ga", hi - lo))
        else:
            op(name, "V", lambda: vec.tensor_copy(T[out][:, lo:hi], T[win][:, 0:whi].indirect(T[off][:, a:b])),
               rd + [(off, a, b)], [(out, lo, hi)], ("gv", hi - lo))

    def gtt(name, out, o0, win, whi, off, in1, lo, hi, o):
        op(name, "V", lambda: vec.tensor_tensor(T[out][:, o0:o0 + hi - lo], T[win][:, 0:whi].indirect(T[off][:, lo // 16:hi // 16]), T[in1][:, lo:hi], o),
           [(win, 0, whi), (off, lo // 16, hi // 16), (in1, lo, hi)], [(out, o0, o0 + hi - lo)], ("gt", hi - lo))

    def two(name, pn, o0, l0, l1, data, lo, hi, x, rnd=False):
        early = lo >= B and hi - lo <= HF and eng("e" + name, "0") == "1"
        if early:
            w0 = lo + M - B
            op("e" + name, "P", lambda: pe.matmul(P(pn, o0, o0 + hi - lo)(), T[l1][:], T[x][:, w0:w0 + hi - lo], True, False),
               [whole(l1)] + ownr(x, lo, hi), [PB(pn, o0, o0 + hi - lo)], ("p", hi - lo))

        def fn():
            for a, b, w in own(lo, hi):
                while a < b:
                    o = o0 + a - lo
                    n = min(b - a, HF - o % HF)
                    if not early:
                        pe.matmul(P(pn, o, o + n)(), T[l1][:], T[x][:, w:w + n], True, False)
                    ins = pe.matmul(P(pn, o, o + n)(), T[l0][:], T[data][:, a:a + n], False, not rnd)
                    if rnd:
                        pe.matmul(P(pn, o, o + n)(), T.eye[:], T.cmg[:, 0:n], False, False)
                        ins = pe.matmul(P(pn, o, o + n)(), T.eyen[:], T.cmg[:, 0:n], False, True)
                    a, w = a + n, w + n
            return ins
        op(name, "P", fn, [whole(l0), whole(l1), (data, lo, hi)] + ownr(x, lo, hi) + ([whole("cmg"), whole("eye"), whole("eyen")] if rnd else []),
           [PB(pn, o0, o0 + hi - lo)], ("p", (2 - early + 2 * rnd) * (hi - lo)))

    def chunks(tag, r):
        e = [0] + [128 * int(a) for a in eng("%s%d" % (tag, r), "8,16").split(",")] + [V]
        return list(zip(e[:-1], e[1:]))

    def cuts(tag, lo, hi):
        return [(lo, hi)] if eng(tag, "2") == "1" else [(a, min(hi, a + HF)) for a in range(lo, hi, HF)]

    def calls2(r):
        return [(lo, hi, eng("g2_%d_%d" % (r, lo // 128), "A")) for c0, c1 in chunks("cb", r) for lo, hi in cuts("n2_%d_%d" % (r, c0 // 128), c0, c1)]

    def runs(r, lo, hi):
        out = []
        for a in range(lo // HF * HF, hi, HF):
            lb = "l%s%d" % (eng("lw_%d_%d" % (r, a // 128), "V"), r)
            if out and out[-1][2] == lb:
                out[-1][1] = min(hi, a + HF)
            else:
                out.append([max(lo, a), min(hi, a + HF), lb])
        return out

    def groups(tag, c0, c1, sub):
        ps = [(a, min(c1, a + HF)) for a in range(c0, c1, HF)]
        out = []
        for k, (a, b) in enumerate(ps):
            if out and eng(tag, "2") == "1" and sub[a] == sub[out[-1][0]] and out[-1][1] - out[-1][0] == HF:
                out[-1] = (out[-1][0], b)
            else:
                out.append((a, b))
        return out

    for lo, hi, e in calls2(0):
        if e == "S":
            for a, b, w in own(lo, hi):
                nm = "dc_0_%d" % (a // 128)
                if eng(nm, "V") == "A":
                    ac(nm, C("d0", a, b), C("x0", w, w + b - a), AF.Identity, [("x0", w, w + b - a)], [("d0", a, b)], b - a)
                else:
                    cp(nm, C("d0", a, b), C("x0", w, w + b - a), [("x0", w, w + b - a)], [("d0", a, b)], (b - a) // 2)
    tabrd = [whole("tab"), ("tabr0", 0, 2), ("tabr1", 0, 2)]
    for r in range(RO):
        x, xn = "x%d" % r, "x%d" % (r + 1)
        idx, hoff, coff, sel = "idx%d" % r, "hoff%d" % r, "coff%d" % r, "sel%d" % r
        p, pn, pp, sf, sg = ("p0", "pp0", "pp1")[r], "p3", "pp%d" % r, "sf%d" % r, "sg%d" % r
        last, vd = r == RO - 1, ("vd", "vd1", "vd2")[r]
        used = [(lo, hi) for lo, hi in zip(four[r][:-1], four[r][1:]) if eng("g4_%d_%d" % (r, lo // 128), "V") == "V"]
        used += [(lo, hi) for lo, hi, e in calls2(r) if e == "S" and r]
        for u in range(0, V, HF):
            cs = [(max(a, u), min(b, u + HF)) for a, b in used if a < u + HF and b > u]
            if cs:
                e = eng("lw_%d_%d" % (r, u // 128), "V")
                for a, b, w in own(min(cs)[0], max(b for a, b in cs)):
                    nm, lb = "lw_%d_%d" % (r, 1 if u == 0 < a else u // 128), "l%s%d" % (e, r)
                    if e == "A":
                        ac(nm, C(lb, a, b), C(x, w, w + b - a), AF.Identity, [(x, w, w + b - a)], [(lb, a, b)], b - a, bias=K(LOW[r]))
                    else:
                        ts(nm, C(lb, a, b), C(x, w, w + b - a), K(LOW[r]), None, A.add, None, [(x, w, w + b - a)], [(lb, a, b)], (b - a) // 2)
        for c0, c1 in chunks("ca", r):
            t = "%d_%d" % (r, c0 // 128)
            for lo, hi in cuts("n1_" + t, c0, c1):
                nm = "g1_%d_%d" % (r, lo // 128)
                gather(nm, eng(nm, "A"), "hg", lo, hi, "tab", NW, idx, tabrd)
            ph, m0, m1 = "@w1_" + t, c0 // 16, c1 // 16
            wrap("w1_" + t, ph, "z1", "hg", c0, c1, False)
            cp("c1_" + t, C(hoff, m0, m1), P(ph, 0, m1 - m0), [PB(ph)], [(hoff, m0, m1)], m1 - m0)
            if eng("hk_" + t, "A") == "A":
                ac("hk_" + t, C("hk", m0, m1), P(ph, 0, m1 - m0), AF.Identity, [PB(ph)], [("hk", m0, m1)], m1 - m0, bias=K(FLAG[r]))
            else:
                ts("hk_" + t, C("hk", m0, m1), C(hoff, m0, m1), K(FLAG[r]), None, A.add, None, [(hoff, m0, m1)], [("hk", m0, m1)], m1 - m0)
        cb = chunks("cb", r)
        for c0, c1 in cb:
            t = "%d_%d" % (r, c0 // 128)
            m0, m1 = c0 // 16, c1 // 16
            n = m1 - m0
            sub = {}
            for lo, hi, e in calls2(r):
                if c0 <= lo < c1:
                    for a in range(lo, hi, HF):
                        sub[a] = e == "S"
                    if e != "S":
                        gather("g2_%d_%d" % (r, lo // 128), e, "de", lo, hi, x, NW, hoff, [(x, 0, NW)])
                    else:
                        for a, b, lb in runs(r, lo, hi) if r else [(lo, hi, "d0")]:
                            gtt("g2_%d_%d" % (r, a // 128), "de", a, x, NW, hoff, lb, a, b, A.subtract)
            for lo, hi in groups("na_" + t, c0, c1, sub):
                u = "%d_%d" % (r, lo // 128)
                if sub[lo]:
                    ac("ab_" + u, C("ab", lo, hi), C("de", lo, hi), AF.Abs, [("de", lo, hi)], [("ab", lo, hi)], hi - lo, scale=0.5 ** r,
                       bias=K(-0.5) if r else 0.0)
                    continue
                for a in range(lo, hi, HF):
                    two("me_%d_%d" % (r, a // 128), "@e" + u, a - lo, "eye", "eyen", "de", a, min(hi, a + HF), x)
                ac("ab_" + u, C("ab", lo, hi), P("@e" + u, 0, hi - lo), AF.Abs, [PB("@e" + u, 0, hi - lo)], [("ab", lo, hi)], hi - lo, scale=0.5 ** r)
            spans = []
            for lo, hi in groups("nb_" + t, c0, c1, sub):
                u = "%d_%d" % (r, lo // 128)
                for a in range(lo, hi, HF):
                    two("ms_%d_%d" % (r, a // 128), "@s" + u, a - lo, "am", "am2" if sub[lo] else "am", "de", a, min(hi, a + HF), x)
                nm = "bt_" + u
                e, rd = eng(nm, "A"), PB("@s" + u, 0, hi - lo)
                sx = "s" if sub[lo] and r else ""
                thr, nb = "thr%d%s" % (r, sx), "nb%d%s" % (min(r, 1), sx)
                need |= {nb if e == "A" else thr, "am2" if sub[lo] else "am"}
                if spans and spans[-1][2] == e:
                    spans[-1][1] = hi // 16
                else:
                    spans.append([lo // 16, hi // 16, e])
                if e == "A":
                    ac(nm, C("bits", lo, hi), P("@s" + u, 0, hi - lo), AF.Sign, [rd, whole(nb)], [("bits", lo, hi)], hi - lo, bias=C(nb, 0, 1),
                       scale=0.5 if last else 1.0)
                else:
                    ts(nm, C("bits", lo, hi), P("@s" + u, 0, hi - lo), C(thr, 0, 1), K(2.0), A.is_gt, A.mult, [rd, whole(thr)],
                       [("bits", lo, hi)], hi - lo)
            wrap("w2_" + t, "@w2_" + t, "z2", "bits", c0, c1, False)
            for a, b, e in spans:
                ts("c2_%d_%d" % (r, a // 8), C(coff, a, b), P("@w2_" + t, a - m0, b - m0), K(0.125), K(1023.5 if e == "A" else 0.0), A.mult, A.add,
                   [PB("@w2_" + t)], [(coff, a, b)], b - a)
            for lo, hi in cuts("n3_" + t, c0, c1):
                gtt("g3_%d_%d" % (r, lo // 128), "vi", lo, "clrs", 2048, coff, "ab", lo, hi, A.is_lt)
            wrap("w3_" + t, "@w3_" + t, "z3", "vi", c0, c1, True)
            tt("p1_" + t, C(pp, m0, m1), P("@w3_" + t, 0, n), C(p, m0, m1), A.max, [PB("@w3_" + t), (p, m0, m1)], [(pp, m0, m1)], n)
        for tag in ("cs", "cq", "cp"):
            ends = [b // 16 for a, b in cb if b == V or eng("%s_%d_%d" % (tag, r, a // 128), "1") == "1"]
            for c, (m0, m1) in enumerate(zip([0] + ends[:-1], ends)):
                t, n = "%d_%d" % (r, m1 // 8), m1 - m0
                if tag == "cs":
                    tt("p2_" + t, C(sf, m0, m1), C(pp, m0, m1), C(vd, m0, m1), A.min, [(pp, m0, m1), (vd, m0, m1)], [(sf, m0, m1)], 2 * n)
                    ts("p4_" + t, C(sg, m0, m1), C(sf, m0, m1), K(4095), None, A.bitwise_and, None, [(sf, m0, m1)], [(sg, m0, m1)], n)
                    cp("p3_" + t, C(sel, m0, m1), C(sg, m0, m1), [(sg, m0, m1)], [(sel, m0, m1)], n)
                elif tag == "cp":
                    if last:
                        ts("q5_" + t, C(pn, m0, m1), C(pp, m0, m1), K(4095), None, A.bitwise_and, None, [(pp, m0, m1)], [(pn, m0, m1)], n)
                        cp("o_" + t, C("po", m0, m1), C(pn, m0, m1), [(pn, m0, m1)], [("po", m0, m1)], n)
                    else:
                        ph, dg, sb = "@pm_" + t, "dg%d" % r, "sb%d" % r

                        def perm(ph=ph, dg=dg, sb=sb, m0=m0, m1=m1):
                            a = max(m0, 8)
                            for j in range(2 if m0 == 0 else 0):
                                pe.matmul(P(ph, 0, 8)(), T[("eyes", "eyeb")[j]][:], T[sb][:, s, j, :], j == 0, j == 1)
                            for j in range(2):
                                ins = pe.matmul(P(ph, a - m0, m1 - m0)(), T[("eyes", "eyeb")[j]][:], T[dg][:, j, 56 + a:56 + m1], j == 0, j == 1)
                            return ins
                        op("pm_" + t, "P", perm, [(dg + "o", m0, m1), whole("eyes"), whole("eyeb")] + ([(sb, 16 * s, 16 * s + 16)] if m0 == 0 else []),
                           [PB(ph)], ("p", 2 * max(64, n) + (128 if m0 == 0 else 0)))
                        cp("q4_" + t, C("idx%d" % (r + 1), m0, m1), P(ph, 0, n), [PB(ph)], [("idx%d" % (r + 1), m0, m1)], n)
                elif not last:
                    dg, sb = "dg%d" % r, "sb%d" % r
                    for j, bitmask in enumerate((0xFF0, 15)):
                        ts("q%d_%s" % (j + 1, t), D("hl", j, m0, m1), C(pp, m0, m1), K(bitmask), None,
                           A.bitwise_and, None, [(pp, m0, m1)], [("hl", 192 * j + m0, 192 * j + m1)], n)
                    hr = [("hl", m0, m1), ("hl", 192 + m0, 192 + m1)]
                    if c == 0:
                        ow = [(sb, 16 * s, 16 * s + 16)]
                        cp("q0_" + t, lambda sb=sb: T[sb][:, s, :, :], lambda: T.hl[:, :, 0:8], hr, ow, 16)
                        send("t%d" % (r + 1), lambda sb=sb: T[sb][:, s, :, :], ow, sb, 16, 4096, every)
                    m0 = max(m0, 8)
                    cp("q3_" + t, lambda dg=dg, m0=m0, m1=m1: T[dg][:, :, 56 + m0:56 + m1], lambda m0=m0, m1=m1: T.hl[:, :, m0:m1], hr,
                       [(dg + "o", m0, m1)], 2 * n)
        if not last:
            dg, sb = "dg%d" % r, "sb%d" % r
            for j in range(2):
                nm, src = "u%d_%d" % (j, r), lambda sb=sb, j=j: T[sb][:, :, j, :]
                if eng(nm, "A") == "A":
                    ac(nm, D(dg, j, 0, 64), src, AF.Identity, [whole(sb)], [(dg, j, j + 1)], 64)
                elif eng(nm, "A") == "V":
                    cp(nm, D(dg, j, 0, 64), src, [whole(sb)], [(dg, j, j + 1)], 32)
                else:
                    op(nm, "G", lambda dg=dg, j=j, src=src: g.affine_select(T[dg][:, j, 0:64], src(), [[0, 64]], A.is_ge, 0.0, 0, 0),
                       [whole(sb)], [(dg, j, j + 1)], ("g", 88))
                dma("tab%d_%d" % (j, r), "S", lambda j=j: T.tab[j:128:16, :], D(dg, j, 0, TW), [(dg, j, j + 1), (dg + "o", 0, 192)],
                    [("tabr%d" % j, 0, 2)], 63488)
        else:
            dma("syp", "S", lambda: T.yp[:], W("po"), [whole("po")], [], 98304)
        for lo, hi in zip(four[r][:-1], four[r][1:]):
            t = "%d_%d" % (r, lo // 128)
            e, n = eng("hv_" + t, "V"), hi - lo
            ob, o0 = ("yo", lo) if last else (xn, own(lo, hi)[0][2])
            if eng("g4_" + t, "V") == "A":
                pq = "@m" + t
                gather("g4_" + t, "A", "bg", lo, hi, x, NW, sel, [(x, 0, NW)])
                two("m4_" + t, pq, 0, "eyeg" if last else "eye", "eyeh" if last else "eye", "bg", lo, hi, x, last and e == "A")
                if e == "A":
                    ac("hv_" + t, C(ob, o0, o0 + n), P(pq, 0, n), AF.Identity, [PB(pq, 0, n)], [(ob, o0, o0 + n)], n, bias=K(-128.0 if last else LOW[r]))
                elif last:
                    ts("hv_" + t, C(ob, o0, o0 + n), P(pq, 0, n), K(MAGIC), K(MAGIC + 128.0), A.add, A.subtract, [PB(pq, 0, n)], [(ob, o0, o0 + n)], n)
                else:
                    ts("hv_" + t, C(ob, o0, o0 + n), P(pq, 0, n), K(LOW[r]), None, A.add, None, [PB(pq, 0, n)], [(ob, o0, o0 + n)], n)
            else:
                for a, b, lb in runs(r, lo, hi):
                    gtt("g4_%d_%d" % (r, a // 128), "y3" if last else ob, o0 + a - lo, x, NW, sel, lb, a, b, A.add)
                if last and e == "A":
                    ac("hv_" + t, C("yo", lo, hi), C("y3", lo, hi), AF.Identity, [("y3", lo, hi)], [("yo", lo, hi)], n, bias=K(-128.0), scale=0.125)
                elif last:
                    ts("hv_" + t, C("yo", lo, hi), C("y3", lo, hi), K(0.125), K(-128.0), A.mult, A.add, [("y3", lo, hi)], [("yo", lo, hi)], n // 2)
            if last:
                dma("syq_%d" % (lo // 128), "S", lambda lo=lo, hi=hi: T.yq[:, lo:hi], C("yo", lo, hi), [("yo", lo, hi)], [], 256 * n)
            elif lo == 0:
                send("x%d" % (r + 1), C(xn, b0, b1), [(xn, b0, b1)], xn, B, 32768, every)
    rounds = ops[late:]
    del ops[late:]
    if "am2" in need:
        ac("c_am2", W("am2"), W("am"), AF.Identity, [whole("am")], [whole("am2")], 128, scale=2.0)
    if "thr0" in need:
        cp("c_thr0", C("thr0", 0, 1), C("thi", 0, 1), [whole("thi")], [whole("thr0")], 1)
    if "nb0" in need:
        ts("c_nb0", C("nb0", 0, 1), C("thi", 0, 1), K(-1.0), K(-0.5), A.mult, A.add, [whole("thi")], [whole("nb0")], 1)
    ts("c_th2", C("th2", 0, 1), C("thi", 0, 1), K(2.0), None, A.mult, None, [whole("thi")], [whole("th2")], 1)
    mm("c_cs", "@c", 1, [("am", C("c32", 0, 1))], [whole("c32")], 64)
    for sx, f in (("", 16.0), ("s", 513.0 / 32)):
        t1 = "thr1" + sx
        if need & {t1, "thr2" + sx, "nb1" + sx}:
            ts("c_" + t1, C(t1, 0, 1), P("@c", 0, 1), K(f), C("th2", 0, 1), A.mult, A.add, [PB("@c"), whole("th2")], [whole(t1)], 1)
        if "thr2" + sx in need:
            ts("c_thr2" + sx, C("thr2" + sx, 0, 1), C(t1, 0, 1), K(2.0), None, A.mult, None, [whole(t1)], [whole("thr2" + sx)], 1)
        if "nb1" + sx in need:
            ts("c_nb1" + sx, C("nb1" + sx, 0, 1), C(t1, 0, 1), K(-1.0), K(-0.25), A.mult, A.add, [whole(t1)], [whole("nb1" + sx)], 1)
    return ops + rounds


def hazards(ops):
    seen = {}
    deps = {}
    for o in ops:
        name, q = o[0], o[1]
        d = {"m_pb"} if name == "lpb1" else set()
        acc = [(a, False) for a in o[3]] + [(a, True) for a in o[4]]
        for (b, lo, hi), w in acc:
            for (n2, q2, l2, h2, w2) in seen.get(b, []):
                if l2 < hi and lo < h2 and (w or w2 or (b[0] == "@" and q2 != q)):
                    d.add(n2)
        for (b, lo, hi), w in acc:
            seen.setdefault(b, []).append((name, q, lo, hi, w))
        deps[name] = d
    return deps


def pieces(ops):
    al = {}
    for o in ops:
        for b, lo, hi in o[3] + o[4]:
            if b[0] == "@":
                n, us = al.get(b, (0, []))
                al[b] = (max(n, hi // HF), us if o[0] in us else us + [o[0]])
    return al


def allocate(al, order, deps, bank):
    pos = {n: i for i, n in enumerate(order)}
    held = [(-1, [])] * 8
    for b in sorted(al, key=lambda a: min(pos[n] for n in al[a][1])):
        n, us = al[b]
        k = min(range(9 - n), key=lambda j: max(h[0] for h in held[j:j + n]))
        for j in range(k, k + n):
            for u in us:
                deps[u] = deps[u] | set(held[j][1])
            held[j] = (max(pos[u] for u in us), us)
        bank[b] = k


def rank_program(g, core, T, topo):
    if T.rank_of(core) is None:
        return
    bank = {}
    ops = build(g, T, topo, core, CFG, bank)
    deps = hazards(ops)
    byname = {o[0]: o for o in ops}
    order = [ops[i][0] for i in ORDER]
    allocate(pieces(ops), order, deps, bank)
    queue = {"A": g.scalar, "V": g.vector, "P": g.tensor, "S": g.sync, "G": g}
    kind = {n: byname[n][5][0] for n in order}
    pos = {n: i for i, n in enumerate(order)}

    known = {q: set() for q in queue}
    done_on = {q: [] for q in queue}
    after = {}
    waits = {}
    for n in order:
        q = byname[n][1]
        if q == "R":
            after[n] = {n}
            continue
        waits[n] = []
        for d in sorted(deps[n], key=lambda a: -pos[a]):
            if d not in known[q] and (q != "P" or byname[d][1] != "P"):
                waits[n].append(d)
                known[q] |= after[d]
        after[n] = known[q] | {n}
        if kind[n] not in ("dma", "send"):
            done_on[q].append(n)
            after[n] |= set(done_on[q])
    waited = set(done_on[q][-1] for q in done_on if done_on[q])
    for n in waits:
        waited |= set(waits[n])

    count = {q: 0 for q in queue}
    mark = {}
    for n in order:
        o = byname[n]
        q = o[1]
        if q == "R":
            mark[n] = (n, mark[o[2]][2])
            continue
        for d in waits[n]:
            queue[q].wait_ge(T.sem[mark[d][0]], mark[d][1])
        ins = o[2]()
        if kind[n] == "dma":
            ins.then_inc(T.sem[n], 16)
            mark[n] = (n, 16)
        elif kind[n] == "send":
            mark[n] = ("out_" + n[4:], ins[0], ins[1])
        elif n in waited:
            count[q] += 1
            ins.then_inc(T.sem["q" + q], 1)
            mark[n] = ("q" + q, count[q])
    for n in order:
        if kind[n] in ("dma", "send", "arr") and n not in waited:
            g.wait_ge(T.sem[mark[n][0]], mark[n][1])
    for q in ("A", "V", "P", "G"):
        g.wait_ge(T.sem["q" + q], count[q])
